import numpy as np
import ml_dtypes


def mxq(x, axis, fmt="e4m3"):
    dtype, down = {"e4m3": (ml_dtypes.float8_e4m3fn, 7), "e5m2": (ml_dtypes.float8_e5m2, 14)}[fmt]
    v = np.moveaxis(np.asarray(x, np.float32).astype(ml_dtypes.bfloat16).astype(np.float64), axis, -1)
    blocks = v.reshape(v.shape[:-1] + (-1, 32))
    amax = np.abs(blocks).max(-1, keepdims=True)
    byte = np.maximum(np.where(amax > 0, np.frexp(amax)[1] - 1 + 127, 0) - down, 1)
    scale = np.exp2(byte - 127.0)
    codes = (blocks / scale).astype(np.float32).astype(dtype).astype(np.float64)
    return np.moveaxis((codes * scale).reshape(v.shape), -1, axis)


WIDE = False


def mx_kscale(k):
    if not WIDE:
        return np.ones(k)
    levels = np.array([10, -10, 5, -5, 0])
    if k % 512:
        return np.exp2(np.random.permutation(np.resize(levels, k // 32))).repeat(32)
    a = np.empty((k // 512, 16))
    for p in range(k // 512):
        a[p, :8] = np.random.permutation(np.resize(levels, 8))
        for g in range(8):
            far = levels[np.abs(levels - a[p, g]) >= 10]
            a[p, g + 8] = far[np.random.randint(len(far))]
    return np.exp2(a.ravel()).repeat(32)


def f64(x):
    return np.asarray(x).astype(np.float64)


def striped(idx):
    return np.tile(idx.reshape(-1, 16).T, (8, 1)).astype(np.uint16)


def unstriped(offs):
    return offs[:16].T.reshape(-1).astype(np.int64)


E2M1 = np.array([0.0, 0.5, 1.0, 1.5, 2.0, 3.0, 4.0, 6.0, -0.0, -0.5, -1.0, -1.5, -2.0, -3.0, -4.0, -6.0])


def pack_weight(w, fmt):
    k, n = w.shape
    w = f64(np.asarray(w, np.float32).astype(ml_dtypes.bfloat16)).reshape(k // 32, 32, n)
    amax = np.abs(w).max(1)
    if fmt == "e4m3":
        byte = np.frexp(amax)[1] - 1 + 127 - 7
    else:
        mant, ex = np.frexp(amax / 6.0)
        byte = np.where(mant > 0.5, ex, ex - 1) + 127
    byte = np.clip(np.where(amax > 0, byte, 1), 1, 254)
    scaled = (w * np.exp2(127.0 - byte)[:, None, :]).reshape(k, n).astype(np.float32)
    by_word = np.ascontiguousarray(scaled.reshape(k // 512, 128, 4, n).transpose(0, 1, 3, 2))
    if fmt == "e4m3":
        words = by_word.astype(ml_dtypes.float8_e4m3fn).view(np.uint8)
    else:
        c = by_word.astype(ml_dtypes.float4_e2m1fn).view(np.uint8) & 0xF
        words = (c[..., 0::2] | (c[..., 1::2] << 4)).reshape(k // 512, 128, 2 * n)
    return np.ascontiguousarray(words), np.ascontiguousarray(byte.astype(np.uint8).reshape(k // 512, 16, n))


def unpack_weight(words, scales, fmt):
    g, _, n = scales.shape
    words = np.ascontiguousarray(words).reshape(g, 128, n, -1)
    if fmt == "e4m3":
        vals = words.view(ml_dtypes.float8_e4m3fn).astype(np.float64)
    else:
        nib = np.empty((g, 128, n, 4), np.uint8)
        nib[..., 0::2] = words & 0xF
        nib[..., 1::2] = words >> 4
        vals = E2M1[nib]
    vals = vals * np.repeat(np.exp2(scales.astype(np.float64) - 127.0), 8, axis=1)[..., None]
    return vals.transpose(0, 1, 3, 2).reshape(g * 512, n)


def gelu(v):
    return 0.5 * v * (1.0 + np.tanh(np.sqrt(2.0 / np.pi) * (v + 0.044715 * v**3)))


K, H, N, T, S = 1024, 512, 384, 2048, 1024


def setup_inputs():
    n = np.random.standard_normal
    s = mx_kscale(K)[:, None]
    u = mx_kscale(H)[:, None]
    tab_words, tab_scales = pack_weight(n((K, T)) * s, "e4m3")
    w2_words, w2_scales = pack_weight(n((K, H)) / np.sqrt(K) / s, "e2m1")
    w3_words, w3_scales = pack_weight(n((K, H)) / np.sqrt(K) / s, "e4m3")
    return {
        "tab_words": tab_words, "tab_scales": tab_scales,
        "offs": striped(np.random.permutation(T)[:S]),
        "offs2": striped(np.random.permutation(T)[:S]),
        "offs3": striped(np.random.permutation(T)[:S]),
        "w1": (n((K, H)) / np.sqrt(K) / s).astype(np.float32),
        "w2_words": w2_words, "w2_scales": w2_scales,
        "w3_words": w3_words, "w3_scales": w3_scales,
        "g": (np.exp(0.3 * n(H)) * u[:, 0]).astype(np.float32),
        "w4": (n((H, N)) / np.sqrt(H) / u).astype(np.float32),
        "b": (0.5 * n(N)).astype(np.float32),
    }


def reference(tab_words, tab_scales, offs, offs2, offs3, w1, w2_words, w2_scales, w3_words, w3_scales, g, w4, b):
    v = unpack_weight(tab_words, tab_scales, "e4m3")[:, unstriped(offs)]
    v2 = unpack_weight(tab_words, tab_scales, "e4m3")[:, unstriped(offs2)]
    v3 = unpack_weight(tab_words, tab_scales, "e4m3")[:, unstriped(offs3)]
    w1q = mxq(f64(w1), 0, "e4m3")
    w2q = unpack_weight(w2_words, w2_scales, "e2m1")
    w3q = unpack_weight(w3_words, w3_scales, "e4m3")
    d = w1q.T @ v + w2q.T @ v2 + w3q.T @ v3
    h = np.sqrt(d * d + 1.0) * f64(g)[:, None]
    y = mxq(f64(w4), 0, "e4m3").T @ mxq(h, 0, "e4m3")
    return y + f64(b)[:, None]

@@ -1,0 +1,291 @@
+from contextlib import ExitStack
+
+import concourse.mybir as mybir
+
+K, H, N, T, S = 1024, 512, 384, 2048, 1024
+FLOPS = 2 * (3 * K * H * S + H * N * S)
+
+F32 = mybir.dt.float32
+BF16 = mybir.dt.bfloat16
+I32 = mybir.dt.int32
+U32 = mybir.dt.uint32
+U16 = mybir.dt.uint16
+U8 = mybir.dt.uint8
+FP8X4 = mybir.dt.float8_e4m3fn_x4
+FP4X4 = mybir.dt.float4_e2m1fn_x4
+ACT = mybir.ActivationFunctionType
+ALU = mybir.AluOpType
+
+P = 128
+PASSES = 2
+SLOTS = 4
+TILES_N = 3
+
+
+def tile_list_cloth_stretch_features_kernel(
+    tc, tab_words, tab_scales, offs, offs2, offs3, w1, w2_words, w2_scales, w3_words, w3_scales, g, w4, b, out
+):
+    nc = tc.nc
+    with ExitStack() as ctx:
+        keep = ctx.enter_context(tc.tile_pool(name="keep", bufs=1))
+        ring = ctx.enter_context(tc.tile_pool(name="ring", bufs=2))
+        d_psum = ctx.enter_context(tc.psum_pool(name="d_psum", bufs=6))
+        y_psum = ctx.enter_context(tc.psum_pool(name="y_psum", bufs=1))
+
+        lists = [keep.tile([P, S // 16], U16, name=f"list{m}") for m in range(3)]
+        table = [keep.tile([P, T], I32, name=f"table{a}", align_bytes=64) for a in range(PASSES)]
+        table_sc = keep.tile([P, T], U8, name="table_sc", align_bytes=64)
+        w3_sc_raw = keep.tile([P, PASSES, H], U8, name="w3_sc_raw", tag="slot_a", align_bytes=64)
+        w2_sc_raw = keep.tile([P, PASSES, H], U8, name="w2_sc_raw", tag="slot_b", align_bytes=64)
+        w3_sc = keep.tile([P, SLOTS, PASSES, P], U8, name="w3_sc", align_bytes=64)
+        w2_sc = keep.tile([P, SLOTS, PASSES, P], U8, name="w2_sc", align_bytes=64)
+        w3_raw = keep.tile([P, PASSES, H], I32, name="w3_raw", align_bytes=64)
+        w3_q = keep.tile([P, SLOTS, PASSES, P], I32, name="w3_q", align_bytes=64)
+        w2_raw = keep.tile([P, PASSES, H // 2], I32, name="w2_raw", align_bytes=64)
+        w2_q = keep.tile([P, SLOTS, PASSES, 2 * P], U8, name="w2_q", align_bytes=64)
+        w1_raw = [keep.tile([P, 4, H], F32, name=f"w1_raw{a}") for a in range(PASSES)]
+        w1_bf = [
+            [keep.tile([P, 2, 4 * P], BF16, name=f"w1_bf{a}{u}", tag=f"w1_bf{a}{u}", align_bytes=64) for u in range(2)]
+            for a in range(PASSES)
+        ]
+        w1_q = keep.tile([P, PASSES, H], U32, name="w1_q", align_bytes=64)
+        w1_sc = keep.tile([P, PASSES, H], U8, name="w1_sc", align_bytes=64)
+        w4_raw = keep.tile([P, SLOTS, N], F32, name="w4_raw")
+        w4_bf = keep.tile([P, N, SLOTS], BF16, name="w4_bf", tag="w4_bf", align_bytes=64)
+        w4_q = keep.tile([P, N], U32, name="w4_q", align_bytes=64)
+        w4_sc = keep.tile([P, N], U8, name="w4_sc", align_bytes=64)
+        g_col = keep.tile([P, SLOTS, 8], F32, name="g_col")
+        b_col = keep.tile([P, TILES_N], F32, name="b_col")
+        ones = keep.tile([P, 1], F32, name="ones")
+        one = keep.tile([P, 1], F32, name="one")
+        v_q = {}
+        v_sc = {}
+        v2_sc = keep.tile([P, S], U8, name="v2_sc", align_bytes=64)
+        v2_sc_pass1 = keep.tile([P, S], U8, name="v2_sc_pass1", align_bytes=64)
+
+        nc.vector.memset(table_sc[:].bitcast(I32), 0)
+        nc.vector.memset(w3_sc_raw[:].rearrange("p a c -> p (a c)").bitcast(I32), 0)
+        nc.vector.memset(w2_sc_raw[:].rearrange("p a c -> p (a c)").bitcast(I32), 0)
+        nc.vector.memset(v2_sc_pass1[:].bitcast(I32), 0)
+        nc.gpsimd.memset(ones[:], 1.0)
+        nc.scalar.activation(out=one[:], in_=ones[:], func=ACT.Sqrt)
+
+        def load_table(a):
+            nc.sync.dma_start(out=table[a][:], in_=tab_words[a].rearrange("p t i -> p (t i)").bitcast(I32))
+
+        nc.sync.dma_start(lists[1][:], offs2)
+        for q in range(4):
+            nc.sync.dma_start(
+                out=table_sc[32 * q : 32 * q + 8, :].bitcast(I32),
+                in_=tab_scales[:, 4 * q : 4 * q + 4, :].bitcast(I32),
+            )
+        nc.sync.dma_start(lists[2][:], offs3)
+        load_table(0)
+        nc.sync.dma_start(out=w3_raw[:], in_=w3_words.rearrange("a p c i -> p a (c i)").bitcast(I32))
+        nc.sync.dma_start(out=w2_raw[:], in_=w2_words.rearrange("a p c -> p a c").bitcast(I32))
+        nc.sync.dma_start(lists[0][:], offs)
+        load_table(1)
+        for plane, scales in ((w3_sc_raw, w3_scales), (w2_sc_raw, w2_scales)):
+            for q in range(4):
+                nc.gpsimd.dma_start(
+                    out=plane[32 * q : 32 * q + 4, :, :].bitcast(I32),
+                    in_=scales[:, 4 * q : 4 * q + 4, :].rearrange("a r c -> r a c").bitcast(I32),
+                )
+        for a in range(PASSES):
+            nc.sync.dma_start(out=w1_raw[a][:], in_=w1[512 * a : 512 * (a + 1), :].rearrange("(p j) r -> p j r", j=4))
+        for t in range(SLOTS):
+            nc.sync.dma_start(out=w4_raw[:, t, :], in_=w4.rearrange("(b t i) n -> t b i n", t=SLOTS, i=8)[t])
+        with nc.allow_non_contiguous_dma(reason="one value a partition"):
+            for t in range(SLOTS):
+                nc.sync.dma_start(
+                    out=g_col[:, t, 0:1], in_=g.rearrange("(b t i e) -> t b i e", t=SLOTS, i=8, e=1)[t]
+                )
+            nc.sync.dma_start(out=b_col[:], in_=b.rearrange("(c p) -> p c", p=P))
+
+        def gather_scales(m, lo, hi, dst):
+            v_sc[m, lo // 512] = dst
+            nc.vector.tensor_copy(out=dst, in_=table_sc[:].indirect(lists[m][:, lo // 16 : hi // 16]))
+
+        def gather_words(m, a, lo, hi, dst):
+            v_q[m, a, lo] = dst
+            nc.vector.tensor_copy(out=dst, in_=table[a][:].bitcast(U32).indirect(lists[m][:, lo // 16 : hi // 16]))
+
+        def d_passes(banks, m, a, lo, hi, start=False, stop=False):
+            words = v_q[m, a, lo]
+            for t in range(SLOTS):
+                if m == 1:
+                    rhs_sc = v2_sc if a == 0 else v2_sc_pass1
+                    step = 512 if hi - lo == 512 else 128
+                    for c0 in range(0, hi - lo, step):
+                        nc.tensor.matmul_mx(
+                            out=banks[t][:, c0 : c0 + step],
+                            lhsT=w2_q[:, t, a, :].bitcast(FP4X4),
+                            lhsT_scale=w2_sc[:, t, a, :],
+                            rhs=words[:, c0 : c0 + step].bitcast(FP8X4),
+                            rhs_scale=rhs_sc[:, lo + c0 : lo + c0 + step],
+                            start=False,
+                            stop=False,
+                        )
+                    continue
+                if m == 0:
+                    lhs, lhs_sc = w1_q[:, a, P * t : P * (t + 1)], w1_sc[:, a, P * t : P * (t + 1)]
+                else:
+                    lhs, lhs_sc = w3_q[:, t, a, :], w3_sc[:, t, a, :]
+                nc.tensor.matmul_mx(
+                    out=banks[t][:],
+                    lhsT=lhs.bitcast(FP8X4),
+                    lhsT_scale=lhs_sc,
+                    rhs=words.bitcast(FP8X4),
+                    rhs_scale=v_sc[m, lo // 512][4 * a : P, lo % 512 : lo % 512 + hi - lo],
+                    start=start,
+                    stop=stop,
+                )
+
+        def cast_w1(a):
+            for t in range(SLOTS):
+                nc.scalar.copy(
+                    out=w1_bf[a][t // 2][:, t % 2, :].rearrange("p (b i j) -> p b i j", i=8, j=4),
+                    in_=w1_raw[a][:].rearrange("p j (b t i) -> p t b i j", t=SLOTS, i=8)[:, t],
+                )
+
+        def quantize_w1(a):
+            for u in range(2):
+                cols = slice(256 * u, 256 * (u + 1))
+                nc.vector.quantize_mx(
+                    out=w1_q[:, a, cols].bitcast(FP8X4),
+                    scales=w1_sc[:, a, cols],
+                    in_=w1_bf[a][u][:].rearrange("p t c -> p (t c)"),
+                )
+
+        def reorder_columns(dst, src, run):
+            nc.vector.tensor_copy(
+                out=dst.rearrange("p t a (b i) -> p t (a b) i", i=run),
+                in_=src.rearrange("p a (b t i) -> p t (a b) i", t=SLOTS, i=run),
+            )
+
+        def new_banks(width):
+            return [d_psum.tile([P, width], F32, name="d_bank", tag="d_bank") for t in range(SLOTS)]
+
+        def square(banks, lo, hi):
+            sq = ring.tile([P, SLOTS, hi - lo], F32, name="sq", tag="sq")
+            for t in range(SLOTS):
+                nc.scalar.activation(out=sq[:, t, :], in_=banks[t][:, lo:hi], func=ACT.Square)
+            return sq
+
+        def magnitude(sq, lo, hi):
+            mag = ring.tile([P, SLOTS, hi - lo], F32, name="mag", tag="mag", bufs=3)
+            nc.scalar.activation(out=mag[:], in_=sq[:, :, lo:hi], func=ACT.Sqrt, bias=one[:])
+            return mag
+
+        def stiffen(engine, mag, width, tag):
+            h_bf = keep.tile([P, width, SLOTS], BF16, name=tag, tag=tag, align_bytes=64)
+            engine.tensor_tensor(
+                out=h_bf[:],
+                in0=mag[:].rearrange("p t n -> p n t"),
+                in1=g_col[:, :, 0].unsqueeze(1).to_broadcast([P, width, SLOTS]),
+                op=ALU.mult,
+            )
+            return h_bf
+
+        def quantize_h(h_bf, width):
+            h_q = ring.tile([P, width], U32, name="h_q", tag="h_q", align_bytes=64)
+            h_sc = ring.tile([P, width], U8, name="h_sc", tag="h_sc", align_bytes=64)
+            nc.vector.quantize_mx(out=h_q[:].bitcast(FP8X4), scales=h_sc[:], in_=h_bf[:].rearrange("p n t -> p (n t)"))
+            return h_q, h_sc
+
+        def readout_pass(dst, c, h_q, h_sc):
+            nc.tensor.matmul_mx(
+                out=dst,
+                lhsT=w4_q[:, P * c : P * (c + 1)].bitcast(FP8X4),
+                lhsT_scale=w4_sc[:, P * c : P * (c + 1)],
+                rhs=h_q[:].bitcast(FP8X4),
+                rhs_scale=h_sc[:],
+                start=True,
+                stop=True,
+            )
+
+        out_view = out.rearrange("(c p) j -> p c j", p=P)
+
+        def readout_wide(h_q, h_sc, lo):
+            y_a = y_psum.tile([P, 2, 256], F32, name="y_a", tag="y_a")
+            y_b = y_psum.tile([P, 256], F32, name="y_b", tag="y_b")
+            ys = [y_a[:, 0, :], y_a[:, 1, :], y_b[:]]
+            res = ring.tile([P, TILES_N, 256], F32, name="res", tag="res", bufs=3)
+            for c in range(TILES_N):
+                readout_pass(ys[c], c, h_q, h_sc)
+            for c in range(TILES_N):
+                nc.scalar.activation(out=res[:, c, :], in_=ys[c], func=ACT.Identity, bias=b_col[:, c : c + 1])
+            nc.sync.dma_start(out=out_view[:, :, lo : lo + 256], in_=res[:])
+
+        def readout_narrow(h_q, h_sc, lo, tag):
+            y = y_psum.tile([P, TILES_N, P], F32, name=tag, tag=tag)
+            res = ring.tile([P, TILES_N, P], F32, name="res", tag="res", bufs=3)
+            for c in range(TILES_N):
+                readout_pass(y[:, c, :], c, h_q, h_sc)
+            nc.vector.tensor_tensor(
+                out=res[:], in0=y[:], in1=b_col[:].unsqueeze(2).to_broadcast([P, TILES_N, P]), op=ALU.add
+            )
+            nc.sync.dma_start(out=out_view[:, :, lo : lo + P], in_=res[:])
+
+        nc.vector.tensor_copy(out=v2_sc[:], in_=table_sc[:].indirect(lists[1][:]))
+        nc.scalar.dma_start(out=v2_sc_pass1[0:112, :].bitcast(I32), in_=v2_sc[4:116, :].bitcast(I32))
+        sc_first = keep.tile([P, 2, 512], U8, name="sc_first", align_bytes=64)
+        words_free = keep.tile([P, 512], U32, name="words_free", align_bytes=64)
+        gather_scales(2, 0, 512, sc_first[:, 0, :])
+        banks = new_banks(512)
+        gather_words(2, 0, 0, 512, words_free[:])
+        reorder_columns(w3_q[:], w3_raw[:], 8)
+        reorder_columns(w3_sc[:].bitcast(I32), w3_sc_raw[:].bitcast(I32), 2)
+        d_passes(banks, 2, 0, 0, 512, start=True)
+        gather_scales(0, 0, 512, sc_first[:, 1, :])
+        words_a = keep.tile([P, 512], U32, name="words_a", tag="slot_a", align_bytes=64)
+        gather_words(1, 0, 0, 512, words_a[:])
+        reorder_columns(w2_q[:].bitcast(I32), w2_raw[:], 4)
+        reorder_columns(w2_sc[:].bitcast(I32), w2_sc_raw[:].bitcast(I32), 2)
+        d_passes(banks, 1, 0, 0, 512)
+        words_b = keep.tile([P, 4, 512], U32, name="words_b", tag="slot_b", align_bytes=64)
+        for place, (m, a) in enumerate(((2, 1), (1, 1))):
+            gather_words(m, a, 0, 512, words_b[:, place, :])
+            d_passes(banks, m, a, 0, 512)
+        for a in range(PASSES):
+            cast_w1(a)
+            gather_words(0, a, 0, 512, words_b[:, 2 + a, :])
+            quantize_w1(a)
+            d_passes(banks, 0, a, 0, 512, stop=(a == PASSES - 1))
+        nc.scalar.copy(out=w4_bf[:], in_=w4_raw[:].rearrange("p t n -> p n t"))
+        sq_first = square(banks, 0, 512)
+
+        order = ((2, 0), (1, 0), (2, 1), (1, 1), (0, 0), (0, 1))
+
+        def stretch(lo, hi, places):
+            chunk_banks = new_banks(hi - lo)
+            for step, (m, a) in enumerate(order):
+                gather_words(m, a, lo, hi, places[step])
+                d_passes(chunk_banks, m, a, lo, hi, start=(step == 0), stop=(step == len(order) - 1))
+            return chunk_banks
+
+        sc_second = keep.tile([P, 2, 512], U8, name="sc_second", tag="w1_bf10", align_bytes=64)
+        gather_scales(2, 512, S, sc_second[:, 0, :])
+        gather_scales(0, 512, S, sc_second[:, 1, :])
+        for lo, hi in ((0, 256), (256, N)):
+            nc.vector.quantize_mx(
+                out=w4_q[:, lo:hi].bitcast(FP8X4),
+                scales=w4_sc[:, lo:hi],
+                in_=w4_bf[:, lo:hi, :].rearrange("p n t -> p (n t)"),
+            )
+        h_first = [stiffen(nc.gpsimd, magnitude(sq_first, 256 * u, 256 * u + 256), 256, f"h_bf{u}") for u in range(2)]
+        words_c = keep.tile([P, 6, 256], U32, name="words_c", tag="w1_bf11", align_bytes=64)
+        banks = stretch(512, 768, [words_c[:, step, :] for step in range(6)])
+        for u in range(2):
+            readout_wide(*quantize_h(h_first[u], 256), 256 * u)
+        mag_third = magnitude(square(banks, 0, 256), 0, 256)
+        words_d = keep.tile([P, 2, 256], U32, name="words_d", tag="w4_bf", align_bytes=64)
+        words_e = keep.tile([P, 4, 256], U32, name="words_e", tag="h_bf0", align_bytes=64)
+        banks = stretch(768, S, [words_d[:, step, :] for step in range(2)] + [words_e[:, step, :] for step in range(4)])
+        mags = [magnitude(square(banks, lo, lo + P), 0, P) for lo in (0, P)]
+        h_third = quantize_h(stiffen(nc.vector, mag_third, 256, "h_bf2"), 256)
+        h_last = [quantize_h(stiffen(nc.vector, mags[0], P, "h_bf3"), P)]
+        readout_wide(*h_third, 512)
+        h_last.append(quantize_h(stiffen(nc.vector, mags[1], P, "h_bf4"), P))
+        readout_narrow(*h_last[0], 768, "y_b")
+        readout_narrow(*h_last[1], 896, "y_a")

@@ -29,17 +29,16 @@ def tile_list_cloth_stretch_features_kernel(
     with ExitStack() as ctx:
         keep = ctx.enter_context(tc.tile_pool(name="keep", bufs=1))
         ring = ctx.enter_context(tc.tile_pool(name="ring", bufs=2))
-        d_psum = ctx.enter_context(tc.psum_pool(name="d_psum", bufs=6))
-        y_psum = ctx.enter_context(tc.psum_pool(name="y_psum", bufs=1))
+        psum = ctx.enter_context(tc.psum_pool(name="psum", bufs=1))
 
         lists = [keep.tile([P, S // 16], U16, name=f"list{m}") for m in range(3)]
-        table = [keep.tile([P, T], I32, name=f"table{a}", align_bytes=64) for a in range(PASSES)]
+        table = [keep.tile([P, T], I32, name=f"table{a}", tag=f"table{a}", align_bytes=64) for a in range(PASSES)]
         table_sc = keep.tile([P, T], U8, name="table_sc", align_bytes=64)
-        w3_sc_raw = keep.tile([P, PASSES, H], U8, name="w3_sc_raw", tag="slot_a", align_bytes=64)
-        w2_sc_raw = keep.tile([P, PASSES, H], U8, name="w2_sc_raw", tag="slot_b", align_bytes=64)
+        w3_sc_raw = keep.tile([P, PASSES, H], U8, name="w3_sc_raw", align_bytes=64)
+        w2_sc_raw = keep.tile([P, PASSES, H], U8, name="w2_sc_raw", align_bytes=64)
         w3_sc = keep.tile([P, SLOTS, PASSES, P], U8, name="w3_sc", align_bytes=64)
         w2_sc = keep.tile([P, SLOTS, PASSES, P], U8, name="w2_sc", align_bytes=64)
-        w3_raw = keep.tile([P, PASSES, H], I32, name="w3_raw", align_bytes=64)
+        w3_raw = keep.tile([P, PASSES, H], I32, name="w3_raw", tag="w3_raw", align_bytes=64)
         w3_q = keep.tile([P, SLOTS, PASSES, P], I32, name="w3_q", align_bytes=64)
         w2_raw = keep.tile([P, PASSES, H // 2], I32, name="w2_raw", align_bytes=64)
         w2_q = keep.tile([P, SLOTS, PASSES, 2 * P], U8, name="w2_q", align_bytes=64)
@@ -50,8 +49,12 @@ def tile_list_cloth_stretch_features_kernel(
         ]
         w1_q = keep.tile([P, PASSES, H], U32, name="w1_q", align_bytes=64)
         w1_sc = keep.tile([P, PASSES, H], U8, name="w1_sc", align_bytes=64)
-        w4_raw = keep.tile([P, SLOTS, N], F32, name="w4_raw")
-        w4_bf = keep.tile([P, N, SLOTS], BF16, name="w4_bf", tag="w4_bf", align_bytes=64)
+        w4_raw = keep.tile([P, SLOTS, N], F32, name="w4_raw", tag="w4_raw")
+        w4_cols = ((0, 256), (256, N))
+        w4_bf = [
+            keep.tile([P, hi - lo, SLOTS], BF16, name=f"w4_bf{u}", tag=f"w4_bf{u}", align_bytes=64)
+            for u, (lo, hi) in enumerate(w4_cols)
+        ]
         w4_q = keep.tile([P, N], U32, name="w4_q", align_bytes=64)
         w4_sc = keep.tile([P, N], U8, name="w4_sc", align_bytes=64)
         g_col = keep.tile([P, SLOTS, 8], F32, name="g_col")
@@ -63,11 +66,11 @@ def tile_list_cloth_stretch_features_kernel(
         v2_sc = keep.tile([P, S], U8, name="v2_sc", align_bytes=64)
         v2_sc_pass1 = keep.tile([P, S], U8, name="v2_sc_pass1", align_bytes=64)
 
-        nc.vector.memset(table_sc[:].bitcast(I32), 0)
-        nc.vector.memset(w3_sc_raw[:].rearrange("p a c -> p (a c)").bitcast(I32), 0)
-        nc.vector.memset(w2_sc_raw[:].rearrange("p a c -> p (a c)").bitcast(I32), 0)
-        nc.vector.memset(v2_sc_pass1[:].bitcast(I32), 0)
+        nc.gpsimd.memset(table_sc[:].bitcast(I32), 0)
         nc.gpsimd.memset(ones[:], 1.0)
+        nc.gpsimd.memset(w3_sc_raw[:].rearrange("p a c -> p (a c)").bitcast(I32), 0)
+        nc.gpsimd.memset(w2_sc_raw[:].rearrange("p a c -> p (a c)").bitcast(I32), 0)
+        nc.gpsimd.memset(v2_sc_pass1[:].bitcast(I32), 0)
         nc.scalar.activation(out=one[:], in_=ones[:], func=ACT.Sqrt)
 
         def load_table(a):
@@ -79,20 +82,29 @@ def tile_list_cloth_stretch_features_kernel(
                 out=table_sc[32 * q : 32 * q + 8, :].bitcast(I32),
                 in_=tab_scales[:, 4 * q : 4 * q + 4, :].bitcast(I32),
             )
+        nc.vector.tensor_copy(out=v2_sc[:], in_=table_sc[:].indirect(lists[1][:]))
         nc.sync.dma_start(lists[2][:], offs3)
         load_table(0)
         nc.sync.dma_start(out=w3_raw[:], in_=w3_words.rearrange("a p c i -> p a (c i)").bitcast(I32))
         nc.sync.dma_start(out=w2_raw[:], in_=w2_words.rearrange("a p c -> p a c").bitcast(I32))
-        nc.sync.dma_start(lists[0][:], offs)
-        load_table(1)
-        for plane, scales in ((w3_sc_raw, w3_scales), (w2_sc_raw, w2_scales)):
+
+        def load_weight_scales(plane, scales):
             for q in range(4):
-                nc.gpsimd.dma_start(
+                nc.sync.dma_start(
                     out=plane[32 * q : 32 * q + 4, :, :].bitcast(I32),
                     in_=scales[:, 4 * q : 4 * q + 4, :].rearrange("a r c -> r a c").bitcast(I32),
                 )
-        for a in range(PASSES):
+
+        def load_w1(a):
             nc.sync.dma_start(out=w1_raw[a][:], in_=w1[512 * a : 512 * (a + 1), :].rearrange("(p j) r -> p j r", j=4))
+
+        load_weight_scales(w3_sc_raw, w3_scales)
+        load_table(1)
+        nc.sync.dma_start(lists[0][:], offs)
+        load_weight_scales(w2_sc_raw, w2_scales)
+        load_w1(0)
+        nc.sync.dma_start(out=v2_sc_pass1[0:112, :].bitcast(I32), in_=v2_sc[4:116, :].bitcast(I32))
+        load_w1(1)
         for t in range(SLOTS):
             nc.sync.dma_start(out=w4_raw[:, t, :], in_=w4.rearrange("(b t i) n -> t b i n", t=SLOTS, i=8)[t])
         with nc.allow_non_contiguous_dma(reason="one value a partition"):
@@ -157,40 +169,45 @@ def tile_list_cloth_stretch_features_kernel(
                     in_=w1_bf[a][u][:].rearrange("p t c -> p (t c)"),
                 )
 
-        def reorder_columns(dst, src, run):
-            nc.vector.tensor_copy(
+        def reorder_columns(engine, dst, src, run):
+            engine.tensor_copy(
                 out=dst.rearrange("p t a (b i) -> p t (a b) i", i=run),
                 in_=src.rearrange("p a (b t i) -> p t (a b) i", t=SLOTS, i=run),
             )
 
-        def new_banks(width):
-            return [d_psum.tile([P, width], F32, name="d_bank", tag="d_bank") for t in range(SLOTS)]
+        def new_banks(width, first):
+            return [psum.tile([P, width], F32, name="d_bank", tag=f"bank{first + t}") for t in range(SLOTS)]
 
-        def square(banks, lo, hi):
-            sq = ring.tile([P, SLOTS, hi - lo], F32, name="sq", tag="sq")
+        def square(banks, lo, hi, tag):
+            sq = keep.tile([P, SLOTS, hi - lo], F32, name="sq", tag=tag)
             for t in range(SLOTS):
                 nc.scalar.activation(out=sq[:, t, :], in_=banks[t][:, lo:hi], func=ACT.Square)
             return sq
 
         def magnitude(sq, lo, hi):
-            mag = ring.tile([P, SLOTS, hi - lo], F32, name="mag", tag="mag", bufs=3)
+            mag = ring.tile([P, SLOTS, hi - lo], F32, name="mag", tag="mag", bufs=5)
             nc.scalar.activation(out=mag[:], in_=sq[:, :, lo:hi], func=ACT.Sqrt, bias=one[:])
-            return mag
+            return mag[:]
 
-        def stiffen(engine, mag, width, tag):
-            h_bf = keep.tile([P, width, SLOTS], BF16, name=tag, tag=tag, align_bytes=64)
+        def new_h_bf(width, tag):
+            return keep.tile([P, width, SLOTS], BF16, name=tag, tag=tag, align_bytes=64)[:]
+
+        def new_h_q(width, tag):
+            return keep.tile([P, width], U32, name=tag, tag=tag, align_bytes=64)[:]
+
+        def stiffen(engine, mag, h_bf):
+            width = h_bf.shape[1]
             engine.tensor_tensor(
-                out=h_bf[:],
-                in0=mag[:].rearrange("p t n -> p n t"),
+                out=h_bf,
+                in0=mag.rearrange("p t n -> p n t"),
                 in1=g_col[:, :, 0].unsqueeze(1).to_broadcast([P, width, SLOTS]),
                 op=ALU.mult,
             )
             return h_bf
 
-        def quantize_h(h_bf, width):
-            h_q = ring.tile([P, width], U32, name="h_q", tag="h_q", align_bytes=64)
-            h_sc = ring.tile([P, width], U8, name="h_sc", tag="h_sc", align_bytes=64)
-            nc.vector.quantize_mx(out=h_q[:].bitcast(FP8X4), scales=h_sc[:], in_=h_bf[:].rearrange("p n t -> p (n t)"))
+        def quantize_h(h_bf, h_q):
+            h_sc = ring.tile([P, h_bf.shape[1]], U8, name="h_sc", tag="h_sc", align_bytes=64, bufs=5)
+            nc.vector.quantize_mx(out=h_q.bitcast(FP8X4), scales=h_sc[:], in_=h_bf.rearrange("p n t -> p (n t)"))
             return h_q, h_sc
 
         def readout_pass(dst, c, h_q, h_sc):
@@ -198,7 +215,7 @@ def tile_list_cloth_stretch_features_kernel(
                 out=dst,
                 lhsT=w4_q[:, P * c : P * (c + 1)].bitcast(FP8X4),
                 lhsT_scale=w4_sc[:, P * c : P * (c + 1)],
-                rhs=h_q[:].bitcast(FP8X4),
+                rhs=h_q.bitcast(FP8X4),
                 rhs_scale=h_sc[:],
                 start=True,
                 stop=True,
@@ -206,86 +223,110 @@ def tile_list_cloth_stretch_features_kernel(
 
         out_view = out.rearrange("(c p) j -> p c j", p=P)
 
-        def readout_wide(h_q, h_sc, lo):
-            y_a = y_psum.tile([P, 2, 256], F32, name="y_a", tag="y_a")
-            y_b = y_psum.tile([P, 256], F32, name="y_b", tag="y_b")
+        def readout_wide(h_q, h_sc, first):
+            y_a = psum.tile([P, 2, 256], F32, name="y_a", tag=f"bank{first}")
+            y_b = psum.tile([P, 256], F32, name="y_b", tag=f"bank{first + 1}")
             ys = [y_a[:, 0, :], y_a[:, 1, :], y_b[:]]
-            res = ring.tile([P, TILES_N, 256], F32, name="res", tag="res", bufs=3)
             for c in range(TILES_N):
                 readout_pass(ys[c], c, h_q, h_sc)
+            return ys
+
+        def finish_wide(ys, lo):
+            res = ring.tile([P, TILES_N, 256], F32, name="res", tag="res", bufs=5)
             for c in range(TILES_N):
                 nc.scalar.activation(out=res[:, c, :], in_=ys[c], func=ACT.Identity, bias=b_col[:, c : c + 1])
             nc.sync.dma_start(out=out_view[:, :, lo : lo + 256], in_=res[:])
 
-        def readout_narrow(h_q, h_sc, lo, tag):
-            y = y_psum.tile([P, TILES_N, P], F32, name=tag, tag=tag)
-            res = ring.tile([P, TILES_N, P], F32, name="res", tag="res", bufs=3)
+        def readout_narrow(h_q, h_sc, bank):
+            y = psum.tile([P, TILES_N, P], F32, name="y", tag=f"bank{bank}")
             for c in range(TILES_N):
                 readout_pass(y[:, c, :], c, h_q, h_sc)
+            return y
+
+        def finish_narrow(y, lo):
+            res = ring.tile([P, TILES_N, P], F32, name="res", tag="res", bufs=5)
             nc.vector.tensor_tensor(
                 out=res[:], in0=y[:], in1=b_col[:].unsqueeze(2).to_broadcast([P, TILES_N, P]), op=ALU.add
             )
             nc.sync.dma_start(out=out_view[:, :, lo : lo + P], in_=res[:])
 
-        nc.vector.tensor_copy(out=v2_sc[:], in_=table_sc[:].indirect(lists[1][:]))
-        nc.scalar.dma_start(out=v2_sc_pass1[0:112, :].bitcast(I32), in_=v2_sc[4:116, :].bitcast(I32))
         sc_first = keep.tile([P, 2, 512], U8, name="sc_first", align_bytes=64)
         words_free = keep.tile([P, 512], U32, name="words_free", align_bytes=64)
         gather_scales(2, 0, 512, sc_first[:, 0, :])
-        banks = new_banks(512)
+        banks = new_banks(512, 0)
         gather_words(2, 0, 0, 512, words_free[:])
-        reorder_columns(w3_q[:], w3_raw[:], 8)
-        reorder_columns(w3_sc[:].bitcast(I32), w3_sc_raw[:].bitcast(I32), 2)
+        reorder_columns(nc.vector, w3_q[:], w3_raw[:], 8)
+        reorder_columns(nc.gpsimd, w3_sc[:].bitcast(I32), w3_sc_raw[:].bitcast(I32), 2)
         d_passes(banks, 2, 0, 0, 512, start=True)
-        gather_scales(0, 0, 512, sc_first[:, 1, :])
-        words_a = keep.tile([P, 512], U32, name="words_a", tag="slot_a", align_bytes=64)
+        words_a = keep.tile([P, 512], U32, name="words_a", tag="w3_raw", align_bytes=64)
         gather_words(1, 0, 0, 512, words_a[:])
-        reorder_columns(w2_q[:].bitcast(I32), w2_raw[:], 4)
-        reorder_columns(w2_sc[:].bitcast(I32), w2_sc_raw[:].bitcast(I32), 2)
+        gather_scales(0, 0, 512, sc_first[:, 1, :])
+        reorder_columns(nc.gpsimd, w2_q[:].bitcast(I32), w2_raw[:], 4)
+        reorder_columns(nc.gpsimd, w2_sc[:].bitcast(I32), w2_sc_raw[:].bitcast(I32), 2)
         d_passes(banks, 1, 0, 0, 512)
-        words_b = keep.tile([P, 4, 512], U32, name="words_b", tag="slot_b", align_bytes=64)
+        words_b = keep.tile([P, 3, 512], U32, name="words_b", align_bytes=64)
         for place, (m, a) in enumerate(((2, 1), (1, 1))):
             gather_words(m, a, 0, 512, words_b[:, place, :])
             d_passes(banks, m, a, 0, 512)
-        for a in range(PASSES):
-            cast_w1(a)
-            gather_words(0, a, 0, 512, words_b[:, 2 + a, :])
-            quantize_w1(a)
-            d_passes(banks, 0, a, 0, 512, stop=(a == PASSES - 1))
-        nc.scalar.copy(out=w4_bf[:], in_=w4_raw[:].rearrange("p t n -> p n t"))
-        sq_first = square(banks, 0, 512)
+        cast_w1(0)
+        gather_words(0, 0, 0, 512, words_b[:, 2, :])
+        quantize_w1(0)
+        d_passes(banks, 0, 0, 0, 512)
+        cast_w1(1)
+        words_f = keep.tile([P, 512], U32, name="words_f", tag="w1_bf01", align_bytes=64)
+        gather_words(0, 1, 0, 512, words_f[:])
+        quantize_w1(1)
+        d_passes(banks, 0, 1, 0, 512, stop=True)
+        for u, (lo, hi) in enumerate(w4_cols):
+            nc.scalar.copy(out=w4_bf[u][:], in_=w4_raw[:, :, lo:hi].rearrange("p t n -> p n t"))
+        mag_first = [magnitude(square(banks, 256 * u, 256 * u + 256, ("w4_raw", "sq1")[u]), 0, 256) for u in range(2)]
 
         order = ((2, 0), (1, 0), (2, 1), (1, 1), (0, 0), (0, 1))
 
-        def stretch(lo, hi, places):
-            chunk_banks = new_banks(hi - lo)
-            for step, (m, a) in enumerate(order):
-                gather_words(m, a, lo, hi, places[step])
+        def stretch(chunk_banks, lo, hi, steps, places):
+            for step, place in zip(steps, places):
+                m, a = order[step]
+                gather_words(m, a, lo, hi, place)
                 d_passes(chunk_banks, m, a, lo, hi, start=(step == 0), stop=(step == len(order) - 1))
-            return chunk_banks
 
-        sc_second = keep.tile([P, 2, 512], U8, name="sc_second", tag="w1_bf10", align_bytes=64)
+        sc_second = keep.tile([P, 2, 512], U8, name="sc_second", tag="w1_bf11", align_bytes=64)
         gather_scales(2, 512, S, sc_second[:, 0, :])
         gather_scales(0, 512, S, sc_second[:, 1, :])
-        for lo, hi in ((0, 256), (256, N)):
+        for u, (lo, hi) in enumerate(w4_cols):
             nc.vector.quantize_mx(
                 out=w4_q[:, lo:hi].bitcast(FP8X4),
                 scales=w4_sc[:, lo:hi],
-                in_=w4_bf[:, lo:hi, :].rearrange("p n t -> p (n t)"),
+                in_=w4_bf[u][:].rearrange("p n t -> p (n t)"),
             )
-        h_first = [stiffen(nc.gpsimd, magnitude(sq_first, 256 * u, 256 * u + 256), 256, f"h_bf{u}") for u in range(2)]
-        words_c = keep.tile([P, 6, 256], U32, name="words_c", tag="w1_bf11", align_bytes=64)
-        banks = stretch(512, 768, [words_c[:, step, :] for step in range(6)])
+        h_zero = [stiffen(nc.gpsimd, mag_first[0][:, :, P * u : P * (u + 1)], new_h_bf(P, f"h_bf0{u}")) for u in range(2)]
+        words_c = keep.tile([P, 6, 256], U32, name="words_c", tag="w4_bf1", align_bytes=64)
+        banks = new_banks(256, 4)
+        stretch(banks, 512, 768, range(6), [words_c[:, step, :] for step in range(6)])
+        mag_third = magnitude(square(banks, 0, 256, "sq1"), 0, 256)
+        h_q0 = new_h_q(256, "h_q0")
+        h_sc0 = keep.tile([P, 256], U8, name="h_sc0", align_bytes=64)
         for u in range(2):
-            readout_wide(*quantize_h(h_first[u], 256), 256 * u)
-        mag_third = magnitude(square(banks, 0, 256), 0, 256)
-        words_d = keep.tile([P, 2, 256], U32, name="words_d", tag="w4_bf", align_bytes=64)
-        words_e = keep.tile([P, 4, 256], U32, name="words_e", tag="h_bf0", align_bytes=64)
-        banks = stretch(768, S, [words_d[:, step, :] for step in range(2)] + [words_e[:, step, :] for step in range(4)])
-        mags = [magnitude(square(banks, lo, lo + P), 0, P) for lo in (0, P)]
-        h_third = quantize_h(stiffen(nc.vector, mag_third, 256, "h_bf2"), 256)
-        h_last = [quantize_h(stiffen(nc.vector, mags[0], P, "h_bf3"), P)]
-        readout_wide(*h_third, 512)
-        h_last.append(quantize_h(stiffen(nc.vector, mags[1], P, "h_bf4"), P))
-        readout_narrow(*h_last[0], 768, "y_b")
-        readout_narrow(*h_last[1], 896, "y_a")
+            nc.vector.quantize_mx(
+                out=h_q0[:, P * u : P * (u + 1)].bitcast(FP8X4),
+                scales=h_sc0[:, P * u : P * (u + 1)],
+                in_=h_zero[u].rearrange("p n t -> p (n t)"),
+            )
+        finish_wide(readout_wide(h_q0, h_sc0, 4), 0)
+        h_one = stiffen(nc.gpsimd, mag_first[1], new_h_bf(256, "h_bf01"))
+        words_e = keep.tile([P, 5, 256], U32, name="words_e", tag="h_bf00", align_bytes=64)
+        words_g = keep.tile([P, 256], U32, name="words_g", tag="h_q0", align_bytes=64)
+        banks = new_banks(256, 0)
+        stretch(banks, 768, S, range(6), [words_e[:, step, :] for step in range(5)] + [words_g[:]])
+        sq_last = square(banks, 0, 256, "sq1")
+        mag_last = [magnitude(sq_last, lo, lo + P) for lo in (0, P)]
+        y_second = readout_wide(*quantize_h(h_one, new_h_q(256, "table1")), 6)
+        h_third = stiffen(nc.vector, mag_third, new_h_bf(256, "h_bf01"))
+        y_third = readout_wide(*quantize_h(h_third, new_h_q(256, "h_q2")), 4)
+        y_last = []
+        for u in range(2):
+            h_last = stiffen(nc.vector, mag_last[u], new_h_bf(P, f"h_bf3{u}"))
+            y_last.append(readout_narrow(*quantize_h(h_last, new_h_q(P, f"h_q3{u}")), u))
+        finish_wide(y_second, 256)
+        finish_wide(y_third, 512)
+        for u in range(2):
+            finish_narrow(y_last[u], 768 + P * u)

@@ -34,15 +34,15 @@ def tile_list_cloth_stretch_features_kernel(
         lists = [keep.tile([P, S // 16], U16, name=f"list{m}") for m in range(3)]
         table = [keep.tile([P, T], I32, name=f"table{a}", tag=f"table{a}", align_bytes=64) for a in range(PASSES)]
         table_sc = keep.tile([P, T], U8, name="table_sc", align_bytes=64)
-        w3_sc_raw = keep.tile([P, PASSES, H], U8, name="w3_sc_raw", align_bytes=64)
-        w2_sc_raw = keep.tile([P, PASSES, H], U8, name="w2_sc_raw", align_bytes=64)
+        w3_sc_raw = keep.tile([P, PASSES, H], U8, name="w3_sc_raw", tag="slot_a", align_bytes=64)
+        w2_sc_raw = keep.tile([P, PASSES, H], U8, name="w2_sc_raw", tag="slot_b", align_bytes=64)
         w3_sc = keep.tile([P, SLOTS, PASSES, P], U8, name="w3_sc", align_bytes=64)
         w2_sc = keep.tile([P, SLOTS, PASSES, P], U8, name="w2_sc", align_bytes=64)
-        w3_raw = keep.tile([P, PASSES, H], I32, name="w3_raw", tag="w3_raw", align_bytes=64)
+        w3_raw = keep.tile([P, PASSES, H], I32, name="w3_raw", align_bytes=64)
         w3_q = keep.tile([P, SLOTS, PASSES, P], I32, name="w3_q", align_bytes=64)
         w2_raw = keep.tile([P, PASSES, H // 2], I32, name="w2_raw", align_bytes=64)
         w2_q = keep.tile([P, SLOTS, PASSES, 2 * P], U8, name="w2_q", align_bytes=64)
-        w1_raw = [keep.tile([P, 4, H], F32, name=f"w1_raw{a}") for a in range(PASSES)]
+        w1_raw = [keep.tile([P, 4, H], F32, name=f"w1_raw{a}", tag=f"w1_raw{a}", align_bytes=64) for a in range(PASSES)]
         w1_bf = [
             [keep.tile([P, 2, 4 * P], BF16, name=f"w1_bf{a}{u}", tag=f"w1_bf{a}{u}", align_bytes=64) for u in range(2)]
             for a in range(PASSES)
@@ -55,13 +55,14 @@ def tile_list_cloth_stretch_features_kernel(
             keep.tile([P, hi - lo, SLOTS], BF16, name=f"w4_bf{u}", tag=f"w4_bf{u}", align_bytes=64)
             for u, (lo, hi) in enumerate(w4_cols)
         ]
-        w4_q = keep.tile([P, N], U32, name="w4_q", align_bytes=64)
         w4_sc = keep.tile([P, N], U8, name="w4_sc", align_bytes=64)
         g_col = keep.tile([P, SLOTS, 8], F32, name="g_col")
+        g_slots = keep.tile([P, SLOTS], F32, name="g_slots")
         b_col = keep.tile([P, TILES_N], F32, name="b_col")
         ones = keep.tile([P, 1], F32, name="ones")
         one = keep.tile([P, 1], F32, name="one")
         v_q = {}
+        late = {}
         v_sc = {}
         v2_sc = keep.tile([P, S], U8, name="v2_sc", align_bytes=64)
         v2_sc_pass1 = keep.tile([P, S], U8, name="v2_sc_pass1", align_bytes=64)
@@ -169,8 +170,8 @@ def tile_list_cloth_stretch_features_kernel(
                     in_=w1_bf[a][u][:].rearrange("p t c -> p (t c)"),
                 )
 
-        def reorder_columns(engine, dst, src, run):
-            engine.tensor_copy(
+        def reorder_columns(dst, src, run):
+            nc.vector.tensor_copy(
                 out=dst.rearrange("p t a (b i) -> p t (a b) i", i=run),
                 in_=src.rearrange("p a (b t i) -> p t (a b) i", t=SLOTS, i=run),
             )
@@ -195,12 +196,12 @@ def tile_list_cloth_stretch_features_kernel(
         def new_h_q(width, tag):
             return keep.tile([P, width], U32, name=tag, tag=tag, align_bytes=64)[:]
 
-        def stiffen(engine, mag, h_bf):
+        def stiffen(mag, h_bf):
             width = h_bf.shape[1]
-            engine.tensor_tensor(
+            nc.vector.tensor_tensor(
                 out=h_bf,
                 in0=mag.rearrange("p t n -> p n t"),
-                in1=g_col[:, :, 0].unsqueeze(1).to_broadcast([P, width, SLOTS]),
+                in1=g_slots[:].unsqueeze(1).to_broadcast([P, width, SLOTS]),
                 op=ALU.mult,
             )
             return h_bf
@@ -211,6 +212,7 @@ def tile_list_cloth_stretch_features_kernel(
             return h_q, h_sc
 
         def readout_pass(dst, c, h_q, h_sc):
+            w4_q = late["w4_q"]
             nc.tensor.matmul_mx(
                 out=dst,
                 lhsT=w4_q[:, P * c : P * (c + 1)].bitcast(FP8X4),
@@ -243,6 +245,12 @@ def tile_list_cloth_stretch_features_kernel(
                 readout_pass(y[:, c, :], c, h_q, h_sc)
             return y
 
+        def finish_narrow_scalar(y, lo):
+            res = ring.tile([P, TILES_N, P], F32, name="res", tag="res", bufs=5)
+            for c in range(TILES_N):
+                nc.scalar.activation(out=res[:, c, :], in_=y[:, c, :], func=ACT.Identity, bias=b_col[:, c : c + 1])
+            nc.sync.dma_start(out=out_view[:, :, lo : lo + P], in_=res[:])
+
         def finish_narrow(y, lo):
             res = ring.tile([P, TILES_N, P], F32, name="res", tag="res", bufs=5)
             nc.vector.tensor_tensor(
@@ -255,16 +263,16 @@ def tile_list_cloth_stretch_features_kernel(
         gather_scales(2, 0, 512, sc_first[:, 0, :])
         banks = new_banks(512, 0)
         gather_words(2, 0, 0, 512, words_free[:])
-        reorder_columns(nc.vector, w3_q[:], w3_raw[:], 8)
-        reorder_columns(nc.gpsimd, w3_sc[:].bitcast(I32), w3_sc_raw[:].bitcast(I32), 2)
+        reorder_columns(w3_q[:], w3_raw[:], 8)
+        reorder_columns(w3_sc[:].bitcast(I32), w3_sc_raw[:].bitcast(I32), 2)
         d_passes(banks, 2, 0, 0, 512, start=True)
-        words_a = keep.tile([P, 512], U32, name="words_a", tag="w3_raw", align_bytes=64)
+        words_a = keep.tile([P, 512], U32, name="words_a", tag="slot_a", align_bytes=64)
         gather_words(1, 0, 0, 512, words_a[:])
         gather_scales(0, 0, 512, sc_first[:, 1, :])
-        reorder_columns(nc.gpsimd, w2_q[:].bitcast(I32), w2_raw[:], 4)
-        reorder_columns(nc.gpsimd, w2_sc[:].bitcast(I32), w2_sc_raw[:].bitcast(I32), 2)
+        reorder_columns(w2_q[:].bitcast(I32), w2_raw[:], 4)
+        reorder_columns(w2_sc[:].bitcast(I32), w2_sc_raw[:].bitcast(I32), 2)
         d_passes(banks, 1, 0, 0, 512)
-        words_b = keep.tile([P, 3, 512], U32, name="words_b", align_bytes=64)
+        words_b = keep.tile([P, 3, 512], U32, name="words_b", tag="slot_b", align_bytes=64)
         for place, (m, a) in enumerate(((2, 1), (1, 1))):
             gather_words(m, a, 0, 512, words_b[:, place, :])
             d_passes(banks, m, a, 0, 512)
@@ -279,6 +287,7 @@ def tile_list_cloth_stretch_features_kernel(
         d_passes(banks, 0, 1, 0, 512, stop=True)
         for u, (lo, hi) in enumerate(w4_cols):
             nc.scalar.copy(out=w4_bf[u][:], in_=w4_raw[:, :, lo:hi].rearrange("p t n -> p n t"))
+        nc.scalar.copy(out=g_slots[:], in_=g_col[:, :, 0])
         mag_first = [magnitude(square(banks, 256 * u, 256 * u + 256, ("w4_raw", "sq1")[u]), 0, 256) for u in range(2)]
 
         order = ((2, 0), (1, 0), (2, 1), (1, 1), (0, 0), (0, 1))
@@ -292,41 +301,33 @@ def tile_list_cloth_stretch_features_kernel(
         sc_second = keep.tile([P, 2, 512], U8, name="sc_second", tag="w1_bf11", align_bytes=64)
         gather_scales(2, 512, S, sc_second[:, 0, :])
         gather_scales(0, 512, S, sc_second[:, 1, :])
-        for u, (lo, hi) in enumerate(w4_cols):
-            nc.vector.quantize_mx(
-                out=w4_q[:, lo:hi].bitcast(FP8X4),
-                scales=w4_sc[:, lo:hi],
-                in_=w4_bf[u][:].rearrange("p n t -> p (n t)"),
-            )
-        h_zero = [stiffen(nc.gpsimd, mag_first[0][:, :, P * u : P * (u + 1)], new_h_bf(P, f"h_bf0{u}")) for u in range(2)]
-        words_c = keep.tile([P, 6, 256], U32, name="words_c", tag="w4_bf1", align_bytes=64)
+        scaled = keep.tile([P, SLOTS, 256], F32, name="scaled")
+        for t in range(SLOTS):
+            nc.scalar.activation(out=scaled[:, t, :], in_=mag_first[0][:, t, :], func=ACT.Copy, scale=g_slots[:, t : t + 1])
+        h_zero = new_h_bf(256, "h_bf")
+        nc.scalar.copy(out=h_zero, in_=scaled[:].rearrange("p t n -> p n t"))
+        words_c = keep.tile([P, 12, 256], U32, name="words_c", tag="w1_raw1", align_bytes=64)
         banks = new_banks(256, 4)
         stretch(banks, 512, 768, range(6), [words_c[:, step, :] for step in range(6)])
         mag_third = magnitude(square(banks, 0, 256, "sq1"), 0, 256)
-        h_q0 = new_h_q(256, "h_q0")
-        h_sc0 = keep.tile([P, 256], U8, name="h_sc0", align_bytes=64)
-        for u in range(2):
-            nc.vector.quantize_mx(
-                out=h_q0[:, P * u : P * (u + 1)].bitcast(FP8X4),
-                scales=h_sc0[:, P * u : P * (u + 1)],
-                in_=h_zero[u].rearrange("p n t -> p (n t)"),
-            )
-        finish_wide(readout_wide(h_q0, h_sc0, 4), 0)
-        h_one = stiffen(nc.gpsimd, mag_first[1], new_h_bf(256, "h_bf01"))
-        words_e = keep.tile([P, 5, 256], U32, name="words_e", tag="h_bf00", align_bytes=64)
-        words_g = keep.tile([P, 256], U32, name="words_g", tag="h_q0", align_bytes=64)
         banks = new_banks(256, 0)
-        stretch(banks, 768, S, range(6), [words_e[:, step, :] for step in range(5)] + [words_g[:]])
+        stretch(banks, 768, S, range(6), [words_c[:, 6 + step, :] for step in range(6)])
         sq_last = square(banks, 0, 256, "sq1")
         mag_last = [magnitude(sq_last, lo, lo + P) for lo in (0, P)]
-        y_second = readout_wide(*quantize_h(h_one, new_h_q(256, "table1")), 6)
-        h_third = stiffen(nc.vector, mag_third, new_h_bf(256, "h_bf01"))
-        y_third = readout_wide(*quantize_h(h_third, new_h_q(256, "h_q2")), 4)
-        y_last = []
-        for u in range(2):
-            h_last = stiffen(nc.vector, mag_last[u], new_h_bf(P, f"h_bf3{u}"))
-            y_last.append(readout_narrow(*quantize_h(h_last, new_h_q(P, f"h_q3{u}")), u))
-        finish_wide(y_second, 256)
-        finish_wide(y_third, 512)
-        for u in range(2):
-            finish_narrow(y_last[u], 768 + P * u)
+        late["w4_q"] = keep.tile([P, N], U32, name="w4_q", tag="table1", align_bytes=64)
+        for u, (lo, hi) in enumerate(w4_cols):
+            nc.vector.quantize_mx(
+                out=late["w4_q"][:, lo:hi].bitcast(FP8X4),
+                scales=w4_sc[:, lo:hi],
+                in_=w4_bf[u][:].rearrange("p n t -> p (n t)"),
+            )
+        y_wide = [readout_wide(*quantize_h(h_zero, new_h_q(256, "w4_bf0")), 4)]
+        y_wide.append(readout_wide(*quantize_h(stiffen(mag_first[1], new_h_bf(256, "h_bf")), new_h_q(256, "h_q1")), 6))
+        h_third = quantize_h(stiffen(mag_third, new_h_bf(256, "h_bf")), new_h_q(256, "h_q2"))
+        y_wide.append(readout_wide(*h_third, 0))
+        h_last = [stiffen(mag_last[u], new_h_bf(P, f"h_bf3{u}")) for u in range(2)]
+        y_last = [readout_narrow(*quantize_h(h_last[u], new_h_q(P, f"h_q3{u}")), 2 + u) for u in range(2)]
+        for u in range(3):
+            finish_wide(y_wide[u], 256 * u)
+        finish_narrow_scalar(y_last[0], 768)
+        finish_narrow(y_last[1], 768 + P)

@@ -154,11 +154,17 @@ def tile_list_cloth_stretch_features_kernel(
                     stop=stop,
                 )
 
+        def by_fours_in(planes):
+            return planes.rearrange("p t (c i) -> p c t i", i=4)
+
+        def by_fours_out(words):
+            return words.rearrange("p (c i) t -> p c t i", i=4)
+
         def cast_w1(a):
             for t in range(SLOTS):
                 nc.scalar.copy(
-                    out=w1_bf[a][t // 2][:, t % 2, :].rearrange("p (b i j) -> p b i j", i=8, j=4),
-                    in_=w1_raw[a][:].rearrange("p j (b t i) -> p t b i j", t=SLOTS, i=8)[:, t],
+                    out=w1_bf[a][t // 2][:, t % 2, :].rearrange("p (b i j) -> p b j i", i=8, j=4),
+                    in_=w1_raw[a][:].rearrange("p j (b t i) -> p t b j i", t=SLOTS, i=8)[:, t],
                 )
 
         def quantize_w1(a):
@@ -199,9 +205,9 @@ def tile_list_cloth_stretch_features_kernel(
         def stiffen(mag, h_bf):
             width = h_bf.shape[1]
             nc.vector.tensor_tensor(
-                out=h_bf,
-                in0=mag.rearrange("p t n -> p n t"),
-                in1=g_slots[:].unsqueeze(1).to_broadcast([P, width, SLOTS]),
+                out=by_fours_out(h_bf),
+                in0=by_fours_in(mag),
+                in1=g_slots[:].unsqueeze(1).unsqueeze(3).to_broadcast([P, width // 4, SLOTS, 4]),
                 op=ALU.mult,
             )
             return h_bf
@@ -233,11 +239,10 @@ def tile_list_cloth_stretch_features_kernel(
                 readout_pass(ys[c], c, h_q, h_sc)
             return ys
 
-        def finish_wide(ys, lo):
-            res = ring.tile([P, TILES_N, 256], F32, name="res", tag="res", bufs=5)
+        def finish_wide(ys, lo, res):
             for c in range(TILES_N):
                 nc.scalar.activation(out=res[:, c, :], in_=ys[c], func=ACT.Identity, bias=b_col[:, c : c + 1])
-            nc.sync.dma_start(out=out_view[:, :, lo : lo + 256], in_=res[:])
+                nc.sync.dma_start(out=out_view[:, c, lo : lo + 256], in_=res[:, c, :])
 
         def readout_narrow(h_q, h_sc, bank):
             y = psum.tile([P, TILES_N, P], F32, name="y", tag=f"bank{bank}")
@@ -286,9 +291,10 @@ def tile_list_cloth_stretch_features_kernel(
         quantize_w1(1)
         d_passes(banks, 0, 1, 0, 512, stop=True)
         for u, (lo, hi) in enumerate(w4_cols):
-            nc.scalar.copy(out=w4_bf[u][:], in_=w4_raw[:, :, lo:hi].rearrange("p t n -> p n t"))
+            nc.scalar.copy(out=by_fours_out(w4_bf[u][:]), in_=by_fours_in(w4_raw[:, :, lo:hi]))
         nc.scalar.copy(out=g_slots[:], in_=g_col[:, :, 0])
-        mag_first = [magnitude(square(banks, 256 * u, 256 * u + 256, ("w4_raw", "sq1")[u]), 0, 256) for u in range(2)]
+        sq_first = square(banks, 0, 512, "w4_raw")
+        mag_first = [magnitude(sq_first, 256 * u, 256 * u + 256) for u in range(2)]
 
         order = ((2, 0), (1, 0), (2, 1), (1, 1), (0, 0), (0, 1))
 
@@ -305,29 +311,32 @@ def tile_list_cloth_stretch_features_kernel(
         for t in range(SLOTS):
             nc.scalar.activation(out=scaled[:, t, :], in_=mag_first[0][:, t, :], func=ACT.Copy, scale=g_slots[:, t : t + 1])
         h_zero = new_h_bf(256, "h_bf")
-        nc.scalar.copy(out=h_zero, in_=scaled[:].rearrange("p t n -> p n t"))
+        nc.scalar.copy(out=by_fours_out(h_zero), in_=by_fours_in(scaled[:]))
         words_c = keep.tile([P, 12, 256], U32, name="words_c", tag="w1_raw1", align_bytes=64)
         banks = new_banks(256, 4)
         stretch(banks, 512, 768, range(6), [words_c[:, step, :] for step in range(6)])
-        mag_third = magnitude(square(banks, 0, 256, "sq1"), 0, 256)
+        mag_third = magnitude(square(banks, 0, 256, "w4_raw"), 0, 256)
         banks = new_banks(256, 0)
         stretch(banks, 768, S, range(6), [words_c[:, 6 + step, :] for step in range(6)])
-        sq_last = square(banks, 0, 256, "sq1")
+        sq_last = square(banks, 0, 256, "w4_raw")
         mag_last = [magnitude(sq_last, lo, lo + P) for lo in (0, P)]
-        late["w4_q"] = keep.tile([P, N], U32, name="w4_q", tag="table1", align_bytes=64)
+        late["w4_q"] = keep.tile([P, N], U32, name="w4_q", tag="table0", align_bytes=64)
         for u, (lo, hi) in enumerate(w4_cols):
             nc.vector.quantize_mx(
                 out=late["w4_q"][:, lo:hi].bitcast(FP8X4),
                 scales=w4_sc[:, lo:hi],
                 in_=w4_bf[u][:].rearrange("p n t -> p (n t)"),
             )
+        h_one = stiffen(mag_first[1], new_h_bf(256, "table1"))
         y_wide = [readout_wide(*quantize_h(h_zero, new_h_q(256, "w4_bf0")), 4)]
-        y_wide.append(readout_wide(*quantize_h(stiffen(mag_first[1], new_h_bf(256, "h_bf")), new_h_q(256, "h_q1")), 6))
-        h_third = quantize_h(stiffen(mag_third, new_h_bf(256, "h_bf")), new_h_q(256, "h_q2"))
-        y_wide.append(readout_wide(*h_third, 0))
-        h_last = [stiffen(mag_last[u], new_h_bf(P, f"h_bf3{u}")) for u in range(2)]
+        h_two = stiffen(mag_third, new_h_bf(256, "w4_bf1"))
+        y_wide.append(readout_wide(*quantize_h(h_one, new_h_q(256, "h_q1")), 6))
+        h_last = [stiffen(mag_last[0], new_h_bf(P, "h_bf30"))]
+        y_wide.append(readout_wide(*quantize_h(h_two, new_h_q(256, "h_q2")), 0))
+        h_last.append(stiffen(mag_last[1], new_h_bf(P, "h_bf31")))
         y_last = [readout_narrow(*quantize_h(h_last[u], new_h_q(P, f"h_q3{u}")), 2 + u) for u in range(2)]
+        res_wide = keep.tile([P, 3, TILES_N, 256], F32, name="res_wide", tag="w4_raw")
         for u in range(3):
-            finish_wide(y_wide[u], 256 * u)
+            finish_wide(y_wide[u], 256 * u, res_wide[:, u])
         finish_narrow_scalar(y_last[0], 768)
         finish_narrow(y_last[1], 768 + P)

@@ -306,7 +306,6 @@ def tile_list_cloth_stretch_features_kernel(
 
         sc_second = keep.tile([P, 2, 512], U8, name="sc_second", tag="w1_bf11", align_bytes=64)
         gather_scales(2, 512, S, sc_second[:, 0, :])
-        gather_scales(0, 512, S, sc_second[:, 1, :])
         scaled = keep.tile([P, SLOTS, 256], F32, name="scaled")
         for t in range(SLOTS):
             nc.scalar.activation(out=scaled[:, t, :], in_=mag_first[0][:, t, :], func=ACT.Copy, scale=g_slots[:, t : t + 1])
@@ -314,7 +313,9 @@ def tile_list_cloth_stretch_features_kernel(
         nc.scalar.copy(out=by_fours_out(h_zero), in_=by_fours_in(scaled[:]))
         words_c = keep.tile([P, 12, 256], U32, name="words_c", tag="w1_raw1", align_bytes=64)
         banks = new_banks(256, 4)
-        stretch(banks, 512, 768, range(6), [words_c[:, step, :] for step in range(6)])
+        stretch(banks, 512, 768, range(4), [words_c[:, step, :] for step in range(4)])
+        gather_scales(0, 512, S, sc_second[:, 1, :])
+        stretch(banks, 512, 768, range(4, 6), [words_c[:, step, :] for step in range(4, 6)])
         mag_third = magnitude(square(banks, 0, 256, "w4_raw"), 0, 256)
         banks = new_banks(256, 0)
         stretch(banks, 768, S, range(6), [words_c[:, 6 + step, :] for step in range(6)])

@@ -34,9 +34,9 @@ def tile_list_cloth_stretch_features_kernel(
         lists = [keep.tile([P, S // 16], U16, name=f"list{m}") for m in range(3)]
         table = [keep.tile([P, T], I32, name=f"table{a}", tag=f"table{a}", align_bytes=64) for a in range(PASSES)]
         table_sc = keep.tile([P, T], U8, name="table_sc", align_bytes=64)
-        w3_sc_raw = keep.tile([P, PASSES, H], U8, name="w3_sc_raw", tag="slot_a", align_bytes=64)
+        w3_sc_raw = keep.tile([P, H], U8, name="w3_sc_raw", tag="slot_a", align_bytes=64)
         w2_sc_raw = keep.tile([P, PASSES, H], U8, name="w2_sc_raw", tag="slot_b", align_bytes=64)
-        w3_sc = keep.tile([P, SLOTS, PASSES, P], U8, name="w3_sc", align_bytes=64)
+        w3_sc = keep.tile([P, SLOTS, P], U8, name="w3_sc", align_bytes=64)
         w2_sc = keep.tile([P, SLOTS, PASSES, P], U8, name="w2_sc", align_bytes=64)
         w3_raw = keep.tile([P, PASSES, H], I32, name="w3_raw", align_bytes=64)
         w3_q = keep.tile([P, SLOTS, PASSES, P], I32, name="w3_q", align_bytes=64)
@@ -69,7 +69,7 @@ def tile_list_cloth_stretch_features_kernel(
 
         nc.gpsimd.memset(table_sc[:].bitcast(I32), 0)
         nc.gpsimd.memset(ones[:], 1.0)
-        nc.gpsimd.memset(w3_sc_raw[:].rearrange("p a c -> p (a c)").bitcast(I32), 0)
+        nc.gpsimd.memset(w3_sc_raw[:].bitcast(I32), 0)
         nc.gpsimd.memset(w2_sc_raw[:].rearrange("p a c -> p (a c)").bitcast(I32), 0)
         nc.gpsimd.memset(v2_sc_pass1[:].bitcast(I32), 0)
         nc.scalar.activation(out=one[:], in_=ones[:], func=ACT.Sqrt)
@@ -89,25 +89,32 @@ def tile_list_cloth_stretch_features_kernel(
         nc.sync.dma_start(out=w3_raw[:], in_=w3_words.rearrange("a p c i -> p a (c i)").bitcast(I32))
         nc.sync.dma_start(out=w2_raw[:], in_=w2_words.rearrange("a p c -> p a c").bitcast(I32))
 
-        def load_weight_scales(plane, scales):
+        def load_w3_scales():
             for q in range(4):
                 nc.sync.dma_start(
-                    out=plane[32 * q : 32 * q + 4, :, :].bitcast(I32),
-                    in_=scales[:, 4 * q : 4 * q + 4, :].rearrange("a r c -> r a c").bitcast(I32),
+                    out=w3_sc_raw[32 * q : 32 * q + 8, :].bitcast(I32),
+                    in_=w3_scales[:, 4 * q : 4 * q + 4, :].bitcast(I32),
+                )
+
+        def load_w2_scales():
+            for r in range(4):
+                nc.sync.dma_start(
+                    out=w2_sc_raw[r:P:32, :, :].bitcast(I32),
+                    in_=w2_scales.rearrange("a (q r) c -> r q a c", r=4)[r].bitcast(I32),
                 )
 
         def load_w1(a):
             nc.sync.dma_start(out=w1_raw[a][:], in_=w1[512 * a : 512 * (a + 1), :].rearrange("(p j) r -> p j r", j=4))
 
-        load_weight_scales(w3_sc_raw, w3_scales)
+        load_w3_scales()
         load_table(1)
         nc.sync.dma_start(lists[0][:], offs)
-        load_weight_scales(w2_sc_raw, w2_scales)
+        load_w2_scales()
         load_w1(0)
-        nc.sync.dma_start(out=v2_sc_pass1[0:112, :].bitcast(I32), in_=v2_sc[4:116, :].bitcast(I32))
         load_w1(1)
         for t in range(SLOTS):
             nc.sync.dma_start(out=w4_raw[:, t, :], in_=w4.rearrange("(b t i) n -> t b i n", t=SLOTS, i=8)[t])
+        nc.sync.dma_start(out=v2_sc_pass1[0:112, :].bitcast(I32), in_=v2_sc[4:116, :].bitcast(I32))
         with nc.allow_non_contiguous_dma(reason="one value a partition"):
             for t in range(SLOTS):
                 nc.sync.dma_start(
@@ -143,7 +150,7 @@ def tile_list_cloth_stretch_features_kernel(
                 if m == 0:
                     lhs, lhs_sc = w1_q[:, a, P * t : P * (t + 1)], w1_sc[:, a, P * t : P * (t + 1)]
                 else:
-                    lhs, lhs_sc = w3_q[:, t, a, :], w3_sc[:, t, a, :]
+                    lhs, lhs_sc = w3_q[:, t, a, :], w3_sc[4 * a : P, t, :]
                 nc.tensor.matmul_mx(
                     out=banks[t][:],
                     lhsT=lhs.bitcast(FP8X4),
@@ -269,7 +276,10 @@ def tile_list_cloth_stretch_features_kernel(
         banks = new_banks(512, 0)
         gather_words(2, 0, 0, 512, words_free[:])
         reorder_columns(w3_q[:], w3_raw[:], 8)
-        reorder_columns(w3_sc[:].bitcast(I32), w3_sc_raw[:].bitcast(I32), 2)
+        nc.vector.tensor_copy(
+            out=w3_sc[:].bitcast(I32).rearrange("p t (b i) -> p t b i", i=2),
+            in_=w3_sc_raw[:].bitcast(I32).rearrange("p (b t i) -> p t b i", t=SLOTS, i=2),
+        )
         d_passes(banks, 2, 0, 0, 512, start=True)
         words_a = keep.tile([P, 512], U32, name="words_a", tag="slot_a", align_bytes=64)
         gather_words(1, 0, 0, 512, words_a[:])
@@ -280,11 +290,12 @@ def tile_list_cloth_stretch_features_kernel(
         words_b = keep.tile([P, 3, 512], U32, name="words_b", tag="slot_b", align_bytes=64)
         for place, (m, a) in enumerate(((2, 1), (1, 1))):
             gather_words(m, a, 0, 512, words_b[:, place, :])
-            d_passes(banks, m, a, 0, 512)
+        d_passes(banks, 2, 1, 0, 512)
         cast_w1(0)
         gather_words(0, 0, 0, 512, words_b[:, 2, :])
         quantize_w1(0)
         d_passes(banks, 0, 0, 0, 512)
+        d_passes(banks, 1, 1, 0, 512)
         cast_w1(1)
         words_f = keep.tile([P, 512], U32, name="words_f", tag="w1_bf01", align_bytes=64)
         gather_words(0, 1, 0, 512, words_f[:])

@@ -77,17 +77,21 @@ def tile_list_cloth_stretch_features_kernel(
         def load_table(a):
             nc.sync.dma_start(out=table[a][:], in_=tab_words[a].rearrange("p t i -> p (t i)").bitcast(I32))
 
+        nc.sync.dma_start(out=w2_raw[:], in_=w2_words.rearrange("a p c -> p a c").bitcast(I32))
         nc.sync.dma_start(lists[1][:], offs2)
         for q in range(4):
             nc.sync.dma_start(
                 out=table_sc[32 * q : 32 * q + 8, :].bitcast(I32),
                 in_=tab_scales[:, 4 * q : 4 * q + 4, :].bitcast(I32),
             )
+        nc.vector.tensor_copy(
+            out=w2_q[:].bitcast(I32).rearrange("p t a (b i) -> p t (a b) i", i=4),
+            in_=w2_raw[:].rearrange("p a (b t i) -> p t (a b) i", t=SLOTS, i=4),
+        )
         nc.vector.tensor_copy(out=v2_sc[:], in_=table_sc[:].indirect(lists[1][:]))
         nc.sync.dma_start(lists[2][:], offs3)
         load_table(0)
         nc.sync.dma_start(out=w3_raw[:], in_=w3_words.rearrange("a p c i -> p a (c i)").bitcast(I32))
-        nc.sync.dma_start(out=w2_raw[:], in_=w2_words.rearrange("a p c -> p a c").bitcast(I32))
 
         def load_w3_scales():
             for q in range(4):
@@ -168,10 +172,10 @@ def tile_list_cloth_stretch_features_kernel(
             return words.rearrange("p (c i) t -> p c t i", i=4)
 
         def cast_w1(a):
-            for t in range(SLOTS):
+            for u in range(2):
                 nc.scalar.copy(
-                    out=w1_bf[a][t // 2][:, t % 2, :].rearrange("p (b i j) -> p b j i", i=8, j=4),
-                    in_=w1_raw[a][:].rearrange("p j (b t i) -> p t b j i", t=SLOTS, i=8)[:, t],
+                    out=w1_bf[a][u][:].rearrange("p t (b i j) -> p t b j i", i=8, j=4),
+                    in_=w1_raw[a][:].rearrange("p j (b t i) -> p t b j i", t=SLOTS, i=8)[:, 2 * u : 2 * u + 2],
                 )
 
         def quantize_w1(a):
@@ -257,12 +261,6 @@ def tile_list_cloth_stretch_features_kernel(
                 readout_pass(y[:, c, :], c, h_q, h_sc)
             return y
 
-        def finish_narrow_scalar(y, lo):
-            res = ring.tile([P, TILES_N, P], F32, name="res", tag="res", bufs=5)
-            for c in range(TILES_N):
-                nc.scalar.activation(out=res[:, c, :], in_=y[:, c, :], func=ACT.Identity, bias=b_col[:, c : c + 1])
-            nc.sync.dma_start(out=out_view[:, :, lo : lo + P], in_=res[:])
-
         def finish_narrow(y, lo):
             res = ring.tile([P, TILES_N, P], F32, name="res", tag="res", bufs=5)
             nc.vector.tensor_tensor(
@@ -284,7 +282,6 @@ def tile_list_cloth_stretch_features_kernel(
         words_a = keep.tile([P, 512], U32, name="words_a", tag="slot_a", align_bytes=64)
         gather_words(1, 0, 0, 512, words_a[:])
         gather_scales(0, 0, 512, sc_first[:, 1, :])
-        reorder_columns(w2_q[:].bitcast(I32), w2_raw[:], 4)
         reorder_columns(w2_sc[:].bitcast(I32), w2_sc_raw[:].bitcast(I32), 2)
         d_passes(banks, 1, 0, 0, 512)
         words_b = keep.tile([P, 3, 512], U32, name="words_b", tag="slot_b", align_bytes=64)
@@ -350,5 +347,5 @@ def tile_list_cloth_stretch_features_kernel(
         res_wide = keep.tile([P, 3, TILES_N, 256], F32, name="res_wide", tag="w4_raw")
         for u in range(3):
             finish_wide(y_wide[u], 256 * u, res_wide[:, u])
-        finish_narrow_scalar(y_last[0], 768)
+        finish_narrow(y_last[0], 768)
         finish_narrow(y_last[1], 768 + P)

@@ -44,8 +44,7 @@ def tile_list_cloth_stretch_features_kernel(
         w2_q = keep.tile([P, SLOTS, PASSES, 2 * P], U8, name="w2_q", align_bytes=64)
         w1_raw = [keep.tile([P, 4, H], F32, name=f"w1_raw{a}", tag=f"w1_raw{a}", align_bytes=64) for a in range(PASSES)]
         w1_bf = [
-            [keep.tile([P, 2, 4 * P], BF16, name=f"w1_bf{a}{u}", tag=f"w1_bf{a}{u}", align_bytes=64) for u in range(2)]
-            for a in range(PASSES)
+            keep.tile([P, SLOTS, 4 * P], BF16, name=f"w1_bf{a}", tag=f"w1_bf{a}1", align_bytes=64) for a in range(PASSES)
         ]
         w1_q = keep.tile([P, PASSES, H], U32, name="w1_q", align_bytes=64)
         w1_sc = keep.tile([P, PASSES, H], U8, name="w1_sc", align_bytes=64)
@@ -59,7 +58,7 @@ def tile_list_cloth_stretch_features_kernel(
         g_col = keep.tile([P, SLOTS, 8], F32, name="g_col")
         g_slots = keep.tile([P, SLOTS], F32, name="g_slots")
         b_col = keep.tile([P, TILES_N], F32, name="b_col")
-        ones = keep.tile([P, 1], F32, name="ones")
+        ones = keep.tile([P, 1], F32, name="ones", tag="ones")
         one = keep.tile([P, 1], F32, name="one")
         v_q = {}
         late = {}
@@ -172,20 +171,17 @@ def tile_list_cloth_stretch_features_kernel(
             return words.rearrange("p (c i) t -> p c t i", i=4)
 
         def cast_w1(a):
-            for u in range(2):
-                nc.scalar.copy(
-                    out=w1_bf[a][u][:].rearrange("p t (b i j) -> p t b j i", i=8, j=4),
-                    in_=w1_raw[a][:].rearrange("p j (b t i) -> p t b j i", t=SLOTS, i=8)[:, 2 * u : 2 * u + 2],
-                )
+            nc.scalar.copy(
+                out=w1_bf[a][:].rearrange("p t (b i j) -> p t b j i", i=8, j=4),
+                in_=w1_raw[a][:].rearrange("p j (b t i) -> p t b j i", t=SLOTS, i=8),
+            )
 
         def quantize_w1(a):
-            for u in range(2):
-                cols = slice(256 * u, 256 * (u + 1))
-                nc.vector.quantize_mx(
-                    out=w1_q[:, a, cols].bitcast(FP8X4),
-                    scales=w1_sc[:, a, cols],
-                    in_=w1_bf[a][u][:].rearrange("p t c -> p (t c)"),
-                )
+            nc.vector.quantize_mx(
+                out=w1_q[:, a, :].bitcast(FP8X4),
+                scales=w1_sc[:, a, :],
+                in_=w1_bf[a][:].rearrange("p t c -> p (t c)"),
+            )
 
         def reorder_columns(dst, src, run):
             nc.vector.tensor_copy(
@@ -202,9 +198,9 @@ def tile_list_cloth_stretch_features_kernel(
                 nc.scalar.activation(out=sq[:, t, :], in_=banks[t][:, lo:hi], func=ACT.Square)
             return sq
 
-        def magnitude(sq, lo, hi):
+        def magnitude(sq, lo, hi, unit=one):
             mag = ring.tile([P, SLOTS, hi - lo], F32, name="mag", tag="mag", bufs=5)
-            nc.scalar.activation(out=mag[:], in_=sq[:, :, lo:hi], func=ACT.Sqrt, bias=one[:])
+            nc.scalar.activation(out=mag[:], in_=sq[:, :, lo:hi], func=ACT.Sqrt, bias=unit[:])
             return mag[:]
 
         def new_h_bf(width, tag):
@@ -328,7 +324,6 @@ def tile_list_cloth_stretch_features_kernel(
         banks = new_banks(256, 0)
         stretch(banks, 768, S, range(6), [words_c[:, 6 + step, :] for step in range(6)])
         sq_last = square(banks, 0, 256, "w4_raw")
-        mag_last = [magnitude(sq_last, lo, lo + P) for lo in (0, P)]
         late["w4_q"] = keep.tile([P, N], U32, name="w4_q", tag="table0", align_bytes=64)
         for u, (lo, hi) in enumerate(w4_cols):
             nc.vector.quantize_mx(
@@ -336,16 +331,33 @@ def tile_list_cloth_stretch_features_kernel(
                 scales=w4_sc[:, lo:hi],
                 in_=w4_bf[u][:].rearrange("p n t -> p (n t)"),
             )
-        h_one = stiffen(mag_first[1], new_h_bf(256, "table1"))
         y_wide = [readout_wide(*quantize_h(h_zero, new_h_q(256, "w4_bf0")), 4)]
+        mag_last = [magnitude(sq_last, 0, P, ones)]
+        res_zero = keep.tile([P, TILES_N, 256], F32, name="res_zero", tag="ones")
+        finish_wide(y_wide[0], 0, res_zero[:])
+        mag_last.append(magnitude(sq_last, P, 2 * P))
+        h_one = stiffen(mag_first[1], new_h_bf(256, "table1"))
         h_two = stiffen(mag_third, new_h_bf(256, "w4_bf1"))
         y_wide.append(readout_wide(*quantize_h(h_one, new_h_q(256, "h_q1")), 6))
         h_last = [stiffen(mag_last[0], new_h_bf(P, "h_bf30"))]
         y_wide.append(readout_wide(*quantize_h(h_two, new_h_q(256, "h_q2")), 0))
         h_last.append(stiffen(mag_last[1], new_h_bf(P, "h_bf31")))
-        y_last = [readout_narrow(*quantize_h(h_last[u], new_h_q(P, f"h_q3{u}")), 2 + u) for u in range(2)]
-        res_wide = keep.tile([P, 3, TILES_N, 256], F32, name="res_wide", tag="w4_raw")
-        for u in range(3):
-            finish_wide(y_wide[u], 256 * u, res_wide[:, u])
-        finish_narrow(y_last[0], 768)
-        finish_narrow(y_last[1], 768 + P)
+        y_next = readout_narrow(*quantize_h(h_last[0], new_h_q(P, "h_q30")), 2)
+        h_q, h_sc = quantize_h(h_last[1], new_h_q(P, "h_q31"))
+        y_end = psum.tile([P, 2, P], F32, name="y_end", tag="bank3")
+        for c in range(2):
+            readout_pass(y_end[:, c, :], c, h_q, h_sc)
+        res_wide = keep.tile([P, 2, TILES_N, 256], F32, name="res_wide", tag="w4_raw")
+        for u in range(1, 3):
+            finish_wide(y_wide[u], 256 * u, res_wide[:, u - 1])
+        y_rest = psum.tile([P, P], F32, name="y_rest", tag="bank5")
+        readout_pass(y_rest[:], 2, h_q, h_sc)
+        finish_narrow(y_next, 768)
+        res_end = keep.tile([P, 2, P], F32, name="res_end")
+        nc.vector.tensor_tensor(
+            out=res_end[:], in0=y_end[:], in1=b_col[:, 0:2].unsqueeze(2).to_broadcast([P, 2, P]), op=ALU.add
+        )
+        nc.sync.dma_start(out=out_view[:, 0:2, 768 + P : S], in_=res_end[:])
+        res_rest = keep.tile([P, P], F32, name="res_rest")
+        nc.scalar.activation(out=res_rest[:], in_=y_rest[:], func=ACT.Identity, bias=b_col[:, 2:3])
+        nc.sync.dma_start(out=out_view[:, 2, 768 + P : S], in_=res_rest[:])

@@ -138,17 +138,15 @@ def tile_list_cloth_stretch_features_kernel(
             for t in range(SLOTS):
                 if m == 1:
                     rhs_sc = v2_sc if a == 0 else v2_sc_pass1
-                    step = 512 if hi - lo == 512 else 128
-                    for c0 in range(0, hi - lo, step):
-                        nc.tensor.matmul_mx(
-                            out=banks[t][:, c0 : c0 + step],
-                            lhsT=w2_q[:, t, a, :].bitcast(FP4X4),
-                            lhsT_scale=w2_sc[:, t, a, :],
-                            rhs=words[:, c0 : c0 + step].bitcast(FP8X4),
-                            rhs_scale=rhs_sc[:, lo + c0 : lo + c0 + step],
-                            start=False,
-                            stop=False,
-                        )
+                    nc.tensor.matmul_mx(
+                        out=banks[t][:],
+                        lhsT=w2_q[:, t, a, :].bitcast(FP4X4),
+                        lhsT_scale=w2_sc[:, t, a, :],
+                        rhs=words.bitcast(FP8X4),
+                        rhs_scale=rhs_sc[:, lo:hi],
+                        start=False,
+                        stop=False,
+                    )
                     continue
                 if m == 0:
                     lhs, lhs_sc = w1_q[:, a, P * t : P * (t + 1)], w1_sc[:, a, P * t : P * (t + 1)]
@@ -184,9 +182,9 @@ def tile_list_cloth_stretch_features_kernel(
             )
 
         def reorder_columns(dst, src, run):
-            nc.vector.tensor_copy(
-                out=dst.rearrange("p t a (b i) -> p t (a b) i", i=run),
-                in_=src.rearrange("p a (b t i) -> p t (a b) i", t=SLOTS, i=run),
+            nc.scalar.copy(
+                out=dst.bitcast(U32).rearrange("p t a (b i) -> p t (a b) i", i=run),
+                in_=src.bitcast(U32).rearrange("p a (b t i) -> p t (a b) i", t=SLOTS, i=run),
             )
 
         def new_banks(width, first):
@@ -270,15 +268,15 @@ def tile_list_cloth_stretch_features_kernel(
         banks = new_banks(512, 0)
         gather_words(2, 0, 0, 512, words_free[:])
         reorder_columns(w3_q[:], w3_raw[:], 8)
-        nc.vector.tensor_copy(
-            out=w3_sc[:].bitcast(I32).rearrange("p t (b i) -> p t b i", i=2),
-            in_=w3_sc_raw[:].bitcast(I32).rearrange("p (b t i) -> p t b i", t=SLOTS, i=2),
+        nc.scalar.copy(
+            out=w3_sc[:].bitcast(U32).rearrange("p t (b i) -> p t b i", i=2),
+            in_=w3_sc_raw[:].bitcast(U32).rearrange("p (b t i) -> p t b i", t=SLOTS, i=2),
         )
         d_passes(banks, 2, 0, 0, 512, start=True)
         words_a = keep.tile([P, 512], U32, name="words_a", tag="slot_a", align_bytes=64)
         gather_words(1, 0, 0, 512, words_a[:])
         gather_scales(0, 0, 512, sc_first[:, 1, :])
-        reorder_columns(w2_sc[:].bitcast(I32), w2_sc_raw[:].bitcast(I32), 2)
+        reorder_columns(w2_sc[:], w2_sc_raw[:], 2)
         d_passes(banks, 1, 0, 0, 512)
         words_b = keep.tile([P, 3, 512], U32, name="words_b", tag="slot_b", align_bytes=64)
         for place, (m, a) in enumerate(((2, 1), (1, 1))):

@@ -20,6 +20,7 @@ P = 128
 PASSES = 2
 SLOTS = 4
 TILES_N = 3
+SHARE = 192
 
 
 def tile_list_cloth_stretch_features_kernel(
@@ -113,11 +114,11 @@ def tile_list_cloth_stretch_features_kernel(
         load_table(1)
         nc.sync.dma_start(lists[0][:], offs)
         load_w2_scales()
+        nc.sync.dma_start(out=v2_sc_pass1[0:112, :].bitcast(I32), in_=v2_sc[4:116, :].bitcast(I32))
         load_w1(0)
         load_w1(1)
         for t in range(SLOTS):
             nc.sync.dma_start(out=w4_raw[:, t, :], in_=w4.rearrange("(b t i) n -> t b i n", t=SLOTS, i=8)[t])
-        nc.sync.dma_start(out=v2_sc_pass1[0:112, :].bitcast(I32), in_=v2_sc[4:116, :].bitcast(I32))
         with nc.allow_non_contiguous_dma(reason="one value a partition"):
             for t in range(SLOTS):
                 nc.sync.dma_start(
@@ -262,9 +263,11 @@ def tile_list_cloth_stretch_features_kernel(
             )
             nc.sync.dma_start(out=out_view[:, :, lo : lo + P], in_=res[:])
 
-        sc_first = keep.tile([P, 2, 512], U8, name="sc_first", align_bytes=64)
+        v3_sc = keep.tile([P, S], U8, name="v3_sc", align_bytes=64)
+        sc_first = keep.tile([P, 512], U8, name="sc_first", align_bytes=64)
         words_free = keep.tile([P, 512], U32, name="words_free", align_bytes=64)
-        gather_scales(2, 0, 512, sc_first[:, 0, :])
+        gather_scales(2, 0, S, v3_sc[:])
+        v_sc[2, 0], v_sc[2, 1] = v3_sc[:, 0:512], v3_sc[:, 512:S]
         banks = new_banks(512, 0)
         gather_words(2, 0, 0, 512, words_free[:])
         reorder_columns(w3_q[:], w3_raw[:], 8)
@@ -275,18 +278,18 @@ def tile_list_cloth_stretch_features_kernel(
         d_passes(banks, 2, 0, 0, 512, start=True)
         words_a = keep.tile([P, 512], U32, name="words_a", tag="slot_a", align_bytes=64)
         gather_words(1, 0, 0, 512, words_a[:])
-        gather_scales(0, 0, 512, sc_first[:, 1, :])
+        gather_scales(0, 0, 512, sc_first[:])
         reorder_columns(w2_sc[:], w2_sc_raw[:], 2)
         d_passes(banks, 1, 0, 0, 512)
         words_b = keep.tile([P, 3, 512], U32, name="words_b", tag="slot_b", align_bytes=64)
         for place, (m, a) in enumerate(((2, 1), (1, 1))):
             gather_words(m, a, 0, 512, words_b[:, place, :])
         d_passes(banks, 2, 1, 0, 512)
+        d_passes(banks, 1, 1, 0, 512)
         cast_w1(0)
         gather_words(0, 0, 0, 512, words_b[:, 2, :])
         quantize_w1(0)
         d_passes(banks, 0, 0, 0, 512)
-        d_passes(banks, 1, 1, 0, 512)
         cast_w1(1)
         words_f = keep.tile([P, 512], U32, name="words_f", tag="w1_bf01", align_bytes=64)
         gather_words(0, 1, 0, 512, words_f[:])
@@ -306,22 +309,24 @@ def tile_list_cloth_stretch_features_kernel(
                 gather_words(m, a, lo, hi, place)
                 d_passes(chunk_banks, m, a, lo, hi, start=(step == 0), stop=(step == len(order) - 1))
 
-        sc_second = keep.tile([P, 2, 512], U8, name="sc_second", tag="w1_bf11", align_bytes=64)
-        gather_scales(2, 512, S, sc_second[:, 0, :])
-        scaled = keep.tile([P, SLOTS, 256], F32, name="scaled")
+        sc_second = keep.tile([P, 512], U8, name="sc_second", tag="w1_bf11", align_bytes=64)
+        scaled = keep.tile([P, SLOTS, SHARE], F32, name="scaled")
         for t in range(SLOTS):
-            nc.scalar.activation(out=scaled[:, t, :], in_=mag_first[0][:, t, :], func=ACT.Copy, scale=g_slots[:, t : t + 1])
+            nc.scalar.activation(
+                out=scaled[:, t, :], in_=mag_first[0][:, t, 0:SHARE], func=ACT.Copy, scale=g_slots[:, t : t + 1]
+            )
         h_zero = new_h_bf(256, "h_bf")
-        nc.scalar.copy(out=by_fours_out(h_zero), in_=by_fours_in(scaled[:]))
+        nc.scalar.copy(out=by_fours_out(h_zero[:, 0:SHARE, :]), in_=by_fours_in(scaled[:]))
         words_c = keep.tile([P, 12, 256], U32, name="words_c", tag="w1_raw1", align_bytes=64)
         banks = new_banks(256, 4)
         stretch(banks, 512, 768, range(4), [words_c[:, step, :] for step in range(4)])
-        gather_scales(0, 512, S, sc_second[:, 1, :])
+        gather_scales(0, 512, S, sc_second[:])
         stretch(banks, 512, 768, range(4, 6), [words_c[:, step, :] for step in range(4, 6)])
         mag_third = magnitude(square(banks, 0, 256, "w4_raw"), 0, 256)
         banks = new_banks(256, 0)
         stretch(banks, 768, S, range(6), [words_c[:, 6 + step, :] for step in range(6)])
         sq_last = square(banks, 0, 256, "w4_raw")
+        stiffen(mag_first[0][:, :, SHARE:256], h_zero[:, SHARE:256, :])
         late["w4_q"] = keep.tile([P, N], U32, name="w4_q", tag="table0", align_bytes=64)
         for u, (lo, hi) in enumerate(w4_cols):
             nc.vector.quantize_mx(

@@ -20,7 +20,7 @@ P = 128
 PASSES = 2
 SLOTS = 4
 TILES_N = 3
-SHARE = 192
+SHARE = 128
 
 
 def tile_list_cloth_stretch_features_kernel(
@@ -299,7 +299,10 @@ def tile_list_cloth_stretch_features_kernel(
             nc.scalar.copy(out=by_fours_out(w4_bf[u][:]), in_=by_fours_in(w4_raw[:, :, lo:hi]))
         nc.scalar.copy(out=g_slots[:], in_=g_col[:, :, 0])
         sq_first = square(banks, 0, 512, "w4_raw")
-        mag_first = [magnitude(sq_first, 256 * u, 256 * u + 256) for u in range(2)]
+        mag_half = keep.tile([P, SLOTS, 512], F32, name="mag_half")
+        for t in range(0, SLOTS, 2):
+            nc.scalar.activation(out=mag_half[:, t : t + 2, :], in_=sq_first[:, t : t + 2, :], func=ACT.Sqrt, bias=one[:])
+        mag_first = [mag_half[:, :, 256 * u : 256 * u + 256] for u in range(2)]
 
         order = ((2, 0), (1, 0), (2, 1), (1, 1), (0, 0), (0, 1))
 
@@ -316,13 +319,14 @@ def tile_list_cloth_stretch_features_kernel(
                 out=scaled[:, t, :], in_=mag_first[0][:, t, 0:SHARE], func=ACT.Copy, scale=g_slots[:, t : t + 1]
             )
         h_zero = new_h_bf(256, "h_bf")
-        nc.scalar.copy(out=by_fours_out(h_zero[:, 0:SHARE, :]), in_=by_fours_in(scaled[:]))
         words_c = keep.tile([P, 12, 256], U32, name="words_c", tag="w1_raw1", align_bytes=64)
         banks = new_banks(256, 4)
         stretch(banks, 512, 768, range(4), [words_c[:, step, :] for step in range(4)])
         gather_scales(0, 512, S, sc_second[:])
         stretch(banks, 512, 768, range(4, 6), [words_c[:, step, :] for step in range(4, 6)])
-        mag_third = magnitude(square(banks, 0, 256, "w4_raw"), 0, 256)
+        sq_third = square(banks, 0, 256, "w4_raw")
+        nc.scalar.copy(out=by_fours_out(h_zero[:, 0:SHARE, :]), in_=by_fours_in(scaled[:]))
+        mag_third = magnitude(sq_third, 0, 256)
         banks = new_banks(256, 0)
         stretch(banks, 768, S, range(6), [words_c[:, 6 + step, :] for step in range(6)])
         sq_last = square(banks, 0, 256, "w4_raw")

@@ -20,7 +20,9 @@ P = 128
 PASSES = 2
 SLOTS = 4
 TILES_N = 3
+Q = 256
 SHARE = 128
+LATE = 20480
 
 
 def tile_list_cloth_stretch_features_kernel(
@@ -29,53 +31,56 @@ def tile_list_cloth_stretch_features_kernel(
     nc = tc.nc
     with ExitStack() as ctx:
         keep = ctx.enter_context(tc.tile_pool(name="keep", bufs=1))
-        ring = ctx.enter_context(tc.tile_pool(name="ring", bufs=2))
+        shared = ctx.enter_context(tc.tile_pool(name="shared", bufs=1))
         psum = ctx.enter_context(tc.psum_pool(name="psum", bufs=1))
 
+        def sbuf(shape, dtype, name, tag=None):
+            return keep.tile(shape, dtype, name=name, tag=tag or name, align_bytes=64)
+
+        def placed(shape, dtype, name, offset):
+            return shared.tile(shape, dtype, name=name, align_bytes=64, offset=offset)
+
         lists = [keep.tile([P, S // 16], U16, name=f"list{m}") for m in range(3)]
-        table = [keep.tile([P, T], I32, name=f"table{a}", tag=f"table{a}", align_bytes=64) for a in range(PASSES)]
-        table_sc = keep.tile([P, T], U8, name="table_sc", align_bytes=64)
-        w3_sc_raw = keep.tile([P, H], U8, name="w3_sc_raw", tag="slot_a", align_bytes=64)
-        w2_sc_raw = keep.tile([P, PASSES, H], U8, name="w2_sc_raw", tag="slot_b", align_bytes=64)
-        w3_sc = keep.tile([P, SLOTS, P], U8, name="w3_sc", align_bytes=64)
-        w2_sc = keep.tile([P, SLOTS, PASSES, P], U8, name="w2_sc", align_bytes=64)
-        w3_raw = keep.tile([P, PASSES, H], I32, name="w3_raw", align_bytes=64)
-        w3_q = keep.tile([P, SLOTS, PASSES, P], I32, name="w3_q", align_bytes=64)
-        w2_raw = keep.tile([P, PASSES, H // 2], I32, name="w2_raw", align_bytes=64)
-        w2_q = keep.tile([P, SLOTS, PASSES, 2 * P], U8, name="w2_q", align_bytes=64)
-        w1_raw = [keep.tile([P, 4, H], F32, name=f"w1_raw{a}", tag=f"w1_raw{a}", align_bytes=64) for a in range(PASSES)]
-        w1_bf = [
-            keep.tile([P, SLOTS, 4 * P], BF16, name=f"w1_bf{a}", tag=f"w1_bf{a}1", align_bytes=64) for a in range(PASSES)
-        ]
-        w1_q = keep.tile([P, PASSES, H], U32, name="w1_q", align_bytes=64)
-        w1_sc = keep.tile([P, PASSES, H], U8, name="w1_sc", align_bytes=64)
-        w4_raw = keep.tile([P, SLOTS, N], F32, name="w4_raw", tag="w4_raw")
-        w4_cols = ((0, 256), (256, N))
-        w4_bf = [
-            keep.tile([P, hi - lo, SLOTS], BF16, name=f"w4_bf{u}", tag=f"w4_bf{u}", align_bytes=64)
-            for u, (lo, hi) in enumerate(w4_cols)
-        ]
-        w4_sc = keep.tile([P, N], U8, name="w4_sc", align_bytes=64)
-        g_col = keep.tile([P, SLOTS, 8], F32, name="g_col")
-        g_slots = keep.tile([P, SLOTS], F32, name="g_slots")
-        b_col = keep.tile([P, TILES_N], F32, name="b_col")
-        ones = keep.tile([P, 1], F32, name="ones", tag="ones")
-        one = keep.tile([P, 1], F32, name="one")
-        v_q = {}
-        late = {}
-        v_sc = {}
-        v2_sc = keep.tile([P, S], U8, name="v2_sc", align_bytes=64)
-        v2_sc_pass1 = keep.tile([P, S], U8, name="v2_sc_pass1", align_bytes=64)
+        table = [sbuf([P, T], I32, f"table{a}") for a in range(PASSES)]
+        table_sc = sbuf([P, T], U8, "table_sc")
+        w3_sc_raw = sbuf([P, H], U8, "w3_sc_raw")
+        w2_sc_raw = sbuf([P, PASSES, H], U8, "w2_sc_raw")
+        w3_raw = sbuf([P, PASSES, H], I32, "w3_raw")
+        w2_raw = sbuf([P, PASSES, H // 2], I32, "w2_raw")
+        w2_q = sbuf([P, SLOTS, PASSES, 2 * P], U8, "w2_q")
+        w1_raw = [placed([P, 4, H], F32, "w1_raw0", 10240), placed([P, 4, H], F32, "w1_raw1", 0)]
+        w1_bf = [sbuf([P, SLOTS, 4 * P], BF16, f"w1_bf{a}") for a in range(PASSES)]
+        w1_q = [sbuf([P, H], U32, f"w1_q{a}") for a in range(PASSES)]
+        w1_sc = [sbuf([P, H], U8, f"w1_sc{a}") for a in range(PASSES)]
+        w4_raw = placed([P, SLOTS, N], F32, "w4_raw", LATE + 2048)
+        w4_bf = sbuf([P, N, SLOTS], BF16, "w4_bf")
+        w4_sc = sbuf([P, N], U8, "w4_sc")
+        g_slots = sbuf([P, SLOTS], F32, "g_slots")
+        b_col = sbuf([P, TILES_N], F32, "b_col")
+        unit = [sbuf([P, 1], F32, f"unit{u}") for u in range(2)]
+        one = sbuf([P, 1], F32, "one")
+        v_sc = [sbuf([P, S], U8, f"v_sc{m}") for m in range(2)]
+        planes = {}
+        v2_sc_pass1 = sbuf([P, S], U8, "v2_sc_pass1")
 
         nc.gpsimd.memset(table_sc[:].bitcast(I32), 0)
-        nc.gpsimd.memset(ones[:], 1.0)
-        nc.gpsimd.memset(w3_sc_raw[:].bitcast(I32), 0)
+        nc.gpsimd.memset(unit[0][:], 1.0)
         nc.gpsimd.memset(w2_sc_raw[:].rearrange("p a c -> p (a c)").bitcast(I32), 0)
+        nc.gpsimd.memset(w3_sc_raw[:].bitcast(I32), 0)
         nc.gpsimd.memset(v2_sc_pass1[:].bitcast(I32), 0)
-        nc.scalar.activation(out=one[:], in_=ones[:], func=ACT.Sqrt)
+        nc.gpsimd.memset(unit[1][:], 1.0)
+        nc.scalar.activation(out=one[:], in_=unit[0][:], func=ACT.Sqrt)
 
         def load_table(a):
             nc.sync.dma_start(out=table[a][:], in_=tab_words[a].rearrange("p t i -> p (t i)").bitcast(I32))
+
+        def load_w1(a):
+            nc.sync.dma_start(out=w1_raw[a][:], in_=w1[512 * a : 512 * (a + 1), :].rearrange("(p j) r -> p j r", j=4))
+
+        def gather_scales(m, dst, lo=0, hi=S):
+            for c in range(lo // Q, hi // Q):
+                planes[m, c] = (dst, slice(Q * c - lo, Q * (c + 1) - lo))
+            nc.vector.tensor_copy(out=dst[:], in_=table_sc[:].indirect(lists[m][:, lo // 16 : hi // 16]))
 
         nc.sync.dma_start(out=w2_raw[:], in_=w2_words.rearrange("a p c -> p a c").bitcast(I32))
         nc.sync.dma_start(lists[1][:], offs2)
@@ -85,128 +90,109 @@ def tile_list_cloth_stretch_features_kernel(
                 in_=tab_scales[:, 4 * q : 4 * q + 4, :].bitcast(I32),
             )
         nc.vector.tensor_copy(
-            out=w2_q[:].bitcast(I32).rearrange("p t a (b i) -> p t (a b) i", i=4),
-            in_=w2_raw[:].rearrange("p a (b t i) -> p t (a b) i", t=SLOTS, i=4),
+            out=w2_q[:].bitcast(I32).rearrange("p t a c -> p (a c) t"),
+            in_=w2_raw[:].rearrange("p a (c t) -> p (a c) t", t=SLOTS),
         )
-        nc.vector.tensor_copy(out=v2_sc[:], in_=table_sc[:].indirect(lists[1][:]))
-        nc.sync.dma_start(lists[2][:], offs3)
-        load_table(0)
-        nc.sync.dma_start(out=w3_raw[:], in_=w3_words.rearrange("a p c i -> p a (c i)").bitcast(I32))
-
-        def load_w3_scales():
-            for q in range(4):
-                nc.sync.dma_start(
-                    out=w3_sc_raw[32 * q : 32 * q + 8, :].bitcast(I32),
-                    in_=w3_scales[:, 4 * q : 4 * q + 4, :].bitcast(I32),
-                )
-
-        def load_w2_scales():
-            for r in range(4):
-                nc.sync.dma_start(
-                    out=w2_sc_raw[r:P:32, :, :].bitcast(I32),
-                    in_=w2_scales.rearrange("a (q r) c -> r q a c", r=4)[r].bitcast(I32),
-                )
-
-        def load_w1(a):
-            nc.sync.dma_start(out=w1_raw[a][:], in_=w1[512 * a : 512 * (a + 1), :].rearrange("(p j) r -> p j r", j=4))
-
-        load_w3_scales()
-        load_table(1)
+        gather_scales(1, v_sc[1])
         nc.sync.dma_start(lists[0][:], offs)
-        load_w2_scales()
-        nc.sync.dma_start(out=v2_sc_pass1[0:112, :].bitcast(I32), in_=v2_sc[4:116, :].bitcast(I32))
         load_w1(0)
+        load_table(0)
+        for r in range(4):
+            nc.sync.dma_start(
+                out=w2_sc_raw[r:P:32, :, :].bitcast(I32),
+                in_=w2_scales.rearrange("a (q r) c -> r q a c", r=4)[r].bitcast(I32),
+            )
+        nc.sync.dma_start(lists[2][:], offs3)
         load_w1(1)
-        for t in range(SLOTS):
-            nc.sync.dma_start(out=w4_raw[:, t, :], in_=w4.rearrange("(b t i) n -> t b i n", t=SLOTS, i=8)[t])
+        nc.sync.dma_start(out=v2_sc_pass1[0:100, :].bitcast(I32), in_=v_sc[1][4:104, :].bitcast(I32))
+        for q in range(4):
+            nc.sync.dma_start(
+                out=w3_sc_raw[32 * q : 32 * q + 8, :].bitcast(I32),
+                in_=w3_scales[:, 4 * q : 4 * q + 4, :].bitcast(I32),
+            )
+        nc.sync.dma_start(out=w3_raw[:], in_=w3_words.rearrange("a p c i -> p a (c i)").bitcast(I32))
+        load_table(1)
+        for i in range(2):
+            nc.sync.dma_start(out=w4_raw[i:P:2, :, :], in_=w4.rearrange("(c t i) n -> i c t n", t=SLOTS, i=2)[i])
         with nc.allow_non_contiguous_dma(reason="one value a partition"):
-            for t in range(SLOTS):
-                nc.sync.dma_start(
-                    out=g_col[:, t, 0:1], in_=g.rearrange("(b t i e) -> t b i e", t=SLOTS, i=8, e=1)[t]
-                )
+            for i in range(2):
+                nc.sync.dma_start(out=g_slots[i:P:2, :], in_=g.rearrange("(c t i) -> i c t", t=SLOTS, i=2)[i])
             nc.sync.dma_start(out=b_col[:], in_=b.rearrange("(c p) -> p c", p=P))
 
-        def gather_scales(m, lo, hi, dst):
-            v_sc[m, lo // 512] = dst
-            nc.vector.tensor_copy(out=dst, in_=table_sc[:].indirect(lists[m][:, lo // 16 : hi // 16]))
+        words = {}
+        late_tiles = {}
 
         def gather_words(m, a, lo, hi, dst):
-            v_q[m, a, lo] = dst
+            for c in range(lo // Q, hi // Q):
+                words[m, a, c] = dst[:, Q * c - lo : Q * (c + 1) - lo]
             nc.vector.tensor_copy(out=dst, in_=table[a][:].bitcast(U32).indirect(lists[m][:, lo // 16 : hi // 16]))
 
-        def d_passes(banks, m, a, lo, hi, start=False, stop=False):
-            words = v_q[m, a, lo]
+        banks = {}
+
+        def open_banks(c):
+            banks[c] = [psum.tile([P, Q], F32, name=f"d{c}{t}", tag=f"bank{4 * (c % 2) + t}") for t in range(SLOTS)]
+
+        def d_passes(m, a, c, first=False, last=False):
+            plane, cols = planes[m, c]
+            if first:
+                open_banks(c)
             for t in range(SLOTS):
-                if m == 1:
-                    rhs_sc = v2_sc if a == 0 else v2_sc_pass1
-                    nc.tensor.matmul_mx(
-                        out=banks[t][:],
-                        lhsT=w2_q[:, t, a, :].bitcast(FP4X4),
-                        lhsT_scale=w2_sc[:, t, a, :],
-                        rhs=words.bitcast(FP8X4),
-                        rhs_scale=rhs_sc[:, lo:hi],
-                        start=False,
-                        stop=False,
-                    )
-                    continue
                 if m == 0:
-                    lhs, lhs_sc = w1_q[:, a, P * t : P * (t + 1)], w1_sc[:, a, P * t : P * (t + 1)]
+                    lhs, lhs_sc = w1_q[a][:, P * t : P * (t + 1)].bitcast(FP8X4), w1_sc[a][:, P * t : P * (t + 1)]
+                    rhs_sc = plane[4 * a : P, cols]
+                elif m == 1:
+                    lhs, lhs_sc = w2_q[:, t, a, :].bitcast(FP4X4), w2_sc[:, t, a, :]
+                    rhs_sc = (plane, v2_sc_pass1)[a][:, cols]
                 else:
-                    lhs, lhs_sc = w3_q[:, t, a, :], w3_sc[4 * a : P, t, :]
+                    lhs, lhs_sc = w3_q[:, t, a, :].bitcast(FP8X4), w3_sc[4 * a : P, t, :]
+                    rhs_sc = plane[4 * a : P, cols]
                 nc.tensor.matmul_mx(
-                    out=banks[t][:],
-                    lhsT=lhs.bitcast(FP8X4),
+                    out=banks[c][t][:],
+                    lhsT=lhs,
                     lhsT_scale=lhs_sc,
-                    rhs=words.bitcast(FP8X4),
-                    rhs_scale=v_sc[m, lo // 512][4 * a : P, lo % 512 : lo % 512 + hi - lo],
-                    start=start,
-                    stop=stop,
+                    rhs=words[m, a, c].bitcast(FP8X4),
+                    rhs_scale=rhs_sc,
+                    start=first,
+                    stop=last,
                 )
 
         def by_fours_in(planes):
             return planes.rearrange("p t (c i) -> p c t i", i=4)
 
-        def by_fours_out(words):
-            return words.rearrange("p (c i) t -> p c t i", i=4)
+        def by_fours_out(woven):
+            return woven.rearrange("p (c i) t -> p c t i", i=4)
 
         def cast_w1(a):
             nc.scalar.copy(
-                out=w1_bf[a][:].rearrange("p t (b i j) -> p t b j i", i=8, j=4),
-                in_=w1_raw[a][:].rearrange("p j (b t i) -> p t b j i", t=SLOTS, i=8),
+                out=w1_bf[a][:].rearrange("p t (c i j) -> p t c j i", i=2, j=4),
+                in_=w1_raw[a][:].rearrange("p j (c t i) -> p t c j i", t=SLOTS, i=2),
             )
 
         def quantize_w1(a):
             nc.vector.quantize_mx(
-                out=w1_q[:, a, :].bitcast(FP8X4),
-                scales=w1_sc[:, a, :],
-                in_=w1_bf[a][:].rearrange("p t c -> p (t c)"),
+                out=w1_q[a][:].bitcast(FP8X4), scales=w1_sc[a][:], in_=w1_bf[a][:].rearrange("p t c -> p (t c)")
             )
 
-        def reorder_columns(dst, src, run):
+        def reorder_columns(dst, src, dtype, run):
             nc.scalar.copy(
-                out=dst.bitcast(U32).rearrange("p t a (b i) -> p t (a b) i", i=run),
-                in_=src.bitcast(U32).rearrange("p a (b t i) -> p t (a b) i", t=SLOTS, i=run),
+                out=dst.bitcast(dtype).rearrange("p t a (c i) -> p (a c) t i", i=run),
+                in_=src.bitcast(dtype).rearrange("p a (c t i) -> p (a c) t i", t=SLOTS, i=run),
             )
 
-        def new_banks(width, first):
-            return [psum.tile([P, width], F32, name="d_bank", tag=f"bank{first + t}") for t in range(SLOTS)]
-
-        def square(banks, lo, hi, tag):
-            sq = keep.tile([P, SLOTS, hi - lo], F32, name="sq", tag=tag)
+        def square(c):
+            sq = placed([P, SLOTS, Q], F32, f"sq{c}", LATE + (4096, 6144, 512, 10240)[c])
             for t in range(SLOTS):
-                nc.scalar.activation(out=sq[:, t, :], in_=banks[t][:, lo:hi], func=ACT.Square)
+                nc.scalar.activation(out=sq[:, t, :], in_=banks[c][t][:], func=ACT.Square)
             return sq
 
-        def magnitude(sq, lo, hi, unit=one):
-            mag = ring.tile([P, SLOTS, hi - lo], F32, name="mag", tag="mag", bufs=5)
-            nc.scalar.activation(out=mag[:], in_=sq[:, :, lo:hi], func=ACT.Sqrt, bias=unit[:])
-            return mag[:]
-
-        def new_h_bf(width, tag):
-            return keep.tile([P, width, SLOTS], BF16, name=tag, tag=tag, align_bytes=64)[:]
-
-        def new_h_q(width, tag):
-            return keep.tile([P, width], U32, name=tag, tag=tag, align_bytes=64)[:]
+        def magnitude(c):
+            sq = square(c)
+            mag = sbuf([P, SLOTS, Q], F32, f"mag{c}")
+            for u in range(2):
+                nc.scalar.activation(
+                    out=mag[:, 2 * u : 2 * u + 2, :], in_=sq[:, 2 * u : 2 * u + 2, :], func=ACT.Sqrt, bias=one[:]
+                )
+            return mag
 
         def stiffen(mag, h_bf):
             width = h_bf.shape[1]
@@ -216,155 +202,137 @@ def tile_list_cloth_stretch_features_kernel(
                 in1=g_slots[:].unsqueeze(1).unsqueeze(3).to_broadcast([P, width // 4, SLOTS, 4]),
                 op=ALU.mult,
             )
-            return h_bf
 
-        def quantize_h(h_bf, h_q):
-            h_sc = ring.tile([P, h_bf.shape[1]], U8, name="h_sc", tag="h_sc", align_bytes=64, bufs=5)
-            nc.vector.quantize_mx(out=h_q.bitcast(FP8X4), scales=h_sc[:], in_=h_bf.rearrange("p n t -> p (n t)"))
+        def quantize_h(h_bf, name, h_q):
+            width = h_bf.shape[1]
+            h_sc = sbuf([P, width], U8, name + "_sc")
+            nc.vector.quantize_mx(out=h_q[:].bitcast(FP8X4), scales=h_sc[:], in_=h_bf.rearrange("p n t -> p (n t)"))
             return h_q, h_sc
 
-        def readout_pass(dst, c, h_q, h_sc):
-            w4_q = late["w4_q"]
+        def readout_pass(dst, f, h_q, h_sc):
+            w4_q = late_tiles["w4_q"]
             nc.tensor.matmul_mx(
                 out=dst,
-                lhsT=w4_q[:, P * c : P * (c + 1)].bitcast(FP8X4),
-                lhsT_scale=w4_sc[:, P * c : P * (c + 1)],
-                rhs=h_q.bitcast(FP8X4),
+                lhsT=w4_q[:, P * f : P * (f + 1)].bitcast(FP8X4),
+                lhsT_scale=w4_sc[:, P * f : P * (f + 1)],
+                rhs=h_q[:].bitcast(FP8X4),
                 rhs_scale=h_sc[:],
                 start=True,
                 stop=True,
             )
 
-        out_view = out.rearrange("(c p) j -> p c j", p=P)
+        out_view = out.rearrange("(f p) j -> p f j", p=P)
 
-        def readout_wide(h_q, h_sc, first):
-            y_a = psum.tile([P, 2, 256], F32, name="y_a", tag=f"bank{first}")
-            y_b = psum.tile([P, 256], F32, name="y_b", tag=f"bank{first + 1}")
+        def readout_wide(c, h_q, h_sc):
+            y_a = psum.tile([P, 2, Q], F32, name="y_a", tag=f"bank{2 * c}")
+            y_b = psum.tile([P, Q], F32, name="y_b", tag=f"bank{2 * c + 1}")
             ys = [y_a[:, 0, :], y_a[:, 1, :], y_b[:]]
-            for c in range(TILES_N):
-                readout_pass(ys[c], c, h_q, h_sc)
+            for f in range(TILES_N):
+                readout_pass(ys[f], f, h_q, h_sc)
             return ys
 
-        def finish_wide(ys, lo, res):
-            for c in range(TILES_N):
-                nc.scalar.activation(out=res[:, c, :], in_=ys[c], func=ACT.Identity, bias=b_col[:, c : c + 1])
-                nc.sync.dma_start(out=out_view[:, c, lo : lo + 256], in_=res[:, c, :])
+        def finish_wide(c, ys, res):
+            for f in range(TILES_N):
+                nc.scalar.activation(out=res[:, f, :], in_=ys[f], func=ACT.Identity, bias=b_col[:, f : f + 1])
+                nc.sync.dma_start(out=out_view[:, f, Q * c : Q * (c + 1)], in_=res[:, f, :])
 
-        def readout_narrow(h_q, h_sc, bank):
-            y = psum.tile([P, TILES_N, P], F32, name="y", tag=f"bank{bank}")
-            for c in range(TILES_N):
-                readout_pass(y[:, c, :], c, h_q, h_sc)
-            return y
-
-        def finish_narrow(y, lo):
-            res = ring.tile([P, TILES_N, P], F32, name="res", tag="res", bufs=5)
-            nc.vector.tensor_tensor(
-                out=res[:], in0=y[:], in1=b_col[:].unsqueeze(2).to_broadcast([P, TILES_N, P]), op=ALU.add
-            )
-            nc.sync.dma_start(out=out_view[:, :, lo : lo + P], in_=res[:])
-
-        v3_sc = keep.tile([P, S], U8, name="v3_sc", align_bytes=64)
-        sc_first = keep.tile([P, 512], U8, name="sc_first", align_bytes=64)
-        words_free = keep.tile([P, 512], U32, name="words_free", align_bytes=64)
-        gather_scales(2, 0, S, v3_sc[:])
-        v_sc[2, 0], v_sc[2, 1] = v3_sc[:, 0:512], v3_sc[:, 512:S]
-        banks = new_banks(512, 0)
-        gather_words(2, 0, 0, 512, words_free[:])
-        reorder_columns(w3_q[:], w3_raw[:], 8)
-        nc.scalar.copy(
-            out=w3_sc[:].bitcast(U32).rearrange("p t (b i) -> p t b i", i=2),
-            in_=w3_sc_raw[:].bitcast(U32).rearrange("p (b t i) -> p t b i", t=SLOTS, i=2),
-        )
-        d_passes(banks, 2, 0, 0, 512, start=True)
-        words_a = keep.tile([P, 512], U32, name="words_a", tag="slot_a", align_bytes=64)
-        gather_words(1, 0, 0, 512, words_a[:])
-        gather_scales(0, 0, 512, sc_first[:])
-        reorder_columns(w2_sc[:], w2_sc_raw[:], 2)
-        d_passes(banks, 1, 0, 0, 512)
-        words_b = keep.tile([P, 3, 512], U32, name="words_b", tag="slot_b", align_bytes=64)
-        for place, (m, a) in enumerate(((2, 1), (1, 1))):
-            gather_words(m, a, 0, 512, words_b[:, place, :])
-        d_passes(banks, 2, 1, 0, 512)
-        d_passes(banks, 1, 1, 0, 512)
+        gather_scales(0, v_sc[0])
         cast_w1(0)
-        gather_words(0, 0, 0, 512, words_b[:, 2, :])
         quantize_w1(0)
-        d_passes(banks, 0, 0, 0, 512)
         cast_w1(1)
-        words_f = keep.tile([P, 512], U32, name="words_f", tag="w1_bf01", align_bytes=64)
-        gather_words(0, 1, 0, 512, words_f[:])
+        w2_sc = placed([P, SLOTS, PASSES, P], U8, "w2_sc", 10240 + 5120)
+        w3_sc = sbuf([P, SLOTS, P], U8, "w3_sc")
+        w3_q = placed([P, SLOTS, PASSES, P], I32, "w3_q", 512)
+        reorder_columns(w2_sc[:], w2_sc_raw[:], U16, 1)
+        nc.scalar.copy(
+            out=w3_sc[:].bitcast(U16).rearrange("p t c -> p c t"),
+            in_=w3_sc_raw[:].bitcast(U16).rearrange("p (c t) -> p c t", t=SLOTS),
+        )
+        reorder_columns(w3_q[:], w3_raw[:], U32, 2)
+
+        for m, quarters, offset in ((0, 2, 10240), (1, 3, 9216 + 8192), (2, 2, 10240 + 2048)):
+            gather_words(m, 0, 0, Q * quarters, placed([P, Q * quarters], U32, f"early{m}", offset)[:])
+            if m == 0:
+                gather_scales(2, placed([P, 2 * Q], U8, "v_sc2a", 10240 + 4096), 0, 2 * Q)
+            for c in range(2):
+                d_passes(m, 0, c, first=(m == 0))
         quantize_w1(1)
-        d_passes(banks, 0, 1, 0, 512, stop=True)
-        for u, (lo, hi) in enumerate(w4_cols):
-            nc.scalar.copy(out=by_fours_out(w4_bf[u][:]), in_=by_fours_in(w4_raw[:, :, lo:hi]))
-        nc.scalar.copy(out=g_slots[:], in_=g_col[:, :, 0])
-        sq_first = square(banks, 0, 512, "w4_raw")
-        mag_half = keep.tile([P, SLOTS, 512], F32, name="mag_half")
-        for t in range(0, SLOTS, 2):
-            nc.scalar.activation(out=mag_half[:, t : t + 2, :], in_=sq_first[:, t : t + 2, :], func=ACT.Sqrt, bias=one[:])
-        mag_first = [mag_half[:, :, 256 * u : 256 * u + 256] for u in range(2)]
+        nc.scalar.copy(out=by_fours_out(w4_bf[:]), in_=by_fours_in(w4_raw[:]))
 
-        order = ((2, 0), (1, 0), (2, 1), (1, 1), (0, 0), (0, 1))
+        def stretch(c, steps, places, first):
+            for n, (m, a) in enumerate(steps):
+                gather_words(m, a, Q * c, Q * (c + 1), places[n])
+                d_passes(m, a, c, first=(first and n == 0), last=(n == len(steps) - 1))
 
-        def stretch(chunk_banks, lo, hi, steps, places):
-            for step, place in zip(steps, places):
-                m, a = order[step]
-                gather_words(m, a, lo, hi, place)
-                d_passes(chunk_banks, m, a, lo, hi, start=(step == 0), stop=(step == len(order) - 1))
-
-        sc_second = keep.tile([P, 512], U8, name="sc_second", tag="w1_bf11", align_bytes=64)
-        scaled = keep.tile([P, SLOTS, SHARE], F32, name="scaled")
-        for t in range(SLOTS):
-            nc.scalar.activation(
-                out=scaled[:, t, :], in_=mag_first[0][:, t, 0:SHARE], func=ACT.Copy, scale=g_slots[:, t : t + 1]
-            )
-        h_zero = new_h_bf(256, "h_bf")
-        words_c = keep.tile([P, 12, 256], U32, name="words_c", tag="w1_raw1", align_bytes=64)
-        banks = new_banks(256, 4)
-        stretch(banks, 512, 768, range(4), [words_c[:, step, :] for step in range(4)])
-        gather_scales(0, 512, S, sc_second[:])
-        stretch(banks, 512, 768, range(4, 6), [words_c[:, step, :] for step in range(4, 6)])
-        sq_third = square(banks, 0, 256, "w4_raw")
-        nc.scalar.copy(out=by_fours_out(h_zero[:, 0:SHARE, :]), in_=by_fours_in(scaled[:]))
-        mag_third = magnitude(sq_third, 0, 256)
-        banks = new_banks(256, 0)
-        stretch(banks, 768, S, range(6), [words_c[:, 6 + step, :] for step in range(6)])
-        sq_last = square(banks, 0, 256, "w4_raw")
-        stiffen(mag_first[0][:, :, SHARE:256], h_zero[:, SHARE:256, :])
-        late["w4_q"] = keep.tile([P, N], U32, name="w4_q", tag="table0", align_bytes=64)
-        for u, (lo, hi) in enumerate(w4_cols):
-            nc.vector.quantize_mx(
-                out=late["w4_q"][:, lo:hi].bitcast(FP8X4),
-                scales=w4_sc[:, lo:hi],
-                in_=w4_bf[u][:].rearrange("p n t -> p (n t)"),
-            )
-        y_wide = [readout_wide(*quantize_h(h_zero, new_h_q(256, "w4_bf0")), 4)]
-        mag_last = [magnitude(sq_last, 0, P, ones)]
-        res_zero = keep.tile([P, TILES_N, 256], F32, name="res_zero", tag="ones")
-        finish_wide(y_wide[0], 0, res_zero[:])
-        mag_last.append(magnitude(sq_last, P, 2 * P))
-        h_one = stiffen(mag_first[1], new_h_bf(256, "table1"))
-        h_two = stiffen(mag_third, new_h_bf(256, "w4_bf1"))
-        y_wide.append(readout_wide(*quantize_h(h_one, new_h_q(256, "h_q1")), 6))
-        h_last = [stiffen(mag_last[0], new_h_bf(P, "h_bf30"))]
-        y_wide.append(readout_wide(*quantize_h(h_two, new_h_q(256, "h_q2")), 0))
-        h_last.append(stiffen(mag_last[1], new_h_bf(P, "h_bf31")))
-        y_next = readout_narrow(*quantize_h(h_last[0], new_h_q(P, "h_q30")), 2)
-        h_q, h_sc = quantize_h(h_last[1], new_h_q(P, "h_q31"))
-        y_end = psum.tile([P, 2, P], F32, name="y_end", tag="bank3")
+        second_half = ((2, 1), (0, 1), (1, 1))
+        mags = []
+        h_bf = [sbuf([P, Q, SLOTS], BF16, f"h_bf{c}") for c in range(3)]
         for c in range(2):
-            readout_pass(y_end[:, c, :], c, h_q, h_sc)
-        res_wide = keep.tile([P, 2, TILES_N, 256], F32, name="res_wide", tag="w4_raw")
-        for u in range(1, 3):
-            finish_wide(y_wide[u], 256 * u, res_wide[:, u - 1])
-        y_rest = psum.tile([P, P], F32, name="y_rest", tag="bank5")
+            if c == 0:
+                late = placed([P, 3, Q], U32, "late0", 4608)
+                places = [late[:, n, :] for n in range(3)]
+            else:
+                gather_scales(2, placed([P, 2 * Q], U8, "v_sc2b", 0), 2 * Q, S)
+                places = [placed([P, Q], U32, f"late1{n}", 4608 + 1024 * n)[:] for n in range(3)]
+            stretch(c, second_half, places, False)
+            mags.append(magnitude(c))
+            if c == 0:
+                scaled = sbuf([P, SLOTS, SHARE], F32, "scaled")
+                for t in range(SLOTS):
+                    nc.scalar.activation(
+                        out=scaled[:, t, :], in_=mags[0][:, t, 0:SHARE], func=ACT.Copy, scale=g_slots[:, t : t + 1]
+                    )
+                nc.scalar.copy(out=by_fours_out(h_bf[0][:, 0:SHARE, :]), in_=by_fours_in(scaled[:]))
+        places = [placed([P, Q], U32, f"late2{n}", 4608 + 1024 * n)[:] for n in range(2)]
+        rest = placed([P, 3, Q], U32, "rest2", 4608 + 2048)
+        d_passes(1, 0, 2, first=True)
+        stretch(2, second_half + ((2, 0), (0, 0)), places + [rest[:, n, :] for n in range(3)], False)
+        mags.append(magnitude(2))
+        stiffen(mags[0][:, :, SHARE:Q], h_bf[0][:, SHARE:Q, :])
+        late_tiles["w4_q"] = placed([P, N], U32, "w4_q", LATE + 4608)
+        nc.vector.quantize_mx(
+            out=late_tiles["w4_q"][:].bitcast(FP8X4), scales=w4_sc[:], in_=w4_bf[:].rearrange("p n t -> p (n t)")
+        )
+        finish_wide(0, readout_wide(0, *quantize_h(h_bf[0][:], "h_q0", sbuf([P, Q], U32, "h_q0"))), sbuf([P, TILES_N, Q], F32, "res0")[:])
+        late = sbuf([P, 6, Q], U32, "late3", "scaled")
+        stretch(3, ((1, 1), (2, 1), (0, 1), (1, 0), (2, 0), (0, 0)), [late[:, n, :] for n in range(6)], True)
+        sq_last = square(3)
+        mag_last = [sbuf([P, SLOTS, P], F32, f"mag3{u}") for u in range(2)]
+        for u in range(2):
+            nc.scalar.activation(
+                out=mag_last[u][:], in_=sq_last[:, :, P * u : P * (u + 1)], func=ACT.Sqrt, bias=unit[u][:]
+            )
+
+        h_last = [sbuf([P, P, SLOTS], BF16, f"h_bf3{u}") for u in range(2)]
+        stiffen(mags[1][:], h_bf[1][:])
+        stiffen(mags[2][:], h_bf[2][:])
+        ys = [readout_wide(1, *quantize_h(h_bf[1][:], "h_q1", placed([P, Q], U32, "h_q1", LATE + 512)))]
+        stiffen(mag_last[0][:], h_last[0][:])
+        ys.append(readout_wide(2, *quantize_h(h_bf[2][:], "h_q2", sbuf([P, Q], U32, "h_q2", "unit0"))))
+        stiffen(mag_last[1][:], h_last[1][:])
+        y_next = psum.tile([P, TILES_N, P], F32, name="y_next", tag="bank6")
+        h_q, h_sc = quantize_h(h_last[0][:], "h_q30", placed([P, P], U32, "h_q30", LATE + 10240))
+        for f in range(TILES_N):
+            readout_pass(y_next[:, f, :], f, h_q, h_sc)
+        h_q, h_sc = quantize_h(h_last[1][:], "h_q31", sbuf([P, P], U32, "h_q31"))
+        y_end = psum.tile([P, 2, P], F32, name="y_end", tag="bank7")
+        for f in range(2):
+            readout_pass(y_end[:, f, :], f, h_q, h_sc)
+        res_wide = sbuf([P, 2, TILES_N, Q], F32, "res_wide", "unit1")
+        for c in range(1, 3):
+            finish_wide(c, ys[c - 1], res_wide[:, c - 1])
+        y_rest = psum.tile([P, P], F32, name="y_rest", tag="bank1")
         readout_pass(y_rest[:], 2, h_q, h_sc)
-        finish_narrow(y_next, 768)
-        res_end = keep.tile([P, 2, P], F32, name="res_end")
+        res_next = sbuf([P, TILES_N, P], F32, "res_next")
+        nc.vector.tensor_tensor(
+            out=res_next[:], in0=y_next[:], in1=b_col[:].unsqueeze(2).to_broadcast([P, TILES_N, P]), op=ALU.add
+        )
+        nc.sync.dma_start(out=out_view[:, :, 3 * Q : 3 * Q + P], in_=res_next[:])
+        res_end = sbuf([P, 2, P], F32, "res_end")
         nc.vector.tensor_tensor(
             out=res_end[:], in0=y_end[:], in1=b_col[:, 0:2].unsqueeze(2).to_broadcast([P, 2, P]), op=ALU.add
         )
-        nc.sync.dma_start(out=out_view[:, 0:2, 768 + P : S], in_=res_end[:])
-        res_rest = keep.tile([P, P], F32, name="res_rest")
+        nc.sync.dma_start(out=out_view[:, 0:2, 3 * Q + P : S], in_=res_end[:])
+        res_rest = sbuf([P, P], F32, "res_rest")
         nc.scalar.activation(out=res_rest[:], in_=y_rest[:], func=ACT.Identity, bias=b_col[:, 2:3])
-        nc.sync.dma_start(out=out_view[:, 2, 768 + P : S], in_=res_rest[:])
+        nc.scalar.dma_start(out=out_view[:, 2, 3 * Q + P : S], in_=res_rest[:])

@@ -21,8 +21,12 @@ PASSES = 2
 SLOTS = 4
 TILES_N = 3
 Q = 256
-SHARE = 128
-LATE = 20480
+E = 128
+CHUNKS = ((0, 256), (256, 512), (512, 768), (768, 896), (896, 1024))
+RAW = (0, 8192)
+MAG = (25600, 31744)
+LAST = 51200
+UNIT = (36864, 40960, 45056)
 
 
 def tile_list_cloth_stretch_features_kernel(
@@ -48,19 +52,18 @@ def tile_list_cloth_stretch_features_kernel(
         w3_raw = sbuf([P, PASSES, H], I32, "w3_raw")
         w2_raw = sbuf([P, PASSES, H // 2], I32, "w2_raw")
         w2_q = sbuf([P, SLOTS, PASSES, 2 * P], U8, "w2_q")
-        w1_raw = [placed([P, 4, H], F32, "w1_raw0", 10240), placed([P, 4, H], F32, "w1_raw1", 0)]
+        w1_raw = [placed([P, 4, H], F32, f"w1_raw{a}", RAW[a]) for a in range(PASSES)]
         w1_bf = [sbuf([P, SLOTS, 4 * P], BF16, f"w1_bf{a}") for a in range(PASSES)]
         w1_q = [sbuf([P, H], U32, f"w1_q{a}") for a in range(PASSES)]
         w1_sc = [sbuf([P, H], U8, f"w1_sc{a}") for a in range(PASSES)]
-        w4_raw = placed([P, SLOTS, N], F32, "w4_raw", LATE + 2048)
-        w4_bf = sbuf([P, N, SLOTS], BF16, "w4_bf")
+        w4_raw = sbuf([P, SLOTS, N], F32, "w4_raw")
         w4_sc = sbuf([P, N], U8, "w4_sc")
         g_slots = sbuf([P, SLOTS], F32, "g_slots")
         b_col = sbuf([P, TILES_N], F32, "b_col")
-        unit = [sbuf([P, 1], F32, f"unit{u}") for u in range(2)]
+        unit = [placed([P, 1], F32, f"unit{u}", UNIT[u]) for u in range(3)]
         one = sbuf([P, 1], F32, "one")
-        v_sc = [sbuf([P, S], U8, f"v_sc{m}") for m in range(2)]
-        planes = {}
+        v2_sc = sbuf([P, S], U8, "v2_sc")
+        planes = {m: [] for m in range(3)}
         v2_sc_pass1 = sbuf([P, S], U8, "v2_sc_pass1")
 
         nc.gpsimd.memset(table_sc[:].bitcast(I32), 0)
@@ -68,7 +71,8 @@ def tile_list_cloth_stretch_features_kernel(
         nc.gpsimd.memset(w2_sc_raw[:].rearrange("p a c -> p (a c)").bitcast(I32), 0)
         nc.gpsimd.memset(w3_sc_raw[:].bitcast(I32), 0)
         nc.gpsimd.memset(v2_sc_pass1[:].bitcast(I32), 0)
-        nc.gpsimd.memset(unit[1][:], 1.0)
+        for u in range(1, 3):
+            nc.gpsimd.memset(unit[u][:], 1.0)
         nc.scalar.activation(out=one[:], in_=unit[0][:], func=ACT.Sqrt)
 
         def load_table(a):
@@ -78,8 +82,7 @@ def tile_list_cloth_stretch_features_kernel(
             nc.sync.dma_start(out=w1_raw[a][:], in_=w1[512 * a : 512 * (a + 1), :].rearrange("(p j) r -> p j r", j=4))
 
         def gather_scales(m, dst, lo=0, hi=S):
-            for c in range(lo // Q, hi // Q):
-                planes[m, c] = (dst, slice(Q * c - lo, Q * (c + 1) - lo))
+            planes[m].append((lo, hi, dst))
             nc.vector.tensor_copy(out=dst[:], in_=table_sc[:].indirect(lists[m][:, lo // 16 : hi // 16]))
 
         nc.sync.dma_start(out=w2_raw[:], in_=w2_words.rearrange("a p c -> p a c").bitcast(I32))
@@ -93,9 +96,8 @@ def tile_list_cloth_stretch_features_kernel(
             out=w2_q[:].bitcast(I32).rearrange("p t a c -> p (a c) t"),
             in_=w2_raw[:].rearrange("p a (c t) -> p (a c) t", t=SLOTS),
         )
-        gather_scales(1, v_sc[1])
+        gather_scales(1, v2_sc)
         nc.sync.dma_start(lists[0][:], offs)
-        load_w1(0)
         load_table(0)
         for r in range(4):
             nc.sync.dma_start(
@@ -103,8 +105,9 @@ def tile_list_cloth_stretch_features_kernel(
                 in_=w2_scales.rearrange("a (q r) c -> r q a c", r=4)[r].bitcast(I32),
             )
         nc.sync.dma_start(lists[2][:], offs3)
+        load_w1(0)
         load_w1(1)
-        nc.sync.dma_start(out=v2_sc_pass1[0:100, :].bitcast(I32), in_=v_sc[1][4:104, :].bitcast(I32))
+        nc.sync.dma_start(out=v2_sc_pass1[0:100, :].bitcast(I32), in_=v2_sc[4:104, :].bitcast(I32))
         for q in range(4):
             nc.sync.dma_start(
                 out=w3_sc_raw[32 * q : 32 * q + 8, :].bitcast(I32),
@@ -119,45 +122,53 @@ def tile_list_cloth_stretch_features_kernel(
                 nc.sync.dma_start(out=g_slots[i:P:2, :], in_=g.rearrange("(c t i) -> i c t", t=SLOTS, i=2)[i])
             nc.sync.dma_start(out=b_col[:], in_=b.rearrange("(c p) -> p c", p=P))
 
-        words = {}
-        late_tiles = {}
-
-        def gather_words(m, a, lo, hi, dst):
-            for c in range(lo // Q, hi // Q):
-                words[m, a, c] = dst[:, Q * c - lo : Q * (c + 1) - lo]
-            nc.vector.tensor_copy(out=dst, in_=table[a][:].bitcast(U32).indirect(lists[m][:, lo // 16 : hi // 16]))
-
+        words = {(m, a): [] for m in range(3) for a in range(PASSES)}
         banks = {}
 
-        def open_banks(c):
-            banks[c] = [psum.tile([P, Q], F32, name=f"d{c}{t}", tag=f"bank{4 * (c % 2) + t}") for t in range(SLOTS)]
+        def gather_words(m, a, lo, hi, dst):
+            words[m, a].append((lo, hi, dst))
+            nc.vector.tensor_copy(out=dst, in_=table[a][:].bitcast(U32).indirect(lists[m][:, lo // 16 : hi // 16]))
+
+        def columns(pieces, lo, hi):
+            return [(dst, slice(lo - begin, hi - begin)) for begin, end, dst in pieces if begin <= lo and hi <= end][0]
+
+        def open_banks(c, first_bank, count):
+            lo, hi = CHUNKS[c]
+            banks[c] = [
+                psum.tile([P, SLOTS // count, hi - lo], F32, name=f"d{c}{u}", tag=f"bank{first_bank + u}")
+                for u in range(count)
+            ]
 
         def d_passes(m, a, c, first=False, last=False):
-            plane, cols = planes[m, c]
-            if first:
-                open_banks(c)
-            for t in range(SLOTS):
-                if m == 0:
-                    lhs, lhs_sc = w1_q[a][:, P * t : P * (t + 1)].bitcast(FP8X4), w1_sc[a][:, P * t : P * (t + 1)]
-                    rhs_sc = plane[4 * a : P, cols]
-                elif m == 1:
-                    lhs, lhs_sc = w2_q[:, t, a, :].bitcast(FP4X4), w2_sc[:, t, a, :]
-                    rhs_sc = (plane, v2_sc_pass1)[a][:, cols]
-                else:
-                    lhs, lhs_sc = w3_q[:, t, a, :].bitcast(FP8X4), w3_sc[4 * a : P, t, :]
-                    rhs_sc = plane[4 * a : P, cols]
-                nc.tensor.matmul_mx(
-                    out=banks[c][t][:],
-                    lhsT=lhs,
-                    lhsT_scale=lhs_sc,
-                    rhs=words[m, a, c].bitcast(FP8X4),
-                    rhs_scale=rhs_sc,
-                    start=first,
-                    stop=last,
-                )
+            lo, hi = CHUNKS[c]
+            rhs, cols = columns(words[m, a], lo, hi)
+            plane, sc_cols = columns(planes[m], lo, hi)
+            count = len(banks[c])
+            share = SLOTS // count
+            for place in range(share):
+                for u in range(count):
+                    t = share * u + place
+                    if m == 0:
+                        lhs, lhs_sc = w1_q[a][:, P * t : P * (t + 1)].bitcast(FP8X4), w1_sc[a][:, P * t : P * (t + 1)]
+                        rhs_sc = plane[4 * a : P, sc_cols]
+                    elif m == 1:
+                        lhs, lhs_sc = w2_q[:, t, a, :].bitcast(FP4X4), w2_sc[:, t, a, :]
+                        rhs_sc = (plane, v2_sc_pass1)[a][:, sc_cols]
+                    else:
+                        lhs, lhs_sc = w3_q[:, t, a, :].bitcast(FP8X4), w3_sc[4 * a : P, t, :]
+                        rhs_sc = plane[4 * a : P, sc_cols]
+                    nc.tensor.matmul_mx(
+                        out=banks[c][u][:, place, :],
+                        lhsT=lhs,
+                        lhsT_scale=lhs_sc,
+                        rhs=rhs[:, cols].bitcast(FP8X4),
+                        rhs_scale=rhs_sc,
+                        start=first and place == 0,
+                        stop=last and place == share - 1,
+                    )
 
-        def by_fours_in(planes):
-            return planes.rearrange("p t (c i) -> p c t i", i=4)
+        def by_fours_in(planar):
+            return planar.rearrange("p t (c i) -> p c t i", i=4)
 
         def by_fours_out(woven):
             return woven.rearrange("p (c i) t -> p c t i", i=4)
@@ -179,19 +190,23 @@ def tile_list_cloth_stretch_features_kernel(
                 in_=src.bitcast(dtype).rearrange("p a (c t i) -> p (a c) t i", t=SLOTS, i=run),
             )
 
-        def square(c):
-            sq = placed([P, SLOTS, Q], F32, f"sq{c}", LATE + (4096, 6144, 512, 10240)[c])
-            for t in range(SLOTS):
-                nc.scalar.activation(out=sq[:, t, :], in_=banks[c][t][:], func=ACT.Square)
+        def square(c, sq):
+            share = SLOTS // len(banks[c])
+            for u, bank in enumerate(banks[c]):
+                nc.scalar.activation(out=sq[:, share * u : share * (u + 1), :], in_=bank[:], func=ACT.Square)
             return sq
 
-        def magnitude(c):
-            sq = square(c)
-            mag = sbuf([P, SLOTS, Q], F32, f"mag{c}")
-            for u in range(2):
-                nc.scalar.activation(
-                    out=mag[:, 2 * u : 2 * u + 2, :], in_=sq[:, 2 * u : 2 * u + 2, :], func=ACT.Sqrt, bias=one[:]
-                )
+        def root(mag, sq, bias):
+            nc.scalar.activation(out=mag, in_=sq, func=ACT.Sqrt, bias=bias[:])
+
+        def magnitude(c, sq, mag, bias):
+            square(c, sq)
+            if c == 0:
+                root(mag[:, :, 0:E], sq[:, :, 0:E], bias)
+                root(mag[:, :, E:Q], sq[:, :, E:Q], one)
+            else:
+                root(mag[:, 0:2, :], sq[:, 0:2, :], bias)
+                root(mag[:, 2:4, :], sq[:, 2:4, :], one)
             return mag
 
         def stiffen(mag, h_bf):
@@ -203,136 +218,149 @@ def tile_list_cloth_stretch_features_kernel(
                 op=ALU.mult,
             )
 
+        def stiffen_beside(mag, h_bf):
+            for lo in range(0, Q, E):
+                nc.gpsimd.tensor_tensor(
+                    out=h_bf[:, lo : lo + E, :],
+                    in0=mag[:, :, lo : lo + E].rearrange("p t n -> p n t"),
+                    in1=g_slots[:].unsqueeze(1).to_broadcast([P, E, SLOTS]),
+                    op=ALU.mult,
+                )
+
         def quantize_h(h_bf, name, h_q):
             width = h_bf.shape[1]
             h_sc = sbuf([P, width], U8, name + "_sc")
-            nc.vector.quantize_mx(out=h_q[:].bitcast(FP8X4), scales=h_sc[:], in_=h_bf.rearrange("p n t -> p (n t)"))
+            nc.vector.quantize_mx(out=h_q[:].bitcast(FP8X4), scales=h_sc[:], in_=h_bf[:].rearrange("p n t -> p (n t)"))
             return h_q, h_sc
 
-        def readout_pass(dst, f, h_q, h_sc):
-            w4_q = late_tiles["w4_q"]
-            nc.tensor.matmul_mx(
-                out=dst,
-                lhsT=w4_q[:, P * f : P * (f + 1)].bitcast(FP8X4),
-                lhsT_scale=w4_sc[:, P * f : P * (f + 1)],
-                rhs=h_q[:].bitcast(FP8X4),
-                rhs_scale=h_sc[:],
-                start=True,
-                stop=True,
-            )
+        def readout(w4_q, h_q, h_sc, targets):
+            for f, dst in enumerate(targets):
+                nc.tensor.matmul_mx(
+                    out=dst,
+                    lhsT=w4_q[:, P * f : P * (f + 1)].bitcast(FP8X4),
+                    lhsT_scale=w4_sc[:, P * f : P * (f + 1)],
+                    rhs=h_q[:].bitcast(FP8X4),
+                    rhs_scale=h_sc[:],
+                    start=True,
+                    stop=True,
+                )
+            return targets
 
         out_view = out.rearrange("(f p) j -> p f j", p=P)
 
-        def readout_wide(c, h_q, h_sc):
-            y_a = psum.tile([P, 2, Q], F32, name="y_a", tag=f"bank{2 * c}")
-            y_b = psum.tile([P, Q], F32, name="y_b", tag=f"bank{2 * c + 1}")
-            ys = [y_a[:, 0, :], y_a[:, 1, :], y_b[:]]
-            for f in range(TILES_N):
-                readout_pass(ys[f], f, h_q, h_sc)
-            return ys
+        def wide_targets(first_bank):
+            y_a = psum.tile([P, 2, Q], F32, name="y_a", tag=f"bank{first_bank}")
+            y_b = psum.tile([P, Q], F32, name="y_b", tag=f"bank{first_bank + 1}")
+            return [y_a[:, 0, :], y_a[:, 1, :], y_b[:]]
 
-        def finish_wide(c, ys, res):
+        def finish_on_scalar(c, ys, res):
+            lo, hi = CHUNKS[c]
             for f in range(TILES_N):
                 nc.scalar.activation(out=res[:, f, :], in_=ys[f], func=ACT.Identity, bias=b_col[:, f : f + 1])
-                nc.sync.dma_start(out=out_view[:, f, Q * c : Q * (c + 1)], in_=res[:, f, :])
+                nc.sync.dma_start(out=out_view[:, f, lo:hi], in_=res[:, f, :])
 
-        gather_scales(0, v_sc[0])
-        cast_w1(0)
-        quantize_w1(0)
-        cast_w1(1)
-        w2_sc = placed([P, SLOTS, PASSES, P], U8, "w2_sc", 10240 + 5120)
-        w3_sc = sbuf([P, SLOTS, P], U8, "w3_sc")
-        w3_q = placed([P, SLOTS, PASSES, P], I32, "w3_q", 512)
+        def finish_on_vector(c, y, res):
+            lo, hi = CHUNKS[c]
+            nc.vector.tensor_tensor(
+                out=res[:], in0=y[:], in1=b_col[:].unsqueeze(2).to_broadcast([P, TILES_N, E]), op=ALU.add
+            )
+            nc.sync.dma_start(out=out_view[:, :, lo:hi], in_=res[:])
+
+        gather_scales(0, sbuf([P, 3 * Q], U8, "v1_sc"), 0, 3 * Q)
+        w2_sc = sbuf([P, SLOTS, PASSES, P], U8, "w2_sc")
         reorder_columns(w2_sc[:], w2_sc_raw[:], U16, 1)
+        cast_w1(0)
+        cast_w1(1)
+        w3_sc = sbuf([P, SLOTS, P], U8, "w3_sc")
+        w3_q = placed([P, SLOTS, PASSES, P], I32, "w3_q", RAW[1])
         nc.scalar.copy(
             out=w3_sc[:].bitcast(U16).rearrange("p t c -> p c t"),
             in_=w3_sc_raw[:].bitcast(U16).rearrange("p (c t) -> p c t", t=SLOTS),
         )
         reorder_columns(w3_q[:], w3_raw[:], U32, 2)
-
-        for m, quarters, offset in ((0, 2, 10240), (1, 3, 9216 + 8192), (2, 2, 10240 + 2048)):
-            gather_words(m, 0, 0, Q * quarters, placed([P, Q * quarters], U32, f"early{m}", offset)[:])
-            if m == 0:
-                gather_scales(2, placed([P, 2 * Q], U8, "v_sc2a", 10240 + 4096), 0, 2 * Q)
-            for c in range(2):
-                d_passes(m, 0, c, first=(m == 0))
-        quantize_w1(1)
-        nc.scalar.copy(out=by_fours_out(w4_bf[:]), in_=by_fours_in(w4_raw[:]))
-
-        def stretch(c, steps, places, first):
-            for n, (m, a) in enumerate(steps):
-                gather_words(m, a, Q * c, Q * (c + 1), places[n])
-                d_passes(m, a, c, first=(first and n == 0), last=(n == len(steps) - 1))
-
-        second_half = ((2, 1), (0, 1), (1, 1))
-        mags = []
-        h_bf = [sbuf([P, Q, SLOTS], BF16, f"h_bf{c}") for c in range(3)]
         for c in range(2):
-            if c == 0:
-                late = placed([P, 3, Q], U32, "late0", 4608)
-                places = [late[:, n, :] for n in range(3)]
+            open_banks(c, 4 * c, 4)
+        for m in (1, 0, 2):
+            if m == 1:
+                gather_words(m, 0, 0, 2 * Q, sbuf([P, 2 * Q], U32, "early1")[:])
+                gather_scales(2, sbuf([P, 3 * Q], U8, "v3_sc"), 0, 3 * Q)
+                quantize_w1(0)
             else:
-                gather_scales(2, placed([P, 2 * Q], U8, "v_sc2b", 0), 2 * Q, S)
-                places = [placed([P, Q], U32, f"late1{n}", 4608 + 1024 * n)[:] for n in range(3)]
-            stretch(c, second_half, places, False)
-            mags.append(magnitude(c))
-            if c == 0:
-                scaled = sbuf([P, SLOTS, SHARE], F32, "scaled")
-                for t in range(SLOTS):
-                    nc.scalar.activation(
-                        out=scaled[:, t, :], in_=mags[0][:, t, 0:SHARE], func=ACT.Copy, scale=g_slots[:, t : t + 1]
-                    )
-                nc.scalar.copy(out=by_fours_out(h_bf[0][:, 0:SHARE, :]), in_=by_fours_in(scaled[:]))
-        places = [placed([P, Q], U32, f"late2{n}", 4608 + 1024 * n)[:] for n in range(2)]
-        rest = placed([P, 3, Q], U32, "rest2", 4608 + 2048)
-        d_passes(1, 0, 2, first=True)
-        stretch(2, second_half + ((2, 0), (0, 0)), places + [rest[:, n, :] for n in range(3)], False)
-        mags.append(magnitude(2))
-        stiffen(mags[0][:, :, SHARE:Q], h_bf[0][:, SHARE:Q, :])
-        late_tiles["w4_q"] = placed([P, N], U32, "w4_q", LATE + 4608)
-        nc.vector.quantize_mx(
-            out=late_tiles["w4_q"][:].bitcast(FP8X4), scales=w4_sc[:], in_=w4_bf[:].rearrange("p n t -> p (n t)")
-        )
-        finish_wide(0, readout_wide(0, *quantize_h(h_bf[0][:], "h_q0", sbuf([P, Q], U32, "h_q0"))), sbuf([P, TILES_N, Q], F32, "res0")[:])
-        late = sbuf([P, 6, Q], U32, "late3", "scaled")
-        stretch(3, ((1, 1), (2, 1), (0, 1), (1, 0), (2, 0), (0, 0)), [late[:, n, :] for n in range(6)], True)
-        sq_last = square(3)
-        mag_last = [sbuf([P, SLOTS, P], F32, f"mag3{u}") for u in range(2)]
-        for u in range(2):
-            nc.scalar.activation(
-                out=mag_last[u][:], in_=sq_last[:, :, P * u : P * (u + 1)], func=ACT.Sqrt, bias=unit[u][:]
+                gather_words(m, 0, 0, 2 * Q, placed([P, 2 * Q], U32, f"early{m}", RAW[0] + 2048 * m)[:])
+            for c in range(2):
+                d_passes(m, 0, c, first=(m == 1))
+        quantize_w1(1)
+        w4_bf = sbuf([P, N, SLOTS], BF16, "w4_bf", "w1_bf1")
+        for lo, hi in ((0, Q), (Q, N)):
+            nc.gpsimd.tensor_scalar(
+                out=w4_bf[:, lo:hi, :],
+                in0=w4_raw[:, :, lo:hi].rearrange("p t n -> p n t"),
+                scalar1=1.0,
+                scalar2=0.0,
+                op0=ALU.mult,
+                op1=ALU.add,
             )
 
-        h_last = [sbuf([P, P, SLOTS], BF16, f"h_bf3{u}") for u in range(2)]
-        stiffen(mags[1][:], h_bf[1][:])
-        stiffen(mags[2][:], h_bf[2][:])
-        ys = [readout_wide(1, *quantize_h(h_bf[1][:], "h_q1", placed([P, Q], U32, "h_q1", LATE + 512)))]
-        stiffen(mag_last[0][:], h_last[0][:])
-        ys.append(readout_wide(2, *quantize_h(h_bf[2][:], "h_q2", sbuf([P, Q], U32, "h_q2", "unit0"))))
-        stiffen(mag_last[1][:], h_last[1][:])
-        y_next = psum.tile([P, TILES_N, P], F32, name="y_next", tag="bank6")
-        h_q, h_sc = quantize_h(h_last[0][:], "h_q30", placed([P, P], U32, "h_q30", LATE + 10240))
-        for f in range(TILES_N):
-            readout_pass(y_next[:, f, :], f, h_q, h_sc)
-        h_q, h_sc = quantize_h(h_last[1][:], "h_q31", sbuf([P, P], U32, "h_q31"))
-        y_end = psum.tile([P, 2, P], F32, name="y_end", tag="bank7")
-        for f in range(2):
-            readout_pass(y_end[:, f, :], f, h_q, h_sc)
-        res_wide = sbuf([P, 2, TILES_N, Q], F32, "res_wide", "unit1")
-        for c in range(1, 3):
-            finish_wide(c, ys[c - 1], res_wide[:, c - 1])
-        y_rest = psum.tile([P, P], F32, name="y_rest", tag="bank1")
-        readout_pass(y_rest[:], 2, h_q, h_sc)
-        res_next = sbuf([P, TILES_N, P], F32, "res_next")
-        nc.vector.tensor_tensor(
-            out=res_next[:], in0=y_next[:], in1=b_col[:].unsqueeze(2).to_broadcast([P, TILES_N, P]), op=ALU.add
+        def stretch(c, steps, places, first=False):
+            lo, hi = CHUNKS[c]
+            for n, (m, a) in enumerate(steps):
+                gather_words(m, a, lo, hi, places[:, n, :])
+                d_passes(m, a, c, first=(first and n == 0), last=(n == len(steps) - 1))
+
+        second_half = ((2, 1), (1, 1), (0, 1))
+        first_half = ((1, 0), (2, 0), (0, 0))
+        late_at = (RAW[1] + 7168, RAW[1] + 4096)
+        stretch(0, second_half, placed([P, 3, Q], U32, "late0", late_at[0]))
+        mag0 = magnitude(0, sbuf([P, SLOTS, Q], F32, "sq0"), placed([P, SLOTS, Q], F32, "mag0", MAG[0]), unit[0])
+        h0 = sbuf([P, Q, SLOTS], BF16, "h_bf0", "h_bf")
+        stiffen_beside(mag0, h0)
+        stretch(1, second_half, placed([P, 3, Q], U32, "late1", late_at[1]))
+        mag1 = magnitude(
+            1, placed([P, SLOTS, Q], F32, "sq1", UNIT[0]), placed([P, SLOTS, Q], F32, "mag1", MAG[1]), unit[1]
         )
-        nc.sync.dma_start(out=out_view[:, :, 3 * Q : 3 * Q + P], in_=res_next[:])
-        res_end = sbuf([P, 2, P], F32, "res_end")
-        nc.vector.tensor_tensor(
-            out=res_end[:], in0=y_end[:], in1=b_col[:, 0:2].unsqueeze(2).to_broadcast([P, 2, P]), op=ALU.add
-        )
-        nc.sync.dma_start(out=out_view[:, 0:2, 3 * Q + P : S], in_=res_end[:])
-        res_rest = sbuf([P, P], F32, "res_rest")
-        nc.scalar.activation(out=res_rest[:], in_=y_rest[:], func=ACT.Identity, bias=b_col[:, 2:3])
-        nc.scalar.dma_start(out=out_view[:, 2, 3 * Q + P : S], in_=res_rest[:])
+        open_banks(2, 0, 2)
+        stretch(2, second_half + first_half, placed([P, 6, Q], U32, "late2", late_at[0] + 2048), True)
+        gather_scales(0, placed([P, Q], U8, "v1_sc_end", late_at[1]), 3 * Q, S)
+        gather_scales(2, placed([P, Q], U8, "v3_sc_end", late_at[1] + 256), 3 * Q, S)
+        for c in (3, 4):
+            open_banks(c, 1 + c, 1)
+
+        def early_end(n, place):
+            m, a = first_half[n]
+            gather_words(m, a, 3 * Q, S, place[:])
+            for c in (3, 4):
+                d_passes(m, a, c, first=(n == 0))
+
+        early_end(0, placed([P, Q], U32, "early_end0", late_at[1] + 512))
+        w4_q = placed([P, N], U32, "w4_q", MAG[0] - 1024)
+        nc.vector.quantize_mx(out=w4_q[:].bitcast(FP8X4), scales=w4_sc[:], in_=w4_bf[:].rearrange("p n t -> p (n t)"))
+        y0 = readout(w4_q, *quantize_h(h0, "h_q0", sbuf([P, Q], U32, "h_q0")), wide_targets(2))
+        h1 = sbuf([P, Q, SLOTS], BF16, "h_bf1", "h_bf")
+        stiffen_beside(mag1, h1)
+        mag2 = magnitude(2, placed([P, SLOTS, Q], F32, "sq2", UNIT[1]), sbuf([P, SLOTS, Q], F32, "mag2"), one)
+        finish_on_scalar(0, y0, sbuf([P, TILES_N, Q], F32, "res0"))
+        for n in (1, 2):
+            early_end(n, placed([P, Q], U32, f"early_end{n}", MAG[0] + 512 + 1024 * (n - 1)))
+        mag_end = []
+        late_end = placed([P, 2, 3, E], U32, "late_end", MAG[0] + 2560)
+        sq_end = [sbuf([P, SLOTS, E], F32, "sq3"), placed([P, SLOTS, E], F32, "sq4", LAST)]
+        for c in (3, 4):
+            stretch(c, second_half, late_end[:, c - 3])
+            mag_end.append(sbuf([P, SLOTS, E], F32, f"mag{c}"))
+            root(mag_end[-1][:], square(c, sq_end[c - 3])[:], one if c == 3 else unit[2])
+        y1 = readout(w4_q, *quantize_h(h1, "h_q1", sbuf([P, Q], U32, "h_q1")), wide_targets(6))
+        h2 = sbuf([P, Q, SLOTS], BF16, "h_bf2")
+        h_end = [sbuf([P, E, SLOTS], BF16, f"h_bf{c}") for c in (3, 4)]
+        stiffen(mag2[:], h2[:])
+        stiffen(mag_end[0][:], h_end[0][:])
+        y2 = readout(w4_q, *quantize_h(h2, "h_q2", sbuf([P, Q], U32, "h_q2", "sq3")), wide_targets(0))
+        stiffen(mag_end[1][:], h_end[1][:])
+        y_end = []
+        for c, h_q in ((3, placed([P, E], U32, "h_q3", LAST)), (4, sbuf([P, E], U32, "h_q4"))):
+            y_end.append(psum.tile([P, TILES_N, E], F32, name=f"y{c}", tag=f"bank{1 + c}"))
+            readout(w4_q, *quantize_h(h_end[c - 3], f"h_q{c}", h_q), [y_end[-1][:, f, :] for f in range(TILES_N)])
+        res = placed([P, 2, TILES_N, Q], F32, "res12", UNIT[2])
+        finish_on_scalar(1, y1, res[:, 0])
+        finish_on_scalar(2, y2, res[:, 1])
+        finish_on_vector(3, y_end[0], placed([P, TILES_N, E], F32, "res3", LAST + 512))
+        finish_on_vector(4, y_end[1], sbuf([P, TILES_N, E], F32, "res4"))

@@ -218,8 +218,8 @@ def tile_list_cloth_stretch_features_kernel(
                 op=ALU.mult,
             )
 
-        def stiffen_beside(mag, h_bf):
-            for lo in range(0, Q, E):
+        def stiffen_beside(mag, h_bf, width):
+            for lo in range(0, width, E):
                 nc.gpsimd.tensor_tensor(
                     out=h_bf[:, lo : lo + E, :],
                     in0=mag[:, :, lo : lo + E].rearrange("p t n -> p n t"),
@@ -266,7 +266,7 @@ def tile_list_cloth_stretch_features_kernel(
             )
             nc.sync.dma_start(out=out_view[:, :, lo:hi], in_=res[:])
 
-        gather_scales(0, sbuf([P, 3 * Q], U8, "v1_sc"), 0, 3 * Q)
+        gather_scales(0, sbuf([P, S], U8, "v1_sc"))
         w2_sc = sbuf([P, SLOTS, PASSES, P], U8, "w2_sc")
         reorder_columns(w2_sc[:], w2_sc_raw[:], U16, 1)
         cast_w1(0)
@@ -278,12 +278,12 @@ def tile_list_cloth_stretch_features_kernel(
             in_=w3_sc_raw[:].bitcast(U16).rearrange("p (c t) -> p c t", t=SLOTS),
         )
         reorder_columns(w3_q[:], w3_raw[:], U32, 2)
-        for c in range(2):
-            open_banks(c, 4 * c, 4)
+        open_banks(0, 0, 4)
+        open_banks(1, 4, 2)
         for m in (1, 0, 2):
             if m == 1:
                 gather_words(m, 0, 0, 2 * Q, sbuf([P, 2 * Q], U32, "early1")[:])
-                gather_scales(2, sbuf([P, 3 * Q], U8, "v3_sc"), 0, 3 * Q)
+                gather_scales(2, sbuf([P, S], U8, "v3_sc"))
                 quantize_w1(0)
             else:
                 gather_words(m, 0, 0, 2 * Q, placed([P, 2 * Q], U32, f"early{m}", RAW[0] + 2048 * m)[:])
@@ -313,17 +313,15 @@ def tile_list_cloth_stretch_features_kernel(
         stretch(0, second_half, placed([P, 3, Q], U32, "late0", late_at[0]))
         mag0 = magnitude(0, sbuf([P, SLOTS, Q], F32, "sq0"), placed([P, SLOTS, Q], F32, "mag0", MAG[0]), unit[0])
         h0 = sbuf([P, Q, SLOTS], BF16, "h_bf0", "h_bf")
-        stiffen_beside(mag0, h0)
+        stiffen_beside(mag0, h0, Q)
         stretch(1, second_half, placed([P, 3, Q], U32, "late1", late_at[1]))
         mag1 = magnitude(
             1, placed([P, SLOTS, Q], F32, "sq1", UNIT[0]), placed([P, SLOTS, Q], F32, "mag1", MAG[1]), unit[1]
         )
         open_banks(2, 0, 2)
         stretch(2, second_half + first_half, placed([P, 6, Q], U32, "late2", late_at[0] + 2048), True)
-        gather_scales(0, placed([P, Q], U8, "v1_sc_end", late_at[1]), 3 * Q, S)
-        gather_scales(2, placed([P, Q], U8, "v3_sc_end", late_at[1] + 256), 3 * Q, S)
         for c in (3, 4):
-            open_banks(c, 1 + c, 1)
+            open_banks(c, 3 + c, 1)
 
         def early_end(n, place):
             m, a = first_half[n]
@@ -331,16 +329,16 @@ def tile_list_cloth_stretch_features_kernel(
             for c in (3, 4):
                 d_passes(m, a, c, first=(n == 0))
 
-        early_end(0, placed([P, Q], U32, "early_end0", late_at[1] + 512))
+        for n in range(2):
+            early_end(n, placed([P, Q], U32, f"early_end{n}", late_at[1] + 1024 * n))
         w4_q = placed([P, N], U32, "w4_q", MAG[0] - 1024)
         nc.vector.quantize_mx(out=w4_q[:].bitcast(FP8X4), scales=w4_sc[:], in_=w4_bf[:].rearrange("p n t -> p (n t)"))
         y0 = readout(w4_q, *quantize_h(h0, "h_q0", sbuf([P, Q], U32, "h_q0")), wide_targets(2))
         h1 = sbuf([P, Q, SLOTS], BF16, "h_bf1", "h_bf")
-        stiffen_beside(mag1, h1)
+        stiffen_beside(mag1, h1, E)
         mag2 = magnitude(2, placed([P, SLOTS, Q], F32, "sq2", UNIT[1]), sbuf([P, SLOTS, Q], F32, "mag2"), one)
         finish_on_scalar(0, y0, sbuf([P, TILES_N, Q], F32, "res0"))
-        for n in (1, 2):
-            early_end(n, placed([P, Q], U32, f"early_end{n}", MAG[0] + 512 + 1024 * (n - 1)))
+        early_end(2, placed([P, Q], U32, "early_end2", MAG[0] + 512))
         mag_end = []
         late_end = placed([P, 2, 3, E], U32, "late_end", MAG[0] + 2560)
         sq_end = [sbuf([P, SLOTS, E], F32, "sq3"), placed([P, SLOTS, E], F32, "sq4", LAST)]
@@ -348,16 +346,17 @@ def tile_list_cloth_stretch_features_kernel(
             stretch(c, second_half, late_end[:, c - 3])
             mag_end.append(sbuf([P, SLOTS, E], F32, f"mag{c}"))
             root(mag_end[-1][:], square(c, sq_end[c - 3])[:], one if c == 3 else unit[2])
-        y1 = readout(w4_q, *quantize_h(h1, "h_q1", sbuf([P, Q], U32, "h_q1")), wide_targets(6))
         h2 = sbuf([P, Q, SLOTS], BF16, "h_bf2")
         h_end = [sbuf([P, E, SLOTS], BF16, f"h_bf{c}") for c in (3, 4)]
+        stiffen(mag1[:, :, E:Q], h1[:, E:Q, :])
         stiffen(mag2[:], h2[:])
+        y1 = readout(w4_q, *quantize_h(h1, "h_q1", placed([P, Q], U32, "h_q1", UNIT[1])), wide_targets(4))
         stiffen(mag_end[0][:], h_end[0][:])
         y2 = readout(w4_q, *quantize_h(h2, "h_q2", sbuf([P, Q], U32, "h_q2", "sq3")), wide_targets(0))
         stiffen(mag_end[1][:], h_end[1][:])
         y_end = []
         for c, h_q in ((3, placed([P, E], U32, "h_q3", LAST)), (4, sbuf([P, E], U32, "h_q4"))):
-            y_end.append(psum.tile([P, TILES_N, E], F32, name=f"y{c}", tag=f"bank{1 + c}"))
+            y_end.append(psum.tile([P, TILES_N, E], F32, name=f"y{c}", tag=f"bank{3 + c}"))
             readout(w4_q, *quantize_h(h_end[c - 3], f"h_q{c}", h_q), [y_end[-1][:, f, :] for f in range(TILES_N)])
         res = placed([P, 2, TILES_N, Q], F32, "res12", UNIT[2])
         finish_on_scalar(1, y1, res[:, 0])

@@ -26,6 +26,7 @@ CHUNKS = ((0, 256), (256, 512), (512, 768), (768, 896), (896, 1024))
 RAW = (0, 8192)
 MAG = (25600, 31744)
 LAST = 51200
+W4 = 57344
 UNIT = (36864, 40960, 45056)
 
 
@@ -56,7 +57,7 @@ def tile_list_cloth_stretch_features_kernel(
         w1_bf = [sbuf([P, SLOTS, 4 * P], BF16, f"w1_bf{a}") for a in range(PASSES)]
         w1_q = [sbuf([P, H], U32, f"w1_q{a}") for a in range(PASSES)]
         w1_sc = [sbuf([P, H], U8, f"w1_sc{a}") for a in range(PASSES)]
-        w4_raw = sbuf([P, SLOTS, N], F32, "w4_raw")
+        w4_raw = placed([P, SLOTS, N], F32, "w4_raw", W4)
         w4_sc = sbuf([P, N], U8, "w4_sc")
         g_slots = sbuf([P, SLOTS], F32, "g_slots")
         b_col = sbuf([P, TILES_N], F32, "b_col")
@@ -199,14 +200,14 @@ def tile_list_cloth_stretch_features_kernel(
         def root(mag, sq, bias):
             nc.scalar.activation(out=mag, in_=sq, func=ACT.Sqrt, bias=bias[:])
 
-        def magnitude(c, sq, mag, bias):
+        def magnitude(c, sq, mag, bias, last_bias=one):
             square(c, sq)
             if c == 0:
                 root(mag[:, :, 0:E], sq[:, :, 0:E], bias)
                 root(mag[:, :, E:Q], sq[:, :, E:Q], one)
             else:
                 root(mag[:, 0:2, :], sq[:, 0:2, :], bias)
-                root(mag[:, 2:4, :], sq[:, 2:4, :], one)
+                root(mag[:, 2:4, :], sq[:, 2:4, :], last_bias)
             return mag
 
         def stiffen(mag, h_bf):
@@ -261,10 +262,11 @@ def tile_list_cloth_stretch_features_kernel(
 
         def finish_on_vector(c, y, res):
             lo, hi = CHUNKS[c]
+            tiles = res.shape[1]
             nc.vector.tensor_tensor(
-                out=res[:], in0=y[:], in1=b_col[:].unsqueeze(2).to_broadcast([P, TILES_N, E]), op=ALU.add
+                out=res[:], in0=y[:], in1=b_col[:, 0:tiles].unsqueeze(2).to_broadcast([P, tiles, E]), op=ALU.add
             )
-            nc.sync.dma_start(out=out_view[:, :, lo:hi], in_=res[:])
+            nc.sync.dma_start(out=out_view[:, 0:tiles, lo:hi], in_=res[:])
 
         gather_scales(0, sbuf([P, S], U8, "v1_sc"))
         w2_sc = sbuf([P, SLOTS, PASSES, P], U8, "w2_sc")
@@ -301,65 +303,64 @@ def tile_list_cloth_stretch_features_kernel(
                 op1=ALU.add,
             )
 
-        def stretch(c, steps, places, first=False):
+        def stretch(c, steps, places, first=False, last=True):
             lo, hi = CHUNKS[c]
             for n, (m, a) in enumerate(steps):
                 gather_words(m, a, lo, hi, places[:, n, :])
-                d_passes(m, a, c, first=(first and n == 0), last=(n == len(steps) - 1))
+                d_passes(m, a, c, first=(first and n == 0), last=(last and n == len(steps) - 1))
 
         second_half = ((2, 1), (1, 1), (0, 1))
         first_half = ((1, 0), (2, 0), (0, 0))
         late_at = (RAW[1] + 7168, RAW[1] + 4096)
         stretch(0, second_half, placed([P, 3, Q], U32, "late0", late_at[0]))
+        w4_q = sbuf([P, N], U32, "w4_q")
+        nc.vector.quantize_mx(out=w4_q[:].bitcast(FP8X4), scales=w4_sc[:], in_=w4_bf[:].rearrange("p n t -> p (n t)"))
         mag0 = magnitude(0, sbuf([P, SLOTS, Q], F32, "sq0"), placed([P, SLOTS, Q], F32, "mag0", MAG[0]), unit[0])
-        h0 = sbuf([P, Q, SLOTS], BF16, "h_bf0", "h_bf")
+        h0 = sbuf([P, Q, SLOTS], BF16, "h_bf0", "w1_bf1")
         stiffen_beside(mag0, h0, Q)
         stretch(1, second_half, placed([P, 3, Q], U32, "late1", late_at[1]))
         mag1 = magnitude(
             1, placed([P, SLOTS, Q], F32, "sq1", UNIT[0]), placed([P, SLOTS, Q], F32, "mag1", MAG[1]), unit[1]
         )
         open_banks(2, 0, 2)
-        stretch(2, second_half + first_half, placed([P, 6, Q], U32, "late2", late_at[0] + 2048), True)
+        stretch(2, second_half[:1], placed([P, 1, Q], U32, "late2a", late_at[0]), first=True, last=False)
+        stretch(2, second_half[1:] + first_half, placed([P, 5, Q], U32, "late2b", W4 - 1024))
         for c in (3, 4):
-            open_banks(c, 3 + c, 1)
+            open_banks(c, 4 * c - 10, 2)
 
-        def early_end(n, place):
-            m, a = first_half[n]
-            gather_words(m, a, 3 * Q, S, place[:])
-            for c in (3, 4):
-                d_passes(m, a, c, first=(n == 0))
-
-        for n in range(2):
-            early_end(n, placed([P, Q], U32, f"early_end{n}", late_at[1] + 1024 * n))
-        w4_q = placed([P, N], U32, "w4_q", MAG[0] - 1024)
-        nc.vector.quantize_mx(out=w4_q[:].bitcast(FP8X4), scales=w4_sc[:], in_=w4_bf[:].rearrange("p n t -> p (n t)"))
-        y0 = readout(w4_q, *quantize_h(h0, "h_q0", sbuf([P, Q], U32, "h_q0")), wide_targets(2))
-        h1 = sbuf([P, Q, SLOTS], BF16, "h_bf1", "h_bf")
-        stiffen_beside(mag1, h1, E)
+        gather_words(1, 0, 3 * Q, S, placed([P, Q], U32, "early_end", W4 + 4096)[:])
+        for c in (3, 4):
+            d_passes(1, 0, c, first=True)
+        stretch(3, second_half[:1], placed([P, 1, E], U32, "late3a", W4 + 5120), last=False)
+        y0 = readout(w4_q, *quantize_h(h0, "h_q0", sbuf([P, Q], U32, "h_q0")), wide_targets(4))
+        h1 = sbuf([P, Q, SLOTS], BF16, "h_bf1", "w1_bf1")
+        stiffen_beside(mag1, h1, Q)
         mag2 = magnitude(2, placed([P, SLOTS, Q], F32, "sq2", UNIT[1]), sbuf([P, SLOTS, Q], F32, "mag2"), one)
         finish_on_scalar(0, y0, sbuf([P, TILES_N, Q], F32, "res0"))
-        early_end(2, placed([P, Q], U32, "early_end2", MAG[0] + 512))
         mag_end = []
-        late_end = placed([P, 2, 3, E], U32, "late_end", MAG[0] + 2560)
+        late_end = placed([P, 2, 5, E], U32, "late_end", MAG[0])
         sq_end = [sbuf([P, SLOTS, E], F32, "sq3"), placed([P, SLOTS, E], F32, "sq4", LAST)]
         for c in (3, 4):
-            stretch(c, second_half, late_end[:, c - 3])
-            mag_end.append(sbuf([P, SLOTS, E], F32, f"mag{c}"))
-            root(mag_end[-1][:], square(c, sq_end[c - 3])[:], one if c == 3 else unit[2])
+            stretch(c, first_half[1:] + second_half[4 - c :], late_end[:, c - 3])
+            mag = sbuf([P, SLOTS, E], F32, f"mag{c}")
+            mag_end.append(magnitude(c, sq_end[c - 3], mag, one, one if c == 3 else unit[2]))
         h2 = sbuf([P, Q, SLOTS], BF16, "h_bf2")
         h_end = [sbuf([P, E, SLOTS], BF16, f"h_bf{c}") for c in (3, 4)]
-        stiffen(mag1[:, :, E:Q], h1[:, E:Q, :])
         stiffen(mag2[:], h2[:])
-        y1 = readout(w4_q, *quantize_h(h1, "h_q1", placed([P, Q], U32, "h_q1", UNIT[1])), wide_targets(4))
+        y1 = readout(w4_q, *quantize_h(h1, "h_q1", placed([P, Q], U32, "h_q1", UNIT[1])), wide_targets(2))
         stiffen(mag_end[0][:], h_end[0][:])
         y2 = readout(w4_q, *quantize_h(h2, "h_q2", sbuf([P, Q], U32, "h_q2", "sq3")), wide_targets(0))
         stiffen(mag_end[1][:], h_end[1][:])
-        y_end = []
-        for c, h_q in ((3, placed([P, E], U32, "h_q3", LAST)), (4, sbuf([P, E], U32, "h_q4"))):
-            y_end.append(psum.tile([P, TILES_N, E], F32, name=f"y{c}", tag=f"bank{3 + c}"))
-            readout(w4_q, *quantize_h(h_end[c - 3], f"h_q{c}", h_q), [y_end[-1][:, f, :] for f in range(TILES_N)])
+        y3 = psum.tile([P, TILES_N, E], F32, name="y3", tag="bank4")
+        readout(w4_q, *quantize_h(h_end[0], "h_q3", placed([P, E], U32, "h_q3", LAST)), [y3[:, f, :] for f in range(TILES_N)])
+        y4 = psum.tile([P, 2, E], F32, name="y4", tag="bank5")
+        y4_rest = psum.tile([P, E], F32, name="y4_rest", tag="bank6")
+        readout(w4_q, *quantize_h(h_end[1], "h_q4", sbuf([P, E], U32, "h_q4")), [y4[:, 0, :], y4[:, 1, :], y4_rest[:]])
         res = placed([P, 2, TILES_N, Q], F32, "res12", UNIT[2])
         finish_on_scalar(1, y1, res[:, 0])
         finish_on_scalar(2, y2, res[:, 1])
-        finish_on_vector(3, y_end[0], placed([P, TILES_N, E], F32, "res3", LAST + 512))
-        finish_on_vector(4, y_end[1], sbuf([P, TILES_N, E], F32, "res4"))
+        finish_on_vector(3, y3, placed([P, TILES_N, E], F32, "res3", LAST + 512))
+        finish_on_vector(4, y4, sbuf([P, 2, E], F32, "res4"))
+        res_rest = sbuf([P, E], F32, "res_rest")
+        nc.scalar.activation(out=res_rest[:], in_=y4_rest[:], func=ACT.Identity, bias=b_col[:, 2:3])
+        nc.scalar.dma_start(out=out_view[:, 2, S - E : S], in_=res_rest[:])

@@ -202,12 +202,19 @@ def tile_list_cloth_stretch_features_kernel(
 
         def magnitude(c, sq, mag, bias, last_bias=one):
             square(c, sq)
-            if c == 0:
-                root(mag[:, :, 0:E], sq[:, :, 0:E], bias)
-                root(mag[:, :, E:Q], sq[:, :, E:Q], one)
-            else:
-                root(mag[:, 0:2, :], sq[:, 0:2, :], bias)
-                root(mag[:, 2:4, :], sq[:, 2:4, :], last_bias)
+            root(mag[:, 0:2, :], sq[:, 0:2, :], bias)
+            root(mag[:, 2:4, :], sq[:, 2:4, :], last_bias)
+            return mag
+
+        def woven_magnitude(c, sq, mag, bias):
+            for u, bank in enumerate(banks[c]):
+                nc.scalar.activation(out=sq[:, u], in_=bank[:].rearrange("p i n -> p n i"), func=ACT.Square)
+            for lo, first_bias in ((0, bias), (E, one)):
+                root(
+                    mag[:, lo : lo + E, :].rearrange("p n (u i) -> p n u i", i=2),
+                    sq[:, :, lo : lo + E, :].rearrange("p u n i -> p n u i"),
+                    first_bias,
+                )
             return mag
 
         def stiffen(mag, h_bf):
@@ -223,7 +230,7 @@ def tile_list_cloth_stretch_features_kernel(
             for lo in range(0, width, E):
                 nc.gpsimd.tensor_tensor(
                     out=h_bf[:, lo : lo + E, :],
-                    in0=mag[:, :, lo : lo + E].rearrange("p t n -> p n t"),
+                    in0=mag[:, lo : lo + E, :],
                     in1=g_slots[:].unsqueeze(1).to_broadcast([P, E, SLOTS]),
                     op=ALU.mult,
                 )
@@ -274,21 +281,23 @@ def tile_list_cloth_stretch_features_kernel(
         cast_w1(0)
         cast_w1(1)
         w3_sc = sbuf([P, SLOTS, P], U8, "w3_sc")
-        w3_q = placed([P, SLOTS, PASSES, P], I32, "w3_q", RAW[1])
+        w3_q = placed([P, SLOTS, PASSES, P], I32, "w3_q", RAW[1] - 3072)
         nc.scalar.copy(
             out=w3_sc[:].bitcast(U16).rearrange("p t c -> p c t"),
             in_=w3_sc_raw[:].bitcast(U16).rearrange("p (c t) -> p c t", t=SLOTS),
         )
         reorder_columns(w3_q[:], w3_raw[:], U32, 2)
-        open_banks(0, 0, 4)
+        open_banks(0, 0, 2)
         open_banks(1, 4, 2)
         for m in (1, 0, 2):
-            if m == 1:
-                gather_words(m, 0, 0, 2 * Q, sbuf([P, 2 * Q], U32, "early1")[:])
-                gather_scales(2, sbuf([P, S], U8, "v3_sc"))
-                quantize_w1(0)
+            if m == 2:
+                gather_words(m, 0, 0, 2 * Q, placed([P, 2 * Q], U32, "early2", RAW[0])[:])
             else:
-                gather_words(m, 0, 0, 2 * Q, placed([P, 2 * Q], U32, f"early{m}", RAW[0] + 2048 * m)[:])
+                gather_words(m, 0, 0, 2 * Q, sbuf([P, 2 * Q], U32, f"early{m}")[:])
+            if m == 1:
+                gather_scales(2, sbuf([P, S], U8, "v3_sc"))
+            if m == 0:
+                quantize_w1(0)
             for c in range(2):
                 d_passes(m, 0, c, first=(m == 1))
         quantize_w1(1)
@@ -311,34 +320,35 @@ def tile_list_cloth_stretch_features_kernel(
 
         second_half = ((2, 1), (1, 1), (0, 1))
         first_half = ((1, 0), (2, 0), (0, 0))
-        late_at = (RAW[1] + 7168, RAW[1] + 4096)
+        late_at = (RAW[1] + 7168, RAW[1] + 1024)
         stretch(0, second_half, placed([P, 3, Q], U32, "late0", late_at[0]))
-        w4_q = sbuf([P, N], U32, "w4_q")
-        nc.vector.quantize_mx(out=w4_q[:].bitcast(FP8X4), scales=w4_sc[:], in_=w4_bf[:].rearrange("p n t -> p (n t)"))
-        mag0 = magnitude(0, sbuf([P, SLOTS, Q], F32, "sq0"), placed([P, SLOTS, Q], F32, "mag0", MAG[0]), unit[0])
-        h0 = sbuf([P, Q, SLOTS], BF16, "h_bf0", "w1_bf1")
+        mag0 = woven_magnitude(0, sbuf([P, 2, Q, 2], F32, "sq0"), placed([P, Q, SLOTS], F32, "mag0", MAG[0]), unit[0])
+        h0 = sbuf([P, Q, SLOTS], BF16, "h_bf0")
         stiffen_beside(mag0, h0, Q)
         stretch(1, second_half, placed([P, 3, Q], U32, "late1", late_at[1]))
-        mag1 = magnitude(
-            1, placed([P, SLOTS, Q], F32, "sq1", UNIT[0]), placed([P, SLOTS, Q], F32, "mag1", MAG[1]), unit[1]
+        mag1 = woven_magnitude(
+            1, placed([P, 2, Q, 2], F32, "sq1", UNIT[0]), placed([P, Q, SLOTS], F32, "mag1", MAG[1]), unit[1]
         )
         open_banks(2, 0, 2)
-        stretch(2, second_half[:1], placed([P, 1, Q], U32, "late2a", late_at[0]), first=True, last=False)
-        stretch(2, second_half[1:] + first_half, placed([P, 5, Q], U32, "late2b", W4 - 1024))
+        stretch(2, second_half[:2], placed([P, 2, Q], U32, "late2a", late_at[0]), first=True, last=False)
+        stretch(2, second_half[2:] + first_half, placed([P, 4, Q], U32, "late2b", late_at[1]))
         for c in (3, 4):
             open_banks(c, 4 * c - 10, 2)
 
-        gather_words(1, 0, 3 * Q, S, placed([P, Q], U32, "early_end", W4 + 4096)[:])
+        gather_words(1, 0, 3 * Q, S, placed([P, Q], U32, "early_end", late_at[0])[:])
         for c in (3, 4):
             d_passes(1, 0, c, first=True)
-        stretch(3, second_half[:1], placed([P, 1, E], U32, "late3a", W4 + 5120), last=False)
-        y0 = readout(w4_q, *quantize_h(h0, "h_q0", sbuf([P, Q], U32, "h_q0")), wide_targets(4))
+        stretch(3, second_half[:1], placed([P, 1, E], U32, "late3a", late_at[0] + 1024), last=False)
+        h0_q = quantize_h(h0, "h_q0", sbuf([P, Q], U32, "h_q0"))
+        w4_q = placed([P, N], U32, "w4_q", MAG[0] - 1024)
+        nc.vector.quantize_mx(out=w4_q[:].bitcast(FP8X4), scales=w4_sc[:], in_=w4_bf[:].rearrange("p n t -> p (n t)"))
+        y0 = readout(w4_q, *h0_q, wide_targets(4))
         h1 = sbuf([P, Q, SLOTS], BF16, "h_bf1", "w1_bf1")
         stiffen_beside(mag1, h1, Q)
         mag2 = magnitude(2, placed([P, SLOTS, Q], F32, "sq2", UNIT[1]), sbuf([P, SLOTS, Q], F32, "mag2"), one)
         finish_on_scalar(0, y0, sbuf([P, TILES_N, Q], F32, "res0"))
         mag_end = []
-        late_end = placed([P, 2, 5, E], U32, "late_end", MAG[0])
+        late_end = placed([P, 2, 5, E], U32, "late_end", MAG[0] + 512)
         sq_end = [sbuf([P, SLOTS, E], F32, "sq3"), placed([P, SLOTS, E], F32, "sq4", LAST)]
         for c in (3, 4):
             stretch(c, first_half[1:] + second_half[4 - c :], late_end[:, c - 3])

@@ -22,6 +22,8 @@ SLOTS = 4
 TILES_N = 3
 Q = 256
 E = 128
+EARLY = 2
+SIDE = 64
 CHUNKS = ((0, 256), (256, 512), (512, 768), (768, 896), (896, 1024))
 RAW = (0, 8192)
 MAG = (25600, 31744)
@@ -146,8 +148,11 @@ def tile_list_cloth_stretch_features_kernel(
             plane, sc_cols = columns(planes[m], lo, hi)
             count = len(banks[c])
             share = SLOTS // count
-            for place in range(share):
-                for u in range(count):
+            order = [(place, u) for place in range(share) for u in range(count)]
+            if last:
+                order.sort(key=lambda pair: pair[1])
+            for place, u in order:
+                if True:
                     t = share * u + place
                     if m == 0:
                         lhs, lhs_sc = w1_q[a][:, P * t : P * (t + 1)].bitcast(FP8X4), w1_sc[a][:, P * t : P * (t + 1)]
@@ -206,9 +211,14 @@ def tile_list_cloth_stretch_features_kernel(
             root(mag[:, 2:4, :], sq[:, 2:4, :], last_bias)
             return mag
 
-        def woven_magnitude(c, sq, mag, bias):
-            for u, bank in enumerate(banks[c]):
-                nc.scalar.activation(out=sq[:, u], in_=bank[:].rearrange("p i n -> p n i"), func=ACT.Square)
+        def woven_magnitude(c, sq, mag, bias, piece=Q):
+            for lo in range(0, Q, piece):
+                for u, bank in enumerate(banks[c]):
+                    nc.scalar.activation(
+                        out=sq[:, u, lo : lo + piece, :],
+                        in_=bank[:, :, lo : lo + piece].rearrange("p i n -> p n i"),
+                        func=ACT.Square,
+                    )
             for lo, first_bias in ((0, bias), (E, one)):
                 root(
                     mag[:, lo : lo + E, :].rearrange("p n (u i) -> p n u i", i=2),
@@ -228,10 +238,11 @@ def tile_list_cloth_stretch_features_kernel(
 
         def stiffen_beside(mag, h_bf, width):
             for lo in range(0, width, E):
+                hi = min(width, lo + E)
                 nc.gpsimd.tensor_tensor(
-                    out=h_bf[:, lo : lo + E, :],
-                    in0=mag[:, lo : lo + E, :],
-                    in1=g_slots[:].unsqueeze(1).to_broadcast([P, E, SLOTS]),
+                    out=h_bf[:, lo:hi, :],
+                    in0=mag[:, lo:hi, :],
+                    in1=g_slots[:].unsqueeze(1).to_broadcast([P, hi - lo, SLOTS]),
                     op=ALU.mult,
                 )
 
@@ -261,9 +272,9 @@ def tile_list_cloth_stretch_features_kernel(
             y_b = psum.tile([P, Q], F32, name="y_b", tag=f"bank{first_bank + 1}")
             return [y_a[:, 0, :], y_a[:, 1, :], y_b[:]]
 
-        def finish_on_scalar(c, ys, res):
+        def finish_on_scalar(c, ys, res, tiles=range(TILES_N)):
             lo, hi = CHUNKS[c]
-            for f in range(TILES_N):
+            for f in tiles:
                 nc.scalar.activation(out=res[:, f, :], in_=ys[f], func=ACT.Identity, bias=b_col[:, f : f + 1])
                 nc.sync.dma_start(out=out_view[:, f, lo:hi], in_=res[:, f, :])
 
@@ -286,7 +297,8 @@ def tile_list_cloth_stretch_features_kernel(
             out=w3_sc[:].bitcast(U16).rearrange("p t c -> p c t"),
             in_=w3_sc_raw[:].bitcast(U16).rearrange("p (c t) -> p c t", t=SLOTS),
         )
-        reorder_columns(w3_q[:], w3_raw[:], U32, 2)
+        for a in range(PASSES):
+            reorder_columns(w3_q[:, :, a : a + 1, :], w3_raw[:, a : a + 1, :], U32, 2)
         open_banks(0, 0, 2)
         open_banks(1, 4, 2)
         for m in (1, 0, 2):
@@ -298,7 +310,7 @@ def tile_list_cloth_stretch_features_kernel(
                 gather_scales(2, sbuf([P, S], U8, "v3_sc"))
             if m == 0:
                 quantize_w1(0)
-            for c in range(2):
+            for c in range(1 if m == 2 else 2):
                 d_passes(m, 0, c, first=(m == 1))
         quantize_w1(1)
         w4_bf = sbuf([P, N, SLOTS], BF16, "w4_bf", "w1_bf1")
@@ -322,9 +334,10 @@ def tile_list_cloth_stretch_features_kernel(
         first_half = ((1, 0), (2, 0), (0, 0))
         late_at = (RAW[1] + 7168, RAW[1] + 1024)
         stretch(0, second_half, placed([P, 3, Q], U32, "late0", late_at[0]))
-        mag0 = woven_magnitude(0, sbuf([P, 2, Q, 2], F32, "sq0"), placed([P, Q, SLOTS], F32, "mag0", MAG[0]), unit[0])
+        mag0 = woven_magnitude(0, sbuf([P, 2, Q, 2], F32, "sq0"), placed([P, Q, SLOTS], F32, "mag0", MAG[0]), unit[0], E)
         h0 = sbuf([P, Q, SLOTS], BF16, "h_bf0")
         stiffen_beside(mag0, h0, Q)
+        d_passes(2, 0, 1)
         stretch(1, second_half, placed([P, 3, Q], U32, "late1", late_at[1]))
         mag1 = woven_magnitude(
             1, placed([P, 2, Q, 2], F32, "sq1", UNIT[0]), placed([P, Q, SLOTS], F32, "mag1", MAG[1]), unit[1]
@@ -335,39 +348,47 @@ def tile_list_cloth_stretch_features_kernel(
         for c in (3, 4):
             open_banks(c, 4 * c - 10, 2)
 
-        gather_words(1, 0, 3 * Q, S, placed([P, Q], U32, "early_end", late_at[0])[:])
-        for c in (3, 4):
-            d_passes(1, 0, c, first=True)
-        stretch(3, second_half[:1], placed([P, 1, E], U32, "late3a", late_at[0] + 1024), last=False)
         h0_q = quantize_h(h0, "h_q0", sbuf([P, Q], U32, "h_q0"))
         w4_q = placed([P, N], U32, "w4_q", MAG[0] - 1024)
         nc.vector.quantize_mx(out=w4_q[:].bitcast(FP8X4), scales=w4_sc[:], in_=w4_bf[:].rearrange("p n t -> p (n t)"))
         y0 = readout(w4_q, *h0_q, wide_targets(4))
         h1 = sbuf([P, Q, SLOTS], BF16, "h_bf1", "w1_bf1")
         stiffen_beside(mag1, h1, Q)
-        mag2 = magnitude(2, placed([P, SLOTS, Q], F32, "sq2", UNIT[1]), sbuf([P, SLOTS, Q], F32, "mag2"), one)
+        mag2 = woven_magnitude(2, placed([P, 2, Q, 2], F32, "sq2", UNIT[1]), sbuf([P, Q, SLOTS], F32, "mag2"), one)
         finish_on_scalar(0, y0, sbuf([P, TILES_N, Q], F32, "res0"))
-        mag_end = []
-        late_end = placed([P, 2, 5, E], U32, "late_end", MAG[0] + 512)
-        sq_end = [sbuf([P, SLOTS, E], F32, "sq3"), placed([P, SLOTS, E], F32, "sq4", LAST)]
+        gather_words(1, 0, 3 * Q, S, placed([P, Q], U32, "early_end", MAG[0] + 512)[:])
         for c in (3, 4):
-            stretch(c, first_half[1:] + second_half[4 - c :], late_end[:, c - 3])
-            mag = sbuf([P, SLOTS, E], F32, f"mag{c}")
-            mag_end.append(magnitude(c, sq_end[c - 3], mag, one, one if c == 3 else unit[2]))
-        h2 = sbuf([P, Q, SLOTS], BF16, "h_bf2")
-        h_end = [sbuf([P, E, SLOTS], BF16, f"h_bf{c}") for c in (3, 4)]
-        stiffen(mag2[:], h2[:])
-        y1 = readout(w4_q, *quantize_h(h1, "h_q1", placed([P, Q], U32, "h_q1", UNIT[1])), wide_targets(2))
+            d_passes(1, 0, c, first=True)
+        late_end = placed([P, 7, E], U32, "late_end", MAG[0] + 1536)
+        steps = first_half[1:] + second_half
+        stretch(3, steps, late_end[:, 0:5])
+        mag_end = [magnitude(3, sbuf([P, SLOTS, E], F32, "sq3"), sbuf([P, SLOTS, E], F32, "mag3"), one)]
+        stretch(4, steps[:2], late_end[:, 5:7], last=False)
+        y1 = readout(w4_q, *quantize_h(h1, "h_q1", sbuf([P, Q], U32, "h_q1")), wide_targets(0))
+        h2 = sbuf([P, Q, SLOTS], BF16, "h_bf2", "w1_bf1")
+        stiffen_beside(mag2, h2, SIDE)
+        stretch(4, steps[2:], placed([P, 3, E], U32, "late4", MAG[1]))
+        finish_on_scalar(1, y1, sbuf([P, EARLY, Q], F32, "res1"), range(EARLY))
+        mag_end.append(
+            magnitude(4, placed([P, SLOTS, E], F32, "sq4", LAST), sbuf([P, SLOTS, E], F32, "mag4"), one, unit[2])
+        )
+        h_end = [placed([P, E, SLOTS], BF16, "h_bf3", MAG[1] + 3072), sbuf([P, E, SLOTS], BF16, "h_bf4")]
+        nc.vector.tensor_tensor(
+            out=h2[:, SIDE:Q, :],
+            in0=mag2[:, SIDE:Q, :],
+            in1=g_slots[:].unsqueeze(1).to_broadcast([P, Q - SIDE, SLOTS]),
+            op=ALU.mult,
+        )
         stiffen(mag_end[0][:], h_end[0][:])
-        y2 = readout(w4_q, *quantize_h(h2, "h_q2", sbuf([P, Q], U32, "h_q2", "sq3")), wide_targets(0))
-        stiffen(mag_end[1][:], h_end[1][:])
+        y2 = readout(w4_q, *quantize_h(h2, "h_q2", sbuf([P, Q], U32, "h_q2", "sq3")), wide_targets(2))
         y3 = psum.tile([P, TILES_N, E], F32, name="y3", tag="bank4")
-        readout(w4_q, *quantize_h(h_end[0], "h_q3", placed([P, E], U32, "h_q3", LAST)), [y3[:, f, :] for f in range(TILES_N)])
+        readout(w4_q, *quantize_h(h_end[0], "h_q3", sbuf([P, E], U32, "h_q3")), [y3[:, f, :] for f in range(TILES_N)])
+        stiffen(mag_end[1][:], h_end[1][:])
         y4 = psum.tile([P, 2, E], F32, name="y4", tag="bank5")
         y4_rest = psum.tile([P, E], F32, name="y4_rest", tag="bank6")
         readout(w4_q, *quantize_h(h_end[1], "h_q4", sbuf([P, E], U32, "h_q4")), [y4[:, 0, :], y4[:, 1, :], y4_rest[:]])
         res = placed([P, 2, TILES_N, Q], F32, "res12", UNIT[2])
-        finish_on_scalar(1, y1, res[:, 0])
+        finish_on_scalar(1, y1, res[:, 0], range(EARLY, TILES_N))
         finish_on_scalar(2, y2, res[:, 1])
         finish_on_vector(3, y3, placed([P, TILES_N, E], F32, "res3", LAST + 512))
         finish_on_vector(4, y4, sbuf([P, 2, E], F32, "res4"))

@@ -22,8 +22,7 @@ SLOTS = 4
 TILES_N = 3
 Q = 256
 E = 128
-EARLY = 2
-SIDE = 64
+SIDE = 96
 CHUNKS = ((0, 256), (256, 512), (512, 768), (768, 896), (896, 1024))
 RAW = (0, 8192)
 MAG = (25600, 31744)
@@ -211,19 +210,17 @@ def tile_list_cloth_stretch_features_kernel(
             root(mag[:, 2:4, :], sq[:, 2:4, :], last_bias)
             return mag
 
-        def woven_magnitude(c, sq, mag, bias, piece=Q):
-            for lo in range(0, Q, piece):
+        def woven_magnitude(c, sq, mag, bias, cut=E, squares=((0, Q),)):
+            for lo, hi in squares:
                 for u, bank in enumerate(banks[c]):
                     nc.scalar.activation(
-                        out=sq[:, u, lo : lo + piece, :],
-                        in_=bank[:, :, lo : lo + piece].rearrange("p i n -> p n i"),
-                        func=ACT.Square,
+                        out=sq[:, u, lo:hi, :], in_=bank[:, :, lo:hi].rearrange("p i n -> p n i"), func=ACT.Square
                     )
-            for lo, first_bias in ((0, bias), (E, one)):
+            for lo, hi, which in ((0, cut, bias), (cut, Q, one)):
                 root(
-                    mag[:, lo : lo + E, :].rearrange("p n (u i) -> p n u i", i=2),
-                    sq[:, :, lo : lo + E, :].rearrange("p u n i -> p n u i"),
-                    first_bias,
+                    mag[:, lo:hi, :].rearrange("p n (u i) -> p n u i", i=2),
+                    sq[:, :, lo:hi, :].rearrange("p u n i -> p n u i"),
+                    which,
                 )
             return mag
 
@@ -236,9 +233,8 @@ def tile_list_cloth_stretch_features_kernel(
                 op=ALU.mult,
             )
 
-        def stiffen_beside(mag, h_bf, width):
-            for lo in range(0, width, E):
-                hi = min(width, lo + E)
+        def stiffen_beside(mag, h_bf, pieces):
+            for lo, hi in pieces:
                 nc.gpsimd.tensor_tensor(
                     out=h_bf[:, lo:hi, :],
                     in0=mag[:, lo:hi, :],
@@ -334,9 +330,12 @@ def tile_list_cloth_stretch_features_kernel(
         first_half = ((1, 0), (2, 0), (0, 0))
         late_at = (RAW[1] + 7168, RAW[1] + 1024)
         stretch(0, second_half, placed([P, 3, Q], U32, "late0", late_at[0]))
-        mag0 = woven_magnitude(0, sbuf([P, 2, Q, 2], F32, "sq0"), placed([P, Q, SLOTS], F32, "mag0", MAG[0]), unit[0], E)
+        lead = ((0, SIDE), (SIDE, Q))
+        mag0 = woven_magnitude(
+            0, sbuf([P, 2, Q, 2], F32, "sq0"), placed([P, Q, SLOTS], F32, "mag0", MAG[0]), unit[0], SIDE, lead
+        )
         h0 = sbuf([P, Q, SLOTS], BF16, "h_bf0")
-        stiffen_beside(mag0, h0, Q)
+        stiffen_beside(mag0, h0, lead)
         d_passes(2, 0, 1)
         stretch(1, second_half, placed([P, 3, Q], U32, "late1", late_at[1]))
         mag1 = woven_magnitude(
@@ -353,44 +352,55 @@ def tile_list_cloth_stretch_features_kernel(
         nc.vector.quantize_mx(out=w4_q[:].bitcast(FP8X4), scales=w4_sc[:], in_=w4_bf[:].rearrange("p n t -> p (n t)"))
         y0 = readout(w4_q, *h0_q, wide_targets(4))
         h1 = sbuf([P, Q, SLOTS], BF16, "h_bf1", "w1_bf1")
-        stiffen_beside(mag1, h1, Q)
+        stiffen_beside(mag1, h1, ((0, Q),))
         mag2 = woven_magnitude(2, placed([P, 2, Q, 2], F32, "sq2", UNIT[1]), sbuf([P, Q, SLOTS], F32, "mag2"), one)
         finish_on_scalar(0, y0, sbuf([P, TILES_N, Q], F32, "res0"))
         gather_words(1, 0, 3 * Q, S, placed([P, Q], U32, "early_end", MAG[0] + 512)[:])
         for c in (3, 4):
             d_passes(1, 0, c, first=True)
-        late_end = placed([P, 7, E], U32, "late_end", MAG[0] + 1536)
+        late_end = placed([P, 6, E], U32, "late_end", MAG[0] + 1536)
         steps = first_half[1:] + second_half
         stretch(3, steps, late_end[:, 0:5])
         mag_end = [magnitude(3, sbuf([P, SLOTS, E], F32, "sq3"), sbuf([P, SLOTS, E], F32, "mag3"), one)]
-        stretch(4, steps[:2], late_end[:, 5:7], last=False)
+        stretch(4, steps[:1], late_end[:, 5:6], last=False)
         y1 = readout(w4_q, *quantize_h(h1, "h_q1", sbuf([P, Q], U32, "h_q1")), wide_targets(0))
         h2 = sbuf([P, Q, SLOTS], BF16, "h_bf2", "w1_bf1")
-        stiffen_beside(mag2, h2, SIDE)
-        stretch(4, steps[2:], placed([P, 3, E], U32, "late4", MAG[1]))
-        finish_on_scalar(1, y1, sbuf([P, EARLY, Q], F32, "res1"), range(EARLY))
-        mag_end.append(
-            magnitude(4, placed([P, SLOTS, E], F32, "sq4", LAST), sbuf([P, SLOTS, E], F32, "mag4"), one, unit[2])
-        )
-        h_end = [placed([P, E, SLOTS], BF16, "h_bf3", MAG[1] + 3072), sbuf([P, E, SLOTS], BF16, "h_bf4")]
+        stiffen_beside(mag2, h2, lead[:1])
+        stretch(4, steps[1:], placed([P, 4, E], U32, "late4", MAG[1]))
+        finish_on_scalar(1, y1, sbuf([P, TILES_N, Q], F32, "res1"))
+        halves = (slice(0, E // 2), slice(E // 2, E))
+        sq4 = sbuf([P, SLOTS, E], F32, "sq4")
+        for half in halves:
+            for u, bank in enumerate(banks[4]):
+                nc.scalar.activation(out=sq4[:, 2 * u : 2 * u + 2, half], in_=bank[:, :, half], func=ACT.Square)
+        mag4 = [placed([P, SLOTS, E // 2], F32, f"mag4{u}", LAST + 1024 * u) for u in range(2)]
+        for u, bias in enumerate((one, unit[2])):
+            root(mag4[u][:], sq4[:, :, halves[u]], bias)
+        h3 = placed([P, E, SLOTS], BF16, "h_bf3", MAG[1] + 3072)
+        h4 = sbuf([P, E, SLOTS], BF16, "h_bf4")
         nc.vector.tensor_tensor(
             out=h2[:, SIDE:Q, :],
             in0=mag2[:, SIDE:Q, :],
             in1=g_slots[:].unsqueeze(1).to_broadcast([P, Q - SIDE, SLOTS]),
             op=ALU.mult,
         )
-        stiffen(mag_end[0][:], h_end[0][:])
+        stiffen(mag_end[0][:], h3[:])
         y2 = readout(w4_q, *quantize_h(h2, "h_q2", sbuf([P, Q], U32, "h_q2", "sq3")), wide_targets(2))
         y3 = psum.tile([P, TILES_N, E], F32, name="y3", tag="bank4")
-        readout(w4_q, *quantize_h(h_end[0], "h_q3", sbuf([P, E], U32, "h_q3")), [y3[:, f, :] for f in range(TILES_N)])
-        stiffen(mag_end[1][:], h_end[1][:])
+        readout(w4_q, *quantize_h(h3, "h_q3", sbuf([P, E], U32, "h_q3")), [y3[:, f, :] for f in range(TILES_N)])
+        for u, half in enumerate(halves):
+            stiffen(mag4[u][:], h4[:, half, :])
         y4 = psum.tile([P, 2, E], F32, name="y4", tag="bank5")
         y4_rest = psum.tile([P, E], F32, name="y4_rest", tag="bank6")
-        readout(w4_q, *quantize_h(h_end[1], "h_q4", sbuf([P, E], U32, "h_q4")), [y4[:, 0, :], y4[:, 1, :], y4_rest[:]])
-        res = placed([P, 2, TILES_N, Q], F32, "res12", UNIT[2])
-        finish_on_scalar(1, y1, res[:, 0], range(EARLY, TILES_N))
-        finish_on_scalar(2, y2, res[:, 1])
-        finish_on_vector(3, y3, placed([P, TILES_N, E], F32, "res3", LAST + 512))
+        h4_q = placed([P, E], U32, "h_q4", LAST + 1024)
+        h4_sc = sbuf([P, E], U8, "h_q4_sc")
+        for half in halves:
+            nc.vector.quantize_mx(
+                out=h4_q[:, half].bitcast(FP8X4), scales=h4_sc[:, half], in_=h4[:, half, :].rearrange("p n t -> p (n t)")
+            )
+        readout(w4_q, h4_q, h4_sc, [y4[:, 0, :], y4[:, 1, :], y4_rest[:]])
+        finish_on_scalar(2, y2, placed([P, TILES_N, Q], F32, "res2", UNIT[2]))
+        finish_on_vector(3, y3, sbuf([P, TILES_N, E], F32, "res3", "h_bf4"))
         finish_on_vector(4, y4, sbuf([P, 2, E], F32, "res4"))
         res_rest = sbuf([P, E], F32, "res_rest")
         nc.scalar.activation(out=res_rest[:], in_=y4_rest[:], func=ACT.Identity, bias=b_col[:, 2:3])

from contextlib import ExitStack

import concourse.mybir as mybir

K, H, N, T, S = 1024, 512, 384, 2048, 1024
FLOPS = 2 * (3 * K * H * S + H * N * S)

F32 = mybir.dt.float32
BF16 = mybir.dt.bfloat16
I32 = mybir.dt.int32
U32 = mybir.dt.uint32
U16 = mybir.dt.uint16
U8 = mybir.dt.uint8
FP8X4 = mybir.dt.float8_e4m3fn_x4
FP4X4 = mybir.dt.float4_e2m1fn_x4
ACT = mybir.ActivationFunctionType
ALU = mybir.AluOpType

P = 128
PASSES = 2
SLOTS = 4
TILES_N = 3
Q = 256
E = 128
SIDE = 96
CHUNKS = ((0, 256), (256, 512), (512, 768), (768, 896), (896, 1024))
RAW = (0, 8192)
MAG = (25600, 31744)
LAST = 51200
W4 = 57344
UNIT = (36864, 40960, 45056)


def tile_list_cloth_stretch_features_kernel(
    tc, tab_words, tab_scales, offs, offs2, offs3, w1, w2_words, w2_scales, w3_words, w3_scales, g, w4, b, out
):
    nc = tc.nc
    with ExitStack() as ctx:
        keep = ctx.enter_context(tc.tile_pool(name="keep", bufs=1))
        shared = ctx.enter_context(tc.tile_pool(name="shared", bufs=1))
        psum = ctx.enter_context(tc.psum_pool(name="psum", bufs=1))

        def sbuf(shape, dtype, name, tag=None):
            return keep.tile(shape, dtype, name=name, tag=tag or name, align_bytes=64)

        def placed(shape, dtype, name, offset):
            return shared.tile(shape, dtype, name=name, align_bytes=64, offset=offset)

        lists = [keep.tile([P, S // 16], U16, name=f"list{m}") for m in range(3)]
        table = [sbuf([P, T], I32, f"table{a}") for a in range(PASSES)]
        table_sc = sbuf([P, T], U8, "table_sc")
        w3_sc_raw = sbuf([P, H], U8, "w3_sc_raw")
        w2_sc_raw = sbuf([P, PASSES, H], U8, "w2_sc_raw")
        w3_raw = sbuf([P, PASSES, H], I32, "w3_raw")
        w2_raw = sbuf([P, PASSES, H // 2], I32, "w2_raw")
        w2_q = sbuf([P, SLOTS, PASSES, 2 * P], U8, "w2_q")
        w1_raw = [placed([P, 4, H], F32, f"w1_raw{a}", RAW[a]) for a in range(PASSES)]
        w1_bf = [sbuf([P, SLOTS, 4 * P], BF16, f"w1_bf{a}") for a in range(PASSES)]
        w1_q = [sbuf([P, H], U32, f"w1_q{a}") for a in range(PASSES)]
        w1_sc = [sbuf([P, H], U8, f"w1_sc{a}") for a in range(PASSES)]
        w4_raw = placed([P, SLOTS, N], F32, "w4_raw", W4)
        w4_sc = sbuf([P, N], U8, "w4_sc")
        g_slots = sbuf([P, SLOTS], F32, "g_slots")
        b_col = sbuf([P, TILES_N], F32, "b_col")
        unit = [placed([P, 1], F32, f"unit{u}", UNIT[u]) for u in range(3)]
        one = sbuf([P, 1], F32, "one")
        v2_sc = sbuf([P, S], U8, "v2_sc")
        planes = {m: [] for m in range(3)}
        v2_sc_pass1 = sbuf([P, S], U8, "v2_sc_pass1")

        nc.gpsimd.memset(table_sc[:].bitcast(I32), 0)
        nc.gpsimd.memset(unit[0][:], 1.0)
        nc.gpsimd.memset(w2_sc_raw[:].rearrange("p a c -> p (a c)").bitcast(I32), 0)
        nc.gpsimd.memset(w3_sc_raw[:].bitcast(I32), 0)
        nc.gpsimd.memset(v2_sc_pass1[:].bitcast(I32), 0)
        for u in range(1, 3):
            nc.gpsimd.memset(unit[u][:], 1.0)
        nc.scalar.activation(out=one[:], in_=unit[0][:], func=ACT.Sqrt)

        def load_table(a):
            nc.sync.dma_start(out=table[a][:], in_=tab_words[a].rearrange("p t i -> p (t i)").bitcast(I32))

        def load_w1(a):
            nc.sync.dma_start(out=w1_raw[a][:], in_=w1[512 * a : 512 * (a + 1), :].rearrange("(p j) r -> p j r", j=4))

        def gather_scales(m, dst, lo=0, hi=S):
            planes[m].append((lo, hi, dst))
            nc.vector.tensor_copy(out=dst[:], in_=table_sc[:].indirect(lists[m][:, lo // 16 : hi // 16]))

        nc.sync.dma_start(out=w2_raw[:], in_=w2_words.rearrange("a p c -> p a c").bitcast(I32))
        nc.sync.dma_start(lists[1][:], offs2)
        for q in range(4):
            nc.sync.dma_start(
                out=table_sc[32 * q : 32 * q + 8, :].bitcast(I32),
                in_=tab_scales[:, 4 * q : 4 * q + 4, :].bitcast(I32),
            )
        nc.vector.tensor_copy(
            out=w2_q[:].bitcast(I32).rearrange("p t a c -> p (a c) t"),
            in_=w2_raw[:].rearrange("p a (c t) -> p (a c) t", t=SLOTS),
        )
        gather_scales(1, v2_sc)
        nc.sync.dma_start(lists[0][:], offs)
        load_table(0)
        for r in range(4):
            nc.sync.dma_start(
                out=w2_sc_raw[r:P:32, :, :].bitcast(I32),
                in_=w2_scales.rearrange("a (q r) c -> r q a c", r=4)[r].bitcast(I32),
            )
        nc.sync.dma_start(lists[2][:], offs3)
        load_w1(0)
        load_w1(1)
        nc.sync.dma_start(out=v2_sc_pass1[0:100, :].bitcast(I32), in_=v2_sc[4:104, :].bitcast(I32))
        for q in range(4):
            nc.sync.dma_start(
                out=w3_sc_raw[32 * q : 32 * q + 8, :].bitcast(I32),
                in_=w3_scales[:, 4 * q : 4 * q + 4, :].bitcast(I32),
            )
        nc.sync.dma_start(out=w3_raw[:], in_=w3_words.rearrange("a p c i -> p a (c i)").bitcast(I32))
        load_table(1)
        for i in range(2):
            nc.sync.dma_start(out=w4_raw[i:P:2, :, :], in_=w4.rearrange("(c t i) n -> i c t n", t=SLOTS, i=2)[i])
        with nc.allow_non_contiguous_dma(reason="one value a partition"):
            for i in range(2):
                nc.sync.dma_start(out=g_slots[i:P:2, :], in_=g.rearrange("(c t i) -> i c t", t=SLOTS, i=2)[i])
            nc.sync.dma_start(out=b_col[:], in_=b.rearrange("(c p) -> p c", p=P))

        words = {(m, a): [] for m in range(3) for a in range(PASSES)}
        banks = {}

        def gather_words(m, a, lo, hi, dst):
            words[m, a].append((lo, hi, dst))
            nc.vector.tensor_copy(out=dst, in_=table[a][:].bitcast(U32).indirect(lists[m][:, lo // 16 : hi // 16]))

        def columns(pieces, lo, hi):
            return [(dst, slice(lo - begin, hi - begin)) for begin, end, dst in pieces if begin <= lo and hi <= end][0]

        def open_banks(c, first_bank, count):
            lo, hi = CHUNKS[c]
            banks[c] = [
                psum.tile([P, SLOTS // count, hi - lo], F32, name=f"d{c}{u}", tag=f"bank{first_bank + u}")
                for u in range(count)
            ]

        def d_passes(m, a, c, first=False, last=False):
            lo, hi = CHUNKS[c]
            rhs, cols = columns(words[m, a], lo, hi)
            plane, sc_cols = columns(planes[m], lo, hi)
            count = len(banks[c])
            share = SLOTS // count
            order = [(place, u) for place in range(share) for u in range(count)]
            if last:
                order.sort(key=lambda pair: pair[1])
            for place, u in order:
                if True:
                    t = share * u + place
                    if m == 0:
                        lhs, lhs_sc = w1_q[a][:, P * t : P * (t + 1)].bitcast(FP8X4), w1_sc[a][:, P * t : P * (t + 1)]
                        rhs_sc = plane[4 * a : P, sc_cols]
                    elif m == 1:
                        lhs, lhs_sc = w2_q[:, t, a, :].bitcast(FP4X4), w2_sc[:, t, a, :]
                        rhs_sc = (plane, v2_sc_pass1)[a][:, sc_cols]
                    else:
                        lhs, lhs_sc = w3_q[:, t, a, :].bitcast(FP8X4), w3_sc[4 * a : P, t, :]
                        rhs_sc = plane[4 * a : P, sc_cols]
                    nc.tensor.matmul_mx(
                        out=banks[c][u][:, place, :],
                        lhsT=lhs,
                        lhsT_scale=lhs_sc,
                        rhs=rhs[:, cols].bitcast(FP8X4),
                        rhs_scale=rhs_sc,
                        start=first and place == 0,
                        stop=last and place == share - 1,
                    )

        def by_fours_in(planar):
            return planar.rearrange("p t (c i) -> p c t i", i=4)

        def by_fours_out(woven):
            return woven.rearrange("p (c i) t -> p c t i", i=4)

        def cast_w1(a):
            nc.scalar.copy(
                out=w1_bf[a][:].rearrange("p t (c i j) -> p t c j i", i=2, j=4),
                in_=w1_raw[a][:].rearrange("p j (c t i) -> p t c j i", t=SLOTS, i=2),
            )

        def quantize_w1(a):
            nc.vector.quantize_mx(
                out=w1_q[a][:].bitcast(FP8X4), scales=w1_sc[a][:], in_=w1_bf[a][:].rearrange("p t c -> p (t c)")
            )

        def reorder_columns(dst, src, dtype, run):
            nc.scalar.copy(
                out=dst.bitcast(dtype).rearrange("p t a (c i) -> p (a c) t i", i=run),
                in_=src.bitcast(dtype).rearrange("p a (c t i) -> p (a c) t i", t=SLOTS, i=run),
            )

        def square(c, sq):
            share = SLOTS // len(banks[c])
            for u, bank in enumerate(banks[c]):
                nc.scalar.activation(out=sq[:, share * u : share * (u + 1), :], in_=bank[:], func=ACT.Square)
            return sq

        def root(mag, sq, bias):
            nc.scalar.activation(out=mag, in_=sq, func=ACT.Sqrt, bias=bias[:])

        def magnitude(c, sq, mag, bias, last_bias=one):
            square(c, sq)
            root(mag[:, 0:2, :], sq[:, 0:2, :], bias)
            root(mag[:, 2:4, :], sq[:, 2:4, :], last_bias)
            return mag

        def woven_magnitude(c, sq, mag, bias, cut=E, squares=((0, Q),)):
            for lo, hi in squares:
                for u, bank in enumerate(banks[c]):
                    nc.scalar.activation(
                        out=sq[:, u, lo:hi, :], in_=bank[:, :, lo:hi].rearrange("p i n -> p n i"), func=ACT.Square
                    )
            for lo, hi, which in ((0, cut, bias), (cut, Q, one)):
                root(
                    mag[:, lo:hi, :].rearrange("p n (u i) -> p n u i", i=2),
                    sq[:, :, lo:hi, :].rearrange("p u n i -> p n u i"),
                    which,
                )
            return mag

        def stiffen(mag, h_bf):
            width = h_bf.shape[1]
            nc.vector.tensor_tensor(
                out=by_fours_out(h_bf),
                in0=by_fours_in(mag),
                in1=g_slots[:].unsqueeze(1).unsqueeze(3).to_broadcast([P, width // 4, SLOTS, 4]),
                op=ALU.mult,
            )

        def stiffen_beside(mag, h_bf, pieces):
            for lo, hi in pieces:
                nc.gpsimd.tensor_tensor(
                    out=h_bf[:, lo:hi, :],
                    in0=mag[:, lo:hi, :],
                    in1=g_slots[:].unsqueeze(1).to_broadcast([P, hi - lo, SLOTS]),
                    op=ALU.mult,
                )

        def quantize_h(h_bf, name, h_q):
            width = h_bf.shape[1]
            h_sc = sbuf([P, width], U8, name + "_sc")
            nc.vector.quantize_mx(out=h_q[:].bitcast(FP8X4), scales=h_sc[:], in_=h_bf[:].rearrange("p n t -> p (n t)"))
            return h_q, h_sc

        def readout(w4_q, h_q, h_sc, targets):
            for f, dst in enumerate(targets):
                nc.tensor.matmul_mx(
                    out=dst,
                    lhsT=w4_q[:, P * f : P * (f + 1)].bitcast(FP8X4),
                    lhsT_scale=w4_sc[:, P * f : P * (f + 1)],
                    rhs=h_q[:].bitcast(FP8X4),
                    rhs_scale=h_sc[:],
                    start=True,
                    stop=True,
                )
            return targets

        out_view = out.rearrange("(f p) j -> p f j", p=P)

        def wide_targets(first_bank):
            y_a = psum.tile([P, 2, Q], F32, name="y_a", tag=f"bank{first_bank}")
            y_b = psum.tile([P, Q], F32, name="y_b", tag=f"bank{first_bank + 1}")
            return [y_a[:, 0, :], y_a[:, 1, :], y_b[:]]

        def finish_on_scalar(c, ys, res, tiles=range(TILES_N)):
            lo, hi = CHUNKS[c]
            for f in tiles:
                nc.scalar.activation(out=res[:, f, :], in_=ys[f], func=ACT.Identity, bias=b_col[:, f : f + 1])
                nc.sync.dma_start(out=out_view[:, f, lo:hi], in_=res[:, f, :])

        def finish_on_vector(c, y, res):
            lo, hi = CHUNKS[c]
            tiles = res.shape[1]
            nc.vector.tensor_tensor(
                out=res[:], in0=y[:], in1=b_col[:, 0:tiles].unsqueeze(2).to_broadcast([P, tiles, E]), op=ALU.add
            )
            nc.sync.dma_start(out=out_view[:, 0:tiles, lo:hi], in_=res[:])

        gather_scales(0, sbuf([P, S], U8, "v1_sc"))
        w2_sc = sbuf([P, SLOTS, PASSES, P], U8, "w2_sc")
        reorder_columns(w2_sc[:], w2_sc_raw[:], U16, 1)
        cast_w1(0)
        cast_w1(1)
        w3_sc = sbuf([P, SLOTS, P], U8, "w3_sc")
        w3_q = placed([P, SLOTS, PASSES, P], I32, "w3_q", RAW[1] - 3072)
        nc.scalar.copy(
            out=w3_sc[:].bitcast(U16).rearrange("p t c -> p c t"),
            in_=w3_sc_raw[:].bitcast(U16).rearrange("p (c t) -> p c t", t=SLOTS),
        )
        for a in range(PASSES):
            reorder_columns(w3_q[:, :, a : a + 1, :], w3_raw[:, a : a + 1, :], U32, 2)
        open_banks(0, 0, 2)
        open_banks(1, 4, 2)
        for m in (1, 0, 2):
            if m == 2:
                gather_words(m, 0, 0, 2 * Q, placed([P, 2 * Q], U32, "early2", RAW[0])[:])
            else:
                gather_words(m, 0, 0, 2 * Q, sbuf([P, 2 * Q], U32, f"early{m}")[:])
            if m == 1:
                gather_scales(2, sbuf([P, S], U8, "v3_sc"))
            if m == 0:
                quantize_w1(0)
            for c in range(1 if m == 2 else 2):
                d_passes(m, 0, c, first=(m == 1))
        quantize_w1(1)
        w4_bf = sbuf([P, N, SLOTS], BF16, "w4_bf", "w1_bf1")
        for lo, hi in ((0, Q), (Q, N)):
            nc.gpsimd.tensor_scalar(
                out=w4_bf[:, lo:hi, :],
                in0=w4_raw[:, :, lo:hi].rearrange("p t n -> p n t"),
                scalar1=1.0,
                scalar2=0.0,
                op0=ALU.mult,
                op1=ALU.add,
            )

        def stretch(c, steps, places, first=False, last=True):
            lo, hi = CHUNKS[c]
            for n, (m, a) in enumerate(steps):
                gather_words(m, a, lo, hi, places[:, n, :])
                d_passes(m, a, c, first=(first and n == 0), last=(last and n == len(steps) - 1))

        second_half = ((2, 1), (1, 1), (0, 1))
        first_half = ((1, 0), (2, 0), (0, 0))
        late_at = (RAW[1] + 7168, RAW[1] + 1024)
        stretch(0, second_half, placed([P, 3, Q], U32, "late0", late_at[0]))
        lead = ((0, SIDE), (SIDE, Q))
        mag0 = woven_magnitude(
            0, sbuf([P, 2, Q, 2], F32, "sq0"), placed([P, Q, SLOTS], F32, "mag0", MAG[0]), unit[0], SIDE, lead
        )
        h0 = sbuf([P, Q, SLOTS], BF16, "h_bf0")
        stiffen_beside(mag0, h0, lead)
        d_passes(2, 0, 1)
        stretch(1, second_half, placed([P, 3, Q], U32, "late1", late_at[1]))
        mag1 = woven_magnitude(
            1, placed([P, 2, Q, 2], F32, "sq1", UNIT[0]), placed([P, Q, SLOTS], F32, "mag1", MAG[1]), unit[1]
        )
        open_banks(2, 0, 2)
        stretch(2, second_half[:2], placed([P, 2, Q], U32, "late2a", late_at[0]), first=True, last=False)
        stretch(2, second_half[2:] + first_half, placed([P, 4, Q], U32, "late2b", late_at[1]))
        for c in (3, 4):
            open_banks(c, 4 * c - 10, 2)

        h0_q = quantize_h(h0, "h_q0", sbuf([P, Q], U32, "h_q0"))
        w4_q = placed([P, N], U32, "w4_q", MAG[0] - 1024)
        nc.vector.quantize_mx(out=w4_q[:].bitcast(FP8X4), scales=w4_sc[:], in_=w4_bf[:].rearrange("p n t -> p (n t)"))
        y0 = readout(w4_q, *h0_q, wide_targets(4))
        h1 = sbuf([P, Q, SLOTS], BF16, "h_bf1", "w1_bf1")
        stiffen_beside(mag1, h1, ((0, Q),))
        mag2 = woven_magnitude(2, placed([P, 2, Q, 2], F32, "sq2", UNIT[1]), sbuf([P, Q, SLOTS], F32, "mag2"), one)
        finish_on_scalar(0, y0, sbuf([P, TILES_N, Q], F32, "res0"))
        gather_words(1, 0, 3 * Q, S, placed([P, Q], U32, "early_end", MAG[0] + 512)[:])
        for c in (3, 4):
            d_passes(1, 0, c, first=True)
        late_end = placed([P, 6, E], U32, "late_end", MAG[0] + 1536)
        steps = first_half[1:] + second_half
        stretch(3, steps, late_end[:, 0:5])
        mag_end = [magnitude(3, sbuf([P, SLOTS, E], F32, "sq3"), sbuf([P, SLOTS, E], F32, "mag3"), one)]
        stretch(4, steps[:1], late_end[:, 5:6], last=False)
        y1 = readout(w4_q, *quantize_h(h1, "h_q1", sbuf([P, Q], U32, "h_q1")), wide_targets(0))
        h2 = sbuf([P, Q, SLOTS], BF16, "h_bf2", "w1_bf1")
        stiffen_beside(mag2, h2, lead[:1])
        stretch(4, steps[1:], placed([P, 4, E], U32, "late4", MAG[1]))
        finish_on_scalar(1, y1, sbuf([P, TILES_N, Q], F32, "res1"))
        halves = (slice(0, E // 2), slice(E // 2, E))
        sq4 = sbuf([P, SLOTS, E], F32, "sq4")
        for half in halves:
            for u, bank in enumerate(banks[4]):
                nc.scalar.activation(out=sq4[:, 2 * u : 2 * u + 2, half], in_=bank[:, :, half], func=ACT.Square)
        mag4 = [placed([P, SLOTS, E // 2], F32, f"mag4{u}", LAST + 1024 * u) for u in range(2)]
        for u, bias in enumerate((one, unit[2])):
            root(mag4[u][:], sq4[:, :, halves[u]], bias)
        h3 = placed([P, E, SLOTS], BF16, "h_bf3", MAG[1] + 3072)
        h4 = sbuf([P, E, SLOTS], BF16, "h_bf4")
        nc.vector.tensor_tensor(
            out=h2[:, SIDE:Q, :],
            in0=mag2[:, SIDE:Q, :],
            in1=g_slots[:].unsqueeze(1).to_broadcast([P, Q - SIDE, SLOTS]),
            op=ALU.mult,
        )
        stiffen(mag_end[0][:], h3[:])
        y2 = readout(w4_q, *quantize_h(h2, "h_q2", sbuf([P, Q], U32, "h_q2", "sq3")), wide_targets(2))
        y3 = psum.tile([P, TILES_N, E], F32, name="y3", tag="bank4")
        readout(w4_q, *quantize_h(h3, "h_q3", sbuf([P, E], U32, "h_q3")), [y3[:, f, :] for f in range(TILES_N)])
        for u, half in enumerate(halves):
            stiffen(mag4[u][:], h4[:, half, :])
        y4 = psum.tile([P, 2, E], F32, name="y4", tag="bank5")
        y4_rest = psum.tile([P, E], F32, name="y4_rest", tag="bank6")
        h4_q = placed([P, E], U32, "h_q4", LAST + 1024)
        h4_sc = sbuf([P, E], U8, "h_q4_sc")
        for half in halves:
            nc.vector.quantize_mx(
                out=h4_q[:, half].bitcast(FP8X4), scales=h4_sc[:, half], in_=h4[:, half, :].rearrange("p n t -> p (n t)")
            )
        readout(w4_q, h4_q, h4_sc, [y4[:, 0, :], y4[:, 1, :], y4_rest[:]])
        finish_on_scalar(2, y2, placed([P, TILES_N, Q], F32, "res2", UNIT[2]))
        finish_on_vector(3, y3, sbuf([P, TILES_N, E], F32, "res3", "h_bf4"))
        finish_on_vector(4, y4, sbuf([P, 2, E], F32, "res4"))
        res_rest = sbuf([P, E], F32, "res_rest")
        nc.scalar.activation(out=res_rest[:], in_=y4_rest[:], func=ACT.Identity, bias=b_col[:, 2:3])
        nc.scalar.dma_start(out=out_view[:, 2, S - E : S], in_=res_rest[:])
